import numpy as np, ml_dtypes
CORES = [1,5,17,21,33,37,49,53]
N = 8
BF = ml_dtypes.bfloat16
def gentries(a):
    return np.ascontiguousarray(a.reshape(8, 16, -1).transpose(0, 2, 1)).reshape(8, -1)
def gtable(e):
    e = np.asarray(e); return np.ascontiguousarray(e.reshape(8, -1, 16).transpose(0, 2, 1)).reshape(128, -1).astype(np.int32)
V, G, CAP, Q, C, CL, RO = 2304, 256, 32, (128, 128), 2, 5, 2
W = V + (N - 1) * G
def ghosted(xs):
    return np.stack([np.concatenate([xs[a]] + [xs[(a - d) % N][:, :, :G] for d in range(1, N)], axis=2) for a in range(N)])
def drawn(n, t, sd):
    r = []
    for c in range(C):
        if n[c] >= Q[c]:
            st = 4096 // Q[c]; b = (41 * t + 13 * n[0] + sd[c]) & (st - 1)
            r.append(V * c + (((np.arange(Q[c]) * st + b) * n[c]) >> 12))
    return np.concatenate(r)
def move(w, nb, s):
    m = np.add.reduce(w[:, nb[:, s]], axis=1) >> 4
    w[:, s] = w[:, s] + np.minimum(np.maximum(m - w[:, s], -CL), CL)
def hand(w, s):
    for a in range(N):
        for g in range(8):
            lo = np.sort(s[a][g]); lo = lo[lo < G][:CAP]
            for d in range(1, N): w[(a + d) % N, g][:, V + (d - 1) * G + lo] = w[a, g][:, lo]
def touched(nb, s):
    return np.unique(np.concatenate([s, nb[0, s]]))
def energy(w, nb, s):
    return np.sum(np.abs(w[:, nb[:, s]] - w[:, None, s]), axis=(0, 1))
def lay(n):
    return np.concatenate([V * c + np.arange(n[c]) for c in range(C)])
def force(rng, c, k):
    cuts = np.sort(rng.integers(0, V - k + 1, C - 2)); p = np.diff(np.concatenate([np.array([0]), cuts, np.array([V - k])]))
    return np.insert(p, c, k)
def parts(rng):
    amp = rng.choice(np.array([3, 12, 40, 127]), (N, 8, 1, V)); xs = 128 + rng.integers(-127, 128, (N, 8, 16, V)) * amp // 127
    nbr = rng.integers(0, W, (N, 8, 16, V)); nbr[:, :, 0] = np.argsort(rng.random((N, 8, V)), axis=2)
    z = np.zeros((N, 8, 1), np.int64); n = np.diff(np.concatenate([z, np.sort(rng.integers(0, V + 1, (N, 8, C - 1)), axis=2), z + V], axis=2), axis=2)
    o = np.argsort(rng.random((N, 8, V)), axis=2); sd = rng.integers(0, 4096, (N, 8, C))
    return xs, nbr, n, o, sd
def quant(rng, xs, nbr):
    w = ghosted(xs); th = np.zeros((N, 8, C - 1), np.int64)
    for a in range(N):
        for g in range(8): th[a, g] = np.sort(energy(w[a, g], nbr[a, g], rng.integers(0, V, 256)))[np.sort(rng.integers(16, 240, C - 1))]
    return th
def watched(rng, g, t, xs, nbr, n, o, th, sd):
    one = V * np.eye(C, dtype=np.int64)[C - 1]
    for a in range(0, N, 2):
        n[a, g] = V // C; n[a, g, C - 1] += V - C * (V // C)
        if t > 0: n[a, g] = one; th[a, g] = 0
        at = [np.searchsorted(lay(n[a, g]), drawn(n[a, g], u, sd[a, g])) for u in range(t + 1)]
        p = at[t]; early = np.concatenate([np.zeros(0, np.int64)] + at[:t]); m = np.ones(V, bool); m[p] = False; m[early] = False
        lo = rng.permutation(G); hi = G + rng.permutation(V - G); q = o[a, g]
        q[p] = lo[:len(p)]; q[early] = hi[:len(early)]; q[m] = rng.permutation(np.concatenate([lo[len(p):], hi[len(early):]]))
        xs[a, g] = 200; xs[a, g][:, :G] = 100; nbr[a, g, 0] = np.arange(V); nbr[a, g, 1:] = rng.integers(G, V, (15, V))
        z = np.sort(q[p]); still = rng.random(len(z)) < 0.5; still[CAP - 1:CAP + 1] = False
        nbr[a, g, 1:][:, z[still]] = z[still]
        b = a + 1; n[b, g] = one; xs[b, g] = 200; th[b, g] = 240 * (100 - CL)
        come = o[b, g][np.searchsorted(lay(one), drawn(one, t, sd[b, g]))]
        nbr[b, g, 0] = np.arange(V); nbr[b, g, 1:] = V + rng.choice(z, V)
        nbr[b, g, 1:][:, come] = V + rng.permutation(z[:len(come)])
def pack(xs, nbr, n, o, th, sd):
    pl = np.zeros((N, 8, V), np.int64)
    for a in range(N):
        for g in range(8): pl[a, g, o[a, g]] = lay(n[a, g])
    return {"x": np.ascontiguousarray(xs.reshape(N, 128, V)).astype(np.float32).astype(BF), "nb": np.ascontiguousarray(nbr.reshape(N, 128, V)).astype(np.int32),
            "plc": np.stack([gtable(p) for p in pl]), "th": th.astype(np.int32), "sd": sd.astype(np.int32)}
def setup_inputs(rng):
    xs, nbr, n, o, sd = parts(rng)
    for a in range(N): n[a, (3 * a + 2) % 8] = force(rng, a % C, int(rng.integers(0, Q[a % C])))
    return pack(xs, nbr, n, o, quant(rng, xs, nbr), sd)
def setup_inputs_room(rng):
    xs, nbr, n, o, sd = parts(rng)
    for a in range(N):
        for g in range(8):
            if a == 0:
                n[a, g] = V // C; n[a, g, C - 1] += V - C * (V // C); k = (CAP, CAP + 1, 2 * CAP, CAP - 1, 1, 0, CAP, CAP + 1)[g]
            else:
                c = (g + a) % C; n[a, g] = force(rng, c, (Q[c] - 1, Q[c], Q[c] + 1, 0)[(g + g // 4) % 4]); k = int(rng.choice(np.array([0, 1, CAP - 1, CAP, CAP + 1, 2 * CAP])))
            p = np.searchsorted(lay(n[a, g]), drawn(n[a, g], 0, sd[a, g])); k = min(k, len(p)); h = len(p) - k
            lo = rng.permutation(G); hi = G + rng.permutation(V - G); m = np.ones(V, bool); m[p] = False; q = o[a, g]
            q[p] = rng.permutation(np.concatenate([lo[:k], hi[:h]])); q[m] = rng.permutation(np.concatenate([lo[k:], hi[h:]]))
    return pack(xs, nbr, n, o, quant(rng, xs, nbr), sd)
def setup_inputs_ties(rng):
    xs, nbr, n, o, sd = parts(rng); xs[:, ::2] = 100 + rng.integers(0, 4, (N, 4, 16, V)); xs[:, 4] = 77
    for a in range(N):
        q = rng.permutation(V); lo = q[:V // 2]; hi = q[V // 2:]; xs[a, 6] = 0; xs[a, 6][:, hi] = 255
        nbr[a, 6, 0][lo] = hi; nbr[a, 6, 0][hi] = np.roll(lo, -1)
        nbr[a, 6, 1:][:, lo] = rng.choice(hi, (15, V // 2)); nbr[a, 6, 1:][:, hi] = rng.choice(lo, (15, V // 2))
    w = ghosted(xs); s = [[o[a, g][np.searchsorted(lay(n[a, g]), drawn(n[a, g], 0, sd[a, g]))] for g in range(8)] for a in range(N)]; th = np.zeros((N, 8, C - 1), np.int64)
    for a in range(N):
        for g in range(8): move(w[a, g], nbr[a, g], s[a][g])
    hand(w, s)
    for a in range(N):
        for g in range(8):
            e = energy(w[a, g], nbr[a, g], touched(nbr[a, g], s[a][g])); th[a, g] = e[rng.integers(0, len(e), C - 1)] + rng.integers(0, 2, C - 1)
    th[:, 1] = th[:, 1, :1]; th[::2, 6, 0] = 65280
    return pack(xs, nbr, n, o, th, sd)
def setup_inputs_flood(rng):
    xs, nbr, n, o, sd = parts(rng); th = quant(rng, xs, nbr); one = V * np.eye(C, dtype=np.int64)
    n[:, 0] = one[0]; th[:, 0] = 0; n[:, 1] = one[C - 1]; th[:, 1] = 65536; nbr[:, 2, 0] = np.arange(V); n[:, 5] = one[C - 1]; th[:, 5] = 0
    th[:, 4] = 0; th[:, 6] = 65536; th[:, 7] = 65536 * rng.integers(0, 2, (N, C - 1))
    for a in range(N):
        nbr[a, 3, 0][o[a, 3]] = np.roll(o[a, 3], -1); n[a, 4] = force(rng, 0, Q[0]); n[a, 6] = force(rng, C - 1, Q[C - 1])
    for a in range(0, N, 2):
        k = V // C; n[a, 5] = k; n[a, 5, C - 1] = V - (C - 1) * k; th[a, 5] = 32768; q = o[a, 5]
        for c in range(C):
            m = q[c * k:c * k + n[a, 5, c]]; nbr[a, 5, 0][m] = np.roll(m, -1)
        nbr[a, 5, 1:] = rng.choice(q[k:], (15, V)); xs[a, 5] = 0; xs[a, 5][:, q[:k]] = 255
    for a in range(1, N, 2):
        n[a, 1] = max(Q); k = (C - 1) * max(Q); n[a, 1, C - 1] = V - k; q = o[a, 1]
        p = np.searchsorted(lay(n[a, 1]), drawn(n[a, 1], 0, sd[a, 1])); m = np.ones(V, bool); m[p] = False
        early = k + np.flatnonzero(m[k:V - len(p) - Q[C - 1]]); early = rng.permutation(early)[:len(p)]; r = np.ones(V, bool); r[early] = False
        nbr[a, 1, 0][q[p]] = q[early]; nbr[a, 1, 0][q[m]] = rng.permutation(q[r])
    return pack(xs, nbr, n, o, th, sd)
def setup_inputs_alike(rng):
    xs, nbr, n, o, sd = parts(rng); xs[:, ::2] = 255 * rng.integers(0, 2, (N, 4, 16, V))
    nbr[:, 1, 1:] = rng.choice(np.array([0, V - 1, V, W - 1]), (N, 15, V)); nbr[:, 2, 1:] = nbr[:, 2, 1:2]
    nbr[:, 3, 1:] = rng.integers(V, W, (N, 15, V)); nbr[:, 5, 1:] = rng.integers(0, V, (N, 15, V)); nbr[:, 7] = np.arange(V)
    th = quant(rng, xs, nbr)
    watched(rng, 0, 0, xs, nbr, n, o, th, sd); watched(rng, 4, RO - 1, xs, nbr, n, o, th, sd)
    return pack(xs, nbr, n, o, th, sd)
def setup_inputs_spread(rng):
    xs, nbr, n, o, sd = parts(rng)
    xs = np.minimum((np.exp2(8 * rng.random((N, 8, 1, V))) * rng.random((N, 8, 16, V))).astype(np.int64), 255)
    nbr[:, :, 1:] = W - 1 - np.minimum((W * rng.random((N, 8, 15, V)) ** 3).astype(np.int64), W - 1)
    th = quant(rng, xs, nbr); th[:, 1::2] = np.minimum(np.exp2(16 * rng.random((N, 4, C - 1))).astype(np.int64), 65536)
    sd[:, ::3] = rng.choice(np.array([0, 1, 31, 4095]), sd[:, ::3].shape)
    return pack(xs, nbr, n, o, th, sd)
def check_inputs(d):
    bad = []
    v = np.asarray(d["x"]).astype(np.float32)
    if not np.all((v >= 0) & (v <= 255) & (v == np.floor(v))): bad.append("x: whole numbers from 0 to 255")
    for k, hi in (("nb", W - 1), ("plc", C * V - 1), ("th", 65536), ("sd", 4095)):
        if np.min(d[k]) < 0 or np.max(d[k]) > hi: bad.append("range of " + k)
    if np.any(np.sort(np.asarray(d["nb"]).reshape(N, 8, 16, V)[:, :, 0], axis=2) != np.arange(V)): bad.append("first neighbours: every own site once")
    k = np.sort(np.stack([gentries(a) for a in d["plc"]]).astype(np.int64), axis=2); c = k // V; p = np.arange(V)[None, None, :]
    for j in range(C): p = p - np.where(c > j, np.count_nonzero(c == j, axis=2)[:, :, None], 0)
    if np.any(k - V * c != p): bad.append("bags filled from position 0 on, each position once")
    return bad
def reference(x, nb, plc, th, sd):
    w = ghosted(x.astype(np.float32).astype(np.int64).reshape(N, 8, 16, V)); nbr = nb.astype(np.int64).reshape(N, 8, 16, V)
    pl = np.stack([gentries(a) for a in plc]).astype(np.int64)
    bag = np.zeros((N, 8, C * V), np.int64); np.put_along_axis(bag, pl, np.broadcast_to(np.arange(V), pl.shape), 2)
    n = np.stack([np.count_nonzero(pl // V == c, axis=2) for c in range(C)], axis=2).astype(np.int64)
    tv = th.astype(np.int64); sv = sd.astype(np.int64)
    for t in range(RO):
        s = [[bag[a, g][drawn(n[a, g], t, sv[a, g])] for g in range(8)] for a in range(N)]
        for a in range(N):
            for g in range(8): move(w[a, g], nbr[a, g], s[a][g])
        hand(w, s)
        for a in range(N):
            for g in range(8):
                k, h, z = bag[a, g], pl[a, g], n[a, g]
                u = touched(nbr[a, g], s[a][g]); e = energy(w[a, g], nbr[a, g], u)
                new = np.sum(e[None, :] >= tv[a, g][:, None], axis=0); old = h[u] // V
                go = new != old; u, new, old = u[go], new[go], old[go]
                for c in range(C):
                    out = u[old == c]; left = z[c] - len(out); p = h[out]; hole = p[p < V * c + left]
                    tail = k[V * c + left:V * c + z[c]]; stay = tail[~np.isin(tail, out)]
                    k[hole] = stay; h[stay] = hole; z[c] = left
                for c in range(C):
                    come = u[new == c]; p = V * c + z[c] + np.arange(len(come))
                    k[p] = come; h[come] = p; z[c] += len(come)
    return {"yx": np.ascontiguousarray(w[:, :, :, :V]).reshape(N, 128, V).astype(np.float32).astype(BF), "yp": pl.astype(np.float32)}

@@ -1,0 +1,603 @@
+from concourse.bass import DstId, RemoteDMATransfer
+from concourse.mybir import AluOpType as AL, ActivationFunctionType as AF
+
+V, G, W = 2304, 256, 4096
+VD = V + 128
+BIG = 262144.0
+MAGIC = 12582912.0
+bf, f32, i32, u16 = "bfloat16", "float32", "int32", "uint16"
+_SB = {
+    bf: dict(w=5888, bag=5248, raw=VD, Z=VD, R=VD, SL=1024, Gb=8192, Mb=8192, pfl=144, seq=128, oneb=256, B1=128, B2=128, Bm=128, B16=128, Bj=128,
+             Bh0=128, I1=128, I16=128, Im=128, Ic=128, Dg=128, X=144, Xj=144, Xj4=144, Xh=144, Xn=144, Xl=144, junk=512, hiB=2, Uraw=512, Sp=256,
+             Y=256, GE=512, SE=32, YE=32, CS=256, pay0=40, pay1=40, land0=238, land1=238, SU=512, SU4=512, cm=512, hm=512, Lf=512, cmp=512,
+             sraw=512, Zg=512, CL=512, Rg=512, SR=512),
+    f32: dict(place=VD + 512, plcf=144, tsf=4, ts=4, rb=8, onef=128, Bt=128, Bf=128, If=128, G8=128, Sel=2048, B12=128, B13=128, BH=128, X0=144,
+              OH=16, jf=80, C=32, q16=32, q=32, j32=8, dB=32, dB8=32, dP=32, dP8=32, K2=2, jh=2, S=40, Uw=32, Nf=256, t2=8, PL=512, Ab=512, J=512,
+              PLw=32, oldw=32, pos8=32, a=320, dr=96),
+    i32: dict(nbw=VD, plci=144, tsi=4, ohi=16, ohj=16),
+    u16: dict(plc16=144, P16=16, Uo=32, Dw=16, N16=512, ix=2, NE=32, go=238, o=256),
+}
+PSUM = ("pS", "pE0", "pE1", "pm", "pa", "pb", "pc", "pd")
+SCRATCH = {k: ("sbuf", [128, n], d) for d, b in _SB.items() for k, n in b.items()}
+SCRATCH.update({k: ("psum", [128, 512], f32) for k in PSUM})
+SEMAPHORES = ["cv", "cs", "cp", "cg", "dx0", "dx1", "dnb", "dpl", "dth", "dsd", "dyx", "dyp",
+              "ga", "gs", "gw", "l0", "l1", "la0", "la1", "ar0", "ar1"]
+
+
+def rank_program(g, core, T, topo):
+    rank = T.rank_of(core)
+    if rank is None:
+        return
+    N = len(T.cores)
+    eng = {"v": g.vector, "s": g.scalar, "p": g.tensor, "g": g, "y": g.sync}
+    known = {k: {} for k in eng}
+    total = {}
+    wr, rd = {}, {}
+
+    def A(name, lo=0, hi=None, step=1, p=None):
+        t = T[name]
+        if hi is None:
+            hi = t.shape[1]
+        ps = slice(None) if p is None else p
+        return (t[ps, lo:hi:step] if step > 1 else t[ps, lo:hi], [(name, lo, hi)], [])
+
+    def col(name, c):
+        return A(name, c, c + 1)
+
+    def IND(win, off):
+        return (win[0].indirect(off[0]), win[1], off[1])
+
+    def need(q, toks):
+        best = {}
+        for t in toks:
+            if t[0] not in best or best[t[0]][1] < t[1]:
+                best[t[0]] = t
+        for t in sorted(best.values(), key=lambda t: -len(t[2])):
+            if known[q].get(t[0], 0) < t[1]:
+                eng[q].wait_ge(T.sem[t[0]], t[1])
+                known[q][t[0]] = t[1]
+                for k, c in t[2].items():
+                    if known[q].get(k, 0) < c:
+                        known[q][k] = c
+
+    def deps(q, R, Wr):
+        toks = []
+        for (n, lo, hi) in R:
+            ps = n in PSUM
+            for e in wr.get(n, []):
+                if (ps or (e[0] < hi and lo < e[1])) and not (q == "p" and e[3] == "p"):
+                    toks.append(e[2])
+            if ps:
+                toks += [e[2] for e in rd.get(n, []) if e[3] != q]
+        for (n, lo, hi) in Wr:
+            ps = n in PSUM
+            for e in wr.get(n, []) + rd.get(n, []):
+                if (ps or (e[0] < hi and lo < e[1])) and not (e[3] == q and q == "p"):
+                    toks.append(e[2])
+        return toks
+
+    def note(q, tok, R, Wr):
+        for (n, lo, hi) in Wr:
+            for d in (wr, rd):
+                d[n] = [e for e in d.get(n, []) if not (lo <= e[0] and e[1] <= hi)]
+            wr[n].append((lo, hi, tok, q))
+        for (n, lo, hi) in R:
+            rd[n] = [e for e in rd.get(n, []) if not (e[3] == q and e[2][0] == tok[0] and lo <= e[0] and e[1] <= hi)]
+            rd[n].append((lo, hi, tok, q))
+
+    def run(q, fn, outs, ins, sem=None, inc=1):
+        R, Wr = [], []
+        for o in outs:
+            Wr += o[1]
+            R += o[2]
+        for i in ins:
+            if isinstance(i, tuple):
+                R += i[1] + i[2]
+        need(q, deps(q, R, Wr))
+        sem = sem or "c" + q
+        total[sem] = total.get(sem, 0) + inc
+        fn().then_inc(T.sem[sem], inc)
+        note(q if sem == "c" + q else sem, (sem, total[sem], dict(known[q])), R, Wr)
+
+    def x(a):
+        return a[0] if isinstance(a, tuple) else a
+
+    def cp(o, i):
+        run("v", lambda: g.vector.tensor_copy(o[0], i[0]), [o], [i])
+
+    def tt(o, a, b, op):
+        run("v", lambda: g.vector.tensor_tensor(o[0], a[0], b[0], op), [o], [a, b])
+
+    def ts(o, a, s1, op0, s2=None, op1=None):
+        if op1 is None:
+            run("v", lambda: g.vector.tensor_scalar(o[0], a[0], x(s1), None, op0), [o], [a, s1])
+        else:
+            run("v", lambda: g.vector.tensor_scalar(o[0], a[0], x(s1), x(s2), op0, op1), [o], [a, s1, s2])
+
+    def ms(o, c):
+        run("v", lambda: g.vector.memset(o[0], c), [o], [])
+
+    def scan(o, a, init, op1):
+        run("v", lambda: g.vector.tensor_tensor_scan(o[0], a[0], a[0], x(init), AL.add, op1), [o], [a, init])
+
+    def act(o, i, scale=1.0, bias=0.0, f=AF.Identity, acc=None):
+        if acc is None:
+            run("s", lambda: g.scalar.activation(o[0], i[0], f, bias=x(bias), scale=x(scale)), [o], [i, scale, bias])
+        else:
+            run("s", lambda: g.scalar.activation(o[0], i[0], f, bias=x(bias), scale=x(scale), accum_out=acc[0]), [o, acc], [i, scale, bias])
+
+    def mm(o, l, r, start, stop):
+        run("p", lambda: g.tensor.matmul(o[0], l[0], r[0], start, stop), [o], [l, r])
+
+    def sel(o, xn, name, lo, hi, start=True, stop=True):
+        for r in range(16):
+            mm(o, A(xn, 15 - r, 143 - r), A(name, lo + r, hi, 16), start and r == 0, stop and r == 15)
+
+    def iota(o, pat, base, cmul, small=False):
+        if small:
+            run("g", lambda: g.iota(o[0], pat, base, cmul, allow_small_or_imprecise_dtypes=True), [o], [])
+        else:
+            run("g", lambda: g.iota(o[0], pat, base, cmul), [o], [])
+
+    def asel(o, i, pat, op, base, cmul):
+        run("g", lambda: g.affine_select(o[0], i[0], pat, op, 0.0, base, cmul), [o], [i])
+
+    def dma(q, o, i, sem):
+        run(q, lambda: eng[q].dma_start(o[0], i[0]), [o], [i], sem, 16)
+
+    def hbm(ap):
+        return (ap, [], [])
+
+    def dst(c):
+        rid, pid, _se = topo.addr(c)
+        return DstId(rid=rid, pnc=pid)
+
+    def bits(es):
+        return sum(1 << e for e in es)
+
+    def send(trs, srcs, lsem):
+        R = []
+        for s in srcs:
+            R += s[1]
+        need("g", deps("g", R, []))
+        g.remote_dma_fused([RemoteDMATransfer(dst_ids=[dst(c) for c, _a in ds], dma_engine_mask=bits(es), remote_sem=T.sem[rs],
+                                              srcs=[s], dsts=[a for _c, a in ds]) for s, ds, es, rs in trs], local_sem=T.sem[lsem])
+        total[lsem] = total.get(lsem, 0) + sum(len(t[2]) for t in trs)
+        note(lsem, (lsem, total[lsem], dict(known["g"])), R, [])
+
+    def landed(sem, n, regions):
+        total[sem] = n
+        note(sem, (sem, n, {}), [], regions)
+
+    cores = list(T.cores)
+    others = [(rank + d) % N for d in range(1, N)]
+    near = [r for r in others if topo.chip(cores[r]) == topo.chip(core)]
+    far = [r for r in others if topo.chip(cores[r]) != topo.chip(core)]
+    sib = near[0]
+    twins = [r for r in far if topo.die(cores[r]) == topo.die(core)]
+    e_far = topo.engines(core, cores[far[0]])
+    e_all = topo.engines(core, cores[sib])
+    e_near = [e for e in e_all if e not in e_far]
+
+    def gcol(recv, sender):
+        return V + ((recv - sender) % N - 1) * G
+
+    dma("y", A("w", 0, G), hbm(T.x[:, 0:G]), "dx0")
+    dma("s", A("plci"), hbm(T.plc[:]), "dpl")
+    dma("y", A("tsi", 0, 1, p=slice(0, 8)), hbm(T.th[:]), "dth")
+    dma("y", A("tsi", 1, 3, p=slice(0, 8)), hbm(T.sd[:]), "dsd")
+    dma("y", A("nbw", 0, V), hbm(T.nb[:]), "dnb")
+    dma("y", A("w", G, V), hbm(T.x[:, G:V]), "dx1")
+
+    cR, cB0, cA, cLo8, cH0, cH1, cW8, cW10, cW12, cSg, cCtr, cAU, cBU, cWh, cWj, cHc, cWn, cThp, cNb0, cBc, cW810, cMW10, cT, cK, cT2, cT3 = range(26)
+    sN0, sN1, sL0, sL1, sT, sTH, sDL, sB1, sB, sU, sI, sE0, sE1, sV0, sV1, sBa0, sBa1, sW0, sW1, sb0, sb1, sM0, sM1, sM2, sD2, sTop, sTL, sR0, sR1, sT1 = range(30)
+    c = lambda k: col("C", k)
+    s = lambda k: col("S", k)
+    oh = lambda k: col("OH", k)
+    ms(A("onef"), 1.0)
+    iota(A("ohi"), [[-1, 16]], 128, 1)
+    iota(A("seq"), [[1, 128]], 0, 0, True)
+    iota(A("q16"), [[16, 32]], 0, 0, True)
+    asel(A("Bt"), A("onef"), [[-16, 8], [0, 16]], AL.is_ge, 0, 1)
+    asel(A("Bf"), A("Bt"), [[16, 8], [0, 16]], AL.is_ge, 15, -1)
+    asel(A("G8"), A("onef"), [[1, 8], [0, 16]], AL.is_equal, 0, -1)
+    ts(A("ohj"), A("ohi"), 15, AL.bitwise_and)
+    ms(A("Z", 0, 608), 0.0)
+    ts(A("OH"), A("ohj"), 0.0, AL.is_equal)
+    cp(c(cR), col("ohj", 0))
+    for k in range(5):
+        act(col("rb", k), oh(0), scale=128.0 * 2 ** k)
+    ms(A("Z", 608, 1216), 0.0)
+    ts(A("raw", 0, 128), A("seq"), oh(1), AL.mult)
+    for k in range(5):
+        n = 128 * 2 ** k
+        m = min(n, VD - n)
+        if k < 4:
+            ms(A("Z", 1216 + 304 * k, 1520 + 304 * k), 0.0)
+        ts(A("raw", n, n + m), A("raw", 0, m), col("rb", k), AL.add)
+
+    send([(T.w[:, 0:G], [(cores[r], T.w[:, gcol(r, rank):gcol(r, rank) + G]) for r in twins], e_far, "ga"),
+          (T.w[:, 0:G], [(cores[sib], T.w[:, gcol(sib, rank):gcol(sib, rank) + G])], e_near, "gs")], [A("w", 0, G)], "l0")
+    landed("ga", len(e_far) * len(twins), [("w", gcol(rank, r), gcol(rank, r) + G) for r in twins])
+    landed("gs", len(e_near), [("w", gcol(rank, sib), gcol(rank, sib) + G)])
+    asel(A("If"), A("onef"), [[-1, 128]], AL.is_equal, 0, 1)
+    iota(A("nbw", V, VD), [[1, 128]], V, 0)
+    nf = len(e_all) // 4
+    send([(T.w[:, gcol(rank, r):gcol(rank, r) + G], [(cores[sib], T.w[:, gcol(sib, r):gcol(sib, r) + G])], e_all[k * nf:(k + 1) * nf], "gw")
+          for k, r in enumerate(twins)], [A("w", gcol(rank, r), gcol(rank, r) + G) for r in twins], "l1")
+    landed("gw", nf * len(twins), [("w", gcol(rank, r), gcol(rank, r) + G) for r in far if r not in twins])
+
+    def osum(k, lo, hi, step=1):
+        act(A("jf", 8 * k, 8 * k + len(range(lo, hi, step))), A("OH", lo, hi, step), acc=c(k))
+
+    act(A("q"), A("q16"), bias=c(cR))
+    act(A("B1"), A("Bf"))
+    for r in range(16):
+        act(A("Sel", 128 * r, 128 * r + 128), A("Bf"), scale=oh(r))
+    cp(A("plc16"), A("plci"))
+    cp(A("plcf"), A("plci"))
+    cp(A("tsf", 0, 3, p=slice(0, 8)), A("tsi", 0, 3, p=slice(0, 8)))
+    cp(IND(A("bag", 0, 2 * V), A("plc16")), A("raw", 0, V))
+    act(A("pfl"), A("plcf"), scale=-1.0, bias=V - 0.5, f=AF.Sign)
+    mm(A("pc", 0, 144), A("B1"), A("pfl"), True, True)
+    mm(A("pd", 0, 3), A("G8", p=slice(0, 8)), A("tsf", 0, 3, p=slice(0, 8)), True, True)
+    banks = ("pS", "pE0", "pE1", "pm", "pa", "pb")
+    for r in range(16):
+        mm(A(banks[r // 3], 144 * (r % 3), 144 * (r % 3) + 144), A("Sel", 128 * r, 128 * r + 128), A("plcf"), True, True)
+    act(A("X"), A("Z", 0, 144))
+    act(A("j32"), A("q", 0, 8), scale=32.0)
+    act(A("junk", 0, 144), A("pc", 0, 144), acc=s(sT))
+    act(A("ts", 0, 3), A("pd", 0, 3))
+    act(s(sN0), s(sT), scale=0.5, bias=0.5 * V)
+    act(s(sN1), s(sT), scale=-0.5, bias=0.5 * V)
+    act(A("X", 15, 143, 16), A("Bf", 0, 128, 16))
+
+    def draw_places(t):
+        n2 = A("S", sN0, sN0 + 2)
+        dr = lambda k, n=2: A("dr", 16 * k, 16 * k + n)
+        act(s(sT1), s(sN0), scale=13.0, bias=41.0 * t)
+        act(A("S", sV0, sV0 + 2), n2, scale=-1.0, bias=127.5, f=AF.Sign)
+        act(dr(0), A("ts", 1, 3), bias=s(sT1))
+        act(A("S", sR0, sR0 + 2), n2, bias=-128.0, f=AF.Relu)
+        act(dr(1), dr(0), scale=1.0 / 32, bias=-31.0 / 64)
+        act(s(sBa0), s(sV0), scale=float(V), bias=V + 0.5 * V - MAGIC)
+        act(dr(2), dr(1), bias=MAGIC)
+        act(s(sBa1), s(sV1), scale=0.5 * V, bias=1.5 * V + 0.5 * V - MAGIC)
+        act(dr(1), dr(2), scale=-32.0, bias=32.0 * MAGIC)
+        act(A("S", sE0, sE0 + 2), A("S", sR0, sR0 + 2), bias=128.0)
+        for k in range(2):
+            act(s(sb0 + k), A("dr", 16 + k, 17 + k), bias=A("dr", k, k + 1))
+        act(A("S", sW0, sW0 + 2), A("S", sV0, sV0 + 2), scale=0.5 * (W - V), bias=0.5 * (W - V))
+        for k in range(2):
+            act(A("dr", 32 + k, 33 + k), s(sb0 + k), scale=s(sE0 + k), bias=-0.5 * V * 4096)
+        for k in range(2):
+            act(A("dr", 48 + 8 * k, 56 + 8 * k), A("j32"), scale=s(sE0 + k), bias=A("dr", 32 + k, 33 + k))
+        act(dr(4, 16), dr(3, 16), scale=1.0 / 4096, bias=-0.5 + 1.0 / 8192)
+        act(dr(5, 16), dr(4, 16), bias=MAGIC)
+
+    def draw_list():
+        for k in range(2):
+            ts(A("P16", 8 * k, 8 * k + 8), A("dr", 80 + 8 * k, 88 + 8 * k), s(sBa0 + k), AL.add)
+
+    draw_places(0)
+    draw_list()
+    act(A("bag", 2 * V, 4736), A("raw", V, VD))
+    act(A("oneb"), A("Z", 0, 256), bias=1.0)
+    act(A("X0"), A("X"), scale=oh(0))
+    act(A("I16"), A("If"), scale=1.0 / 16)
+    act(A("Im"), A("If"), scale=-1.0)
+    act(A("Ic"), A("If"), scale=-15.0 / 32)
+    act(A("K2"), A("q", 0, 2), scale=8.0, bias=1792.0)
+    act(A("jh"), A("q", 0, 2), bias=0.5)
+    act(A("SL", 0, 512), A("Z", 0, 512))
+    for r in range(16):
+        act((T.place[:, r:V:16], [("place", r, r + 1) if r < 15 else ("place", 15, V)], []), A(banks[r // 3], 144 * (r % 3), 144 * (r % 3) + 144))
+    act(A("place", V, VD), A("seq"), bias=2.0 * V)
+
+    def constants_a():
+        osum(cB0, 1, 16, 2)
+        osum(cA, 0, 4)
+        osum(cLo8, 0, 8)
+        osum(cH0, 2, 7, 4)
+        osum(cH1, 3, 8, 4)
+        osum(cW8, 8, 10)
+        osum(cW10, 10, 12)
+        osum(cW12, 12, 14)
+        act(c(cSg), c(cB0), scale=-2.0 * BIG, bias=BIG)
+        act(c(cCtr), c(cB0), scale=-float(V), bias=-1151.5)
+        act(c(cT), c(cA), scale=-1.0, bias=c(cLo8))
+        act(c(cT2), c(cA), bias=c(cW12))
+        act(c(cWh), c(cH0), bias=c(cH1))
+        act(c(cAU), c(cT), bias=c(cW12))
+        act(A("I1"), A("If"))
+        act(c(cBU), c(cAU), scale=-1.0, bias=c(cA))
+
+    def constants_b():
+        ts(c(cWj), c(cWh), -1.0, AL.mult, c(cLo8), AL.add)
+        ts(c(cT3), c(cLo8), -1.0, AL.add)
+        tt(c(cT), c(cW8), c(cW10), AL.add)
+        ts(c(cThp), c(cSg), 2.0, AL.mult, col("ts", 0), AL.add)
+        ts(c(cK), c(cWj), BIG, AL.mult, c(cT3), AL.add)
+        ts(c(cWn), c(cWj), 0.5, AL.mult, c(cT), AL.add)
+        ts(c(cNb0), c(cB0), -1.0, AL.mult, 1.0, AL.add)
+        ts(c(cHc), c(cH1), float(V), AL.mult, c(cK), AL.add)
+        tt(c(cW810), c(cW8), c(cW10), AL.subtract)
+        ts(c(cMW10), c(cW10), -1.0, AL.mult)
+        ts(c(cBc), c(cNb0), float(V), AL.mult)
+        ms(A("BH"), 0.0)
+        ts(A("B12"), A("B1"), oh(12), AL.mult)
+        ts(A("B13"), A("B1"), oh(13), AL.mult)
+        ts(A("hm", 0, 256), A("oneb"), c(cT2), AL.mult)
+        ts(A("Dg"), A("If"), c(cSg), AL.mult)
+        ts(A("B2"), A("B1"), 2.0, AL.mult)
+        ts(A("Bm"), A("B1"), -1.0, AL.mult)
+        ts(A("B16"), A("B1"), -16.0, AL.mult)
+        ts(A("Bj"), A("B1"), c(cWn), AL.mult)
+        ts(A("Bh0"), A("B1"), c(cH0), AL.mult, 0.5, AL.mult)
+        ts(A("Xj"), A("X"), c(cWj), AL.mult)
+        ts(A("Xj4"), A("X"), c(cWj), AL.mult, -4096.0, AL.mult)
+        ts(A("Xh"), A("X"), c(cWh), AL.mult, 0.5, AL.mult)
+        ts(A("Xn"), A("X"), c(cWn), AL.mult)
+        ts(A("Xl"), A("X"), c(cW12), AL.mult, -8192.0, AL.mult)
+        for r in (2, 3, 6, 7):
+            cp((T.BH[:, r:128:16], [("BH", r, r + 1) if r < 7 else ("BH", 7, 128)], []), A("B13" if r & 1 else "B12", r, 128, 16))
+
+    def constants_c():
+        act(A("dB"), A("q"), bias=4736.0)
+        act(A("dB8"), A("q"), bias=4736.0 - 8192.0)
+        act(A("dP"), A("q"), bias=float(VD))
+        act(A("dP8"), A("q"), bias=VD - 8192.0)
+
+    a = lambda k: A("a", 32 * k, 32 * k + 32)
+    o = lambda k: A("o", 32 * k, 32 * k + 32)
+    ww = A("w", 0, W)
+    early, later = [], []
+    for t in range(2):
+        pay, land = "pay%d" % t, "land%d" % t
+        D = A("Uo", 0, 16)
+        cp(A("Uraw", 0, 256), IND(A("bag", 0, 4736), A("P16")))
+        sel(A("pa", 0, 16), "X", "Uraw", 0, 256)
+        for f in early:
+            f()
+        cp(D, A("pa", 0, 16))
+        cp(A("N16", 0, 256), IND(A("nbw"), D))
+        act(A("Sp"), IND(ww, D), bias=-192.0)
+        cp(A("Nf"), A("N16", 0, 256))
+        cuts = (0, 48, 128, 192, 256)
+
+        def sums(k):
+            for i in range(16):
+                mm(A("pm", cuts[k], cuts[k + 1]), A("I16"), A("Gb", 16 * cuts[k] + i, 16 * cuts[k + 1], 16), False, k == 3 and i == 15)
+
+        def take(k, f):
+            f(A("Gb", 16 * cuts[k], 16 * cuts[k + 1]), IND(ww, A("N16", cuts[k], cuts[k + 1])))
+
+        take(0, act)
+        cp(IND(A("Z"), D), A("oneb"))
+        cp(A("Uw", 0, 16), A("pa", 0, 16))
+        scan(A("CS"), A("Z", 0, 256), 0.0, AL.max)
+        for k in range(2):
+            act(A("junk", 256 * k, 256 * k + 256), A("CS"), scale=-1.0, bias=col("jh", k), f=AF.Sign, acc=col("t2", k))
+        take(1, act)
+        take(2, act)
+        for k in range(2):
+            ts(A("Dw", 8 * k, 8 * k + 8), A("Uw", 8 * k, 8 * k + 8), s(sW0 + k), AL.add)
+        sel(A("pb", 0, 16), "X0", "Nf", 0, 256)
+        mm(A("pm", 0, 256), A("Im"), A("Sp"), True, False)
+        mm(A("pm", 0, 256), A("Ic"), A("oneb"), False, False)
+        sums(0)
+        ts(A("ix"), A("t2", 0, 2), 0.5, AL.mult, 128.0, AL.add)
+        ts(A("t2", 2, 4), A("t2", 0, 2), 0.5, AL.mult, 128.0, AL.add)
+        cp(A("NE"), IND(A("nbw"), A("ix")))
+        ts(A("SE"), IND(ww, A("ix")), -192.0, AL.add)
+        cp(A("GE"), IND(ww, A("NE")))
+        mm(A("pd", 0, 32), A("Im"), A("SE"), True, False)
+        mm(A("pd", 0, 32), A("Ic"), A("oneb", 0, 32), False, False)
+        for i in range(16):
+            mm(A("pd", 0, 32), A("I16"), A("GE", i, 512, 16), False, i == 15)
+        ts(A("t2", 4, 6), A("t2", 0, 2), 256.0, AL.is_ge, 4096.0, AL.mult)
+        cp(A("Uo", 16, 32), A("pb", 0, 16))
+        tt(A("t2", 6, 8), A("t2", 2, 4), A("t2", 4, 6), AL.add)
+        cp(A("Uw", 16, 32), A("pb", 0, 16))
+        tt(A(pay, 32, 34), A("t2", 6, 8), A("K2"), AL.min)
+        ts(A("YE"), A("pd", 0, 32), 187.0, AL.max, 197.0, AL.min)
+        tt(A(pay, 0, 32), A("YE"), A("SE"), AL.add)
+        slot = lambda r: T[land][:, 34 * ((r - rank) % N - 1):34 * ((r - rank) % N)]
+        send([(T[pay][:, 0:34], [(cores[r], slot(r)) for r in far], e_far, "ar%d" % t),
+              (T[pay][:, 0:34], [(cores[r], slot(r)) for r in near], e_near, "ar%d" % t)], [A(pay)], "la%d" % t)
+        landed("ar%d" % t, len(e_far) * len(far) + len(e_near) * len(near), [(land, 0, 238)])
+        take(3, cp)
+        for k in (1, 2, 3):
+            sums(k)
+        U, U2 = A("Uo"), A("Uo", 16, 32)
+        cp(A("N16", 256, 512), IND(A("nbw"), U2))
+        if t == 0:
+            constants_a()
+        ts(A("Y"), A("pm", 0, 256), 187.0, AL.max, 197.0, AL.min)
+        tt(IND(A("w", 0, W + 128), A("Dw")), A("Y"), A("Sp"), AL.add)
+        if t == 1:
+            dma("y", hbm(T.yx[:]), A("w", 0, V), "dyx")
+        act(A("hm", 256, 512), IND(A("Z"), U2), scale=c(cBU), bias=c(cAU))
+        act(A("SU"), IND(ww, U))
+        mm(A("pS"), A("I1"), A("SU"), True, True)
+        for k in range(4):
+            act(A("SU4", 128 * k, 128 * k + 128), A("SU", 384, 512))
+        if t == 0:
+            constants_b()
+        for f in later:
+            f()
+        act(A("PL"), IND(A("place", 0, VD), U))
+        act(A("Ab"), A("PL"), bias=c(cCtr), f=AF.Abs)
+        cp(A("go"), A(land))
+        for d in range(N - 1):
+            cp(IND(A("w", V + G * d, V + G * d + 2048), A("go", 34 * d + 32, 34 * d + 34)), A(land, 34 * d, 34 * d + 32))
+        cp(A("Gb", 0, 16 * 160), IND(ww, A("N16", 0, 160)))
+        for lo, hi in ((160, 256), (256, 384), (384, 512)):
+            act(A("Gb", 16 * lo, 16 * hi), IND(ww, A("N16", lo, hi)))
+        parts = (("pE0", 0, 256), ("pE1", 256, 384), ("pm", 384, 512))
+        dbank = ("pb", "pc", "pd", "pa")
+
+        def gsum(k, lo, hi):
+            for i in range(16):
+                mm(A(parts[k][0], lo - parts[k][1], hi - parts[k][1]), A("Bm"), A("Gb", 16 * lo + i, 16 * hi, 16), False, False)
+
+        def mo(k, i):
+            b, lo, hi = parts[k]
+            return A("Mb", 16 * lo + (hi - lo) * i, 16 * lo + (hi - lo) * (i + 1))
+
+        def vmax(k, i):
+            b, lo, hi = parts[k]
+            tt(mo(k, i), A("Gb", 16 * lo + i, 16 * hi, 16), A("pS", lo, hi), AL.max)
+
+        def msum(k, i):
+            b, lo, hi = parts[k]
+            mm(A(b, 0, hi - lo), A("B1" if k == 2 else "B2"), mo(k, i), False, i == 15)
+
+        def masks(k):
+            b, lo, hi = parts[k]
+            mm(A(b, 0, hi - lo), A("Dg"), A("hm", lo, hi), k == 2, False)
+            mm(A(b, 0, hi - lo), A("Dg"), A("cm", lo, hi), False, False)
+
+        def flags(k):
+            b, lo, hi = parts[k]
+            ts(A("Lf", lo, hi), A(b, 0, hi - lo), c(cThp), AL.is_ge, c(cB0), AL.not_equal)
+
+        def count(k):
+            b, lo, hi = parts[k]
+            act(A("junk", lo, hi), A("Lf", lo, hi), acc=s(sM0 + k))
+
+        sel(A("pa", 0, 32), "X0", "PL", 0, 512)
+        for b, lo, hi in parts[:2]:
+            mm(A(b, 0, hi - lo), A("B16"), A("SU", lo, hi), True, False)
+        for b in dbank[:3]:
+            mm(A(b), A("Im"), A("SU4"), True, False)
+        ts(A("cm"), A("Ab"), 1152.0, AL.is_lt)
+        cp(A("PLw"), A("pa", 0, 32))
+        ts(A("oldw"), A("pa", 0, 32), float(V), AL.is_ge)
+        gsum(0, 160, 256)
+        gsum(0, 0, 160)
+        for k in range(3):
+            masks(k)
+        mm(A("pa"), A("Im"), A("SU4"), True, False)
+        for i in range(16):
+            vmax(0, i)
+            msum(0, i)
+            if i == 7:
+                gsum(1, 256, 384)
+        ts(a(7), A("oldw"), -float(V), AL.mult, 8192.0, AL.add)
+        for i in range(16):
+            mm(A(dbank[i // 4], 128 * (i % 4), 128 * (i % 4) + 128), A("I1"), A("Gb", 16 * 384 + i, 8192, 16), False, i % 4 == 3)
+        vmax(1, 0)
+        flags(0)
+        tt(A("pos8"), a(7), A("PLw"), AL.add)
+        act(s(sT), s(sN1), scale=c(cH1), bias=c(cHc))
+        act(s(sTop), s(sN1), bias=float(V))
+        act(s(sTH), s(sN0), scale=c(cH0), bias=s(sT))
+        for j in range(4):
+            act(A("Mb", 6144 + 512 * j, 6144 + 512 * j + 512), A(dbank[j]), f=AF.Abs)
+        count(0)
+        for i in range(1, 16):
+            vmax(1, i)
+        for j in range(4):
+            for i in range(4 * j, 4 * j + 4):
+                msum(2, i)
+            for i in range(4 * j, 4 * j + 4):
+                msum(1, i)
+        flags(2)
+        count(2)
+        flags(1)
+        count(1)
+        for j, l in ((0, "BH"), (1, "B12"), (2, "B13")):
+            b = "pc" if j == 0 else "pd"
+            for i, k in enumerate((0, 2, 1)):
+                mm(col(b, j), A(l), s(sM0 + k), i == 0, i == 2)
+        m0, m1 = col("pd", 1), col("pd", 2)
+        ts(A("cmp"), A("PL"), col("pc", 0), AL.add, s(sTH), AL.is_lt)
+        tt(A("S", sL0, sL0 + 2), A("S", sN0, sN0 + 2), A("pd", 1, 3), AL.subtract)
+        act(s(sDL), s(sL1), bias=s(sN1))
+        act(s(sTL), s(sL0), scale=-1.0, bias=s(sTop))
+        act(s(sB1), s(sL1), scale=c(cNb0), bias=c(cBc))
+        act(s(sD2), s(sL0), scale=-1.0, bias=s(sL1))
+        act(s(sB), s(sL0), scale=c(cB0), bias=s(sB1))
+        tt(IND(A("Z"), D), A("cmp", 0, 256), A("Lf", 0, 256), AL.mult)
+        ts(a(1), A("q"), m0, AL.is_ge, s(sDL), AL.mult)
+        if t == 0:
+            tt(s(sN0), s(sL0), m1, AL.add)
+        tt(a(2), a(1), A("q"), AL.add)
+        if t == 0:
+            tt(s(sN1), s(sL1), m0, AL.add)
+        ts(a(0), a(2), s(sTL), AL.is_ge, 8192.0, AL.mult)
+        ts(a(6), A("oldw"), s(sD2), AL.mult, s(sL0), AL.add)
+        tt(a(1), a(2), a(0), AL.add)
+        ts(o(0), a(1), s(sL0), AL.add, 4700.0, AL.min)
+        act(col("hiB", 0), s(sB))
+        act(s(sU), s(sB), scale=c(cW10), bias=c(cMW10))
+        act(A("sraw"), IND(A("bag", 0, 4736), o(0)))
+        act(s(sI), col("hiB", 0), scale=c(cW810), bias=s(sU))
+        if t == 0:
+            act(A("Uraw", 256, 512), IND(A("raw"), U2))
+            constants_c()
+        sel(A("pE0", 0, 32), "Xl", "Lf", 0, 512)
+        if t == 0:
+            sel(A("pE1", 0, 32), "Xl", "Lf", 0, 512, True, False)
+        sel(A("pa", 0, 32), "X", "sraw", 0, 512)
+        tt(IND(A("Z"), U2), A("cmp", 256, 512), A("Lf", 256, 512), AL.mult)
+        tt(a(7), A("pos8"), A("pE0", 0, 32), AL.add)
+        tt(a(3), A("Uw"), A("pE0", 0, 32), AL.add)
+        cp(o(1), A("pa", 0, 32))
+        act(A("Zg"), IND(A("Z"), o(1)), scale=-1.0)
+        sel(A("pb", 0, 32), "Xj4", "Zg", 0, 512, True, False)
+        scan(A("R"), A("Z"), s(sI), AL.add)
+        scan(A("CL"), A("Zg"), 0.0, AL.min)
+        sel(A("pb", 0, 32), "Xj", "CL", 0, 512, False, True)
+        mm(col("pc", 2), A("Bh0"), col("R", VD - 1), True, True)
+        tt(A("Rg"), IND(A("R"), U), A("cm"), AL.mult)
+        if t == 0:
+            draw_places(1)
+        ts(a(0), A("pb", 0, 32), 512.0, AL.min)
+        ts(a(4), A("oldw"), col("pc", 2), AL.mult, -1.0, AL.add)
+        tt(a(1), a(0), A("q"), AL.add)
+        sel(A("pa", 0, 32), "Xh", "Rg", 0, 512)
+        if t == 0:
+            sel(A("pE1", 0, 32), "Xn", "Rg", 0, 512, False, True)
+        mm(A("pS"), A("Bj"), A("Rg"), True, True)
+        if t == 1:
+            act(A("J"), A("pS"))
+        tt(a(8), a(7), a(6), AL.is_ge)
+        cp(o(2), a(1))
+        tt(a(5), a(4), A("pa", 0, 32), AL.add)
+        ts(a(9), a(8), 8192.0, AL.mult)
+        cp(o(3), a(5))
+        cp(IND(A("SL"), o(2)), A("sraw"))
+        act(A("SR"), IND(A("SL", 0, 512), o(3)))
+        sel(A("pb", 0, 32), "X", "SR", 0, 512)
+
+        def place_leavers():
+            tt(a(1), a(3), A("dP8"), AL.min)
+            ts(o(6), a(1), 8192.0, AL.add)
+
+        def place_stayers():
+            tt(a(4), a(9), A("pb", 0, 32), AL.add)
+            tt(a(5), a(4), A("dP"), AL.min)
+            cp(o(7), a(5))
+
+        if t == 0:
+            tt(a(0), A("pE1", 0, 32), A("dB8"), AL.min)
+            tt(a(2), a(9), A("PLw"), AL.add)
+            ts(o(4), a(0), 8192.0, AL.add)
+            tt(a(1), a(2), A("dB"), AL.min)
+            draw_list()
+            cp(o(5), a(1))
+            cp(IND(A("bag"), o(4)), A("Uraw"))
+            act(A("Z"), A("R"), scale=0.0)
+            act(A("J"), A("pS"))
+            cp(IND(A("bag"), o(5)), A("SR"))
+            early = [place_leavers, place_stayers]
+            later = [lambda: cp(IND(A("place"), o(6)), A("J")), lambda: cp(IND(A("place"), o(7)), A("PL"))]
+        else:
+            place_leavers()
+            cp(IND(A("place"), o(6)), A("J"))
+            place_stayers()
+            cp(IND(A("place"), o(7)), A("PL"))
+            dma("y", hbm(T.yp[:]), A("place", 0, V, p=slice(0, 128, 16)), "dyp")
+    need("g", [(k, n, {}) for k, n in total.items()])

@@ -9,19 +9,19 @@ bf, f32, i32, u16 = "bfloat16", "float32", "int32", "uint16"
 _SB = {
     bf: dict(w=5888, bag=5248, raw=VD, Z=VD, R=VD, SL=1024, Gb=8192, Mb=8192, pfl=144, seq=128, oneb=256, B1=128, B2=128, Bm=128, B16=128, Bj=128,
              Bh0=128, I1=128, I16=128, Im=128, Ic=128, Dg=128, X=144, Xj=144, Xj4=144, Xh=144, Xn=144, Xl=144, junk=512, hiB=2, Uraw=512, Sp=256,
-             Y=256, GE=512, SE=32, YE=32, CS=256, pay0=40, pay1=40, land0=238, land1=238, SU=512, SU4=512, cm=512, hm=512, Lf=512, cmp=512,
-             sraw=512, Zg=512, CL=512, Rg=512, SR=512),
-    f32: dict(place=VD + 512, plcf=144, tsf=4, ts=4, rb=8, onef=128, Bt=128, Bf=128, If=128, G8=128, Sel=2048, B12=128, B13=128, BH=128, X0=144,
-              OH=16, jf=80, C=32, q16=32, q=32, j32=8, dB=32, dB8=32, dP=32, dP8=32, K2=2, jh=2, S=40, Uw=32, Nf=256, t2=8, PL=512, Ab=512, J=512,
-              PLw=32, oldw=32, pos8=32, a=320, dr=96),
+             Y=256, GE=512, SE=32, YE=32, CS=256, CT=512, pay0=40, pay1=40, land0=238, land1=238, SU=512, SU4=512, cm=512, hm=512, Lf=512,
+             cmp=512, sraw=512, Zg=512, CL=512, Rg=512, SR=512),
+    f32: dict(place=VD + 512, plcf=144, tsf=4, ts=4, rb=8, onef=128, Bt=128, Bu=128, Bf=128, If=128, G8=128, Sel=2048, B12=128, B13=128, BH=128,
+              X0=144, OH=16, jf=80, C=32, q16=32, q=32, j32=8, dB=32, dB8=32, dP=32, dP8=32, K2=2, S=40, Uw=32, Nf=256, t2=8, PL=512, PL64=512,
+              Ab=512, J=512, PLw=32, oldw=32, a=320, dr=96),
     i32: dict(nbw=VD, plci=144, tsi=4, ohi=16, ohj=16),
     u16: dict(plc16=144, P16=16, Uo=32, Dw=16, N16=512, ix=2, NE=32, go=238, o=256),
 }
 PSUM = ("pS", "pE0", "pE1", "pm", "pa", "pb", "pc", "pd")
 SCRATCH = {k: ("sbuf", [128, n], d) for d, b in _SB.items() for k, n in b.items()}
 SCRATCH.update({k: ("psum", [128, 512], f32) for k in PSUM})
-SEMAPHORES = ["cv", "cs", "cp", "cg", "dx0", "dx1", "dnb", "dpl", "dth", "dsd", "dyx", "dyp",
-              "ga", "gs", "gw", "l0", "l1", "la0", "la1", "ar0", "ar1"]
+SEMAPHORES = ["cv", "cs", "cp", "cg", "dx0", "dx1", "dnb", "dpl", "dth", "dsd", "dyx", "dyp", "ga", "gs", "gw", "l0", "l1",
+              "la0", "la1", "lb0", "lb1", "ar0", "ar1", "as0", "as1", "aw0", "aw1"]
 
 
 def rank_program(g, core, T, topo):
@@ -126,6 +126,9 @@ def rank_program(g, core, T, topo):
         else:
             run("s", lambda: g.scalar.activation(o[0], i[0], f, bias=x(bias), scale=x(scale), accum_out=acc[0]), [o, acc], [i, scale, bias])
 
+    def spread(o, i):
+        run("s", lambda: g.scalar.activation(o[0], i[0], AF.Silu), [o], [i])
+
     def mm(o, l, r, start, stop):
         run("p", lambda: g.tensor.matmul(o[0], l[0], r[0], start, stop), [o], [l, r])
 
@@ -174,13 +177,31 @@ def rank_program(g, core, T, topo):
     near = [r for r in others if topo.chip(cores[r]) == topo.chip(core)]
     far = [r for r in others if topo.chip(cores[r]) != topo.chip(core)]
     sib = near[0]
-    twins = [r for r in far if topo.die(cores[r]) == topo.die(core)]
     e_far = topo.engines(core, cores[far[0]])
     e_all = topo.engines(core, cores[sib])
     e_near = [e for e in e_all if e not in e_far]
 
-    def gcol(recv, sender):
-        return V + ((recv - sender) % N - 1) * G
+    def takes(r):
+        both = [k for k in range(N) if topo.chip(cores[k]) == topo.chip(cores[r])]
+        out = sorted((k for k in range(N) if k not in both), key=lambda k: (both[0] - k) % N)
+        return out[len(out) // 2:] if r == both[0] else out[:len(out) // 2]
+
+    takers = [r for r in far if rank in takes(r)]
+    mine = takes(rank)
+
+    def exchange(src, buf, base, n, sems, between=None):
+        def span(recv, ss):
+            return base + n * ((recv - ss[0]) % N - 1), base + n * ((recv - ss[-1]) % N)
+        s_far, s_near, s_on, l0, l1 = sems
+        send([(src[0], [(cores[r], A(buf, *span(r, [rank]))[0]) for r in takers], e_far, s_far),
+              (src[0], [(cores[sib], A(buf, *span(sib, [rank]))[0])], e_near, s_near)], [src], l0)
+        landed(s_far, len(e_far) * len(mine), [(buf,) + span(rank, mine)])
+        landed(s_near, len(e_near), [(buf,) + span(rank, [sib])])
+        if between:
+            between()
+        fw = A(buf, *span(rank, mine))
+        send([(fw[0], [(cores[sib], A(buf, *span(sib, mine))[0])], e_all, s_on)], [fw], l1)
+        landed(s_on, len(e_all), [(buf,) + span(rank, takes(sib))])
 
     dma("y", A("w", 0, G), hbm(T.x[:, 0:G]), "dx0")
     dma("s", A("plci"), hbm(T.plc[:]), "dpl")
@@ -202,30 +223,30 @@ def rank_program(g, core, T, topo):
     asel(A("Bf"), A("Bt"), [[16, 8], [0, 16]], AL.is_ge, 15, -1)
     asel(A("G8"), A("onef"), [[1, 8], [0, 16]], AL.is_equal, 0, -1)
     ts(A("ohj"), A("ohi"), 15, AL.bitwise_and)
-    ms(A("Z", 0, 608), 0.0)
+    ms(A("Z", 0, 400), 0.0)
     ts(A("OH"), A("ohj"), 0.0, AL.is_equal)
     cp(c(cR), col("ohj", 0))
     for k in range(5):
         act(col("rb", k), oh(0), scale=128.0 * 2 ** k)
-    ms(A("Z", 608, 1216), 0.0)
     ts(A("raw", 0, 128), A("seq"), oh(1), AL.mult)
     for k in range(5):
         n = 128 * 2 ** k
         m = min(n, VD - n)
-        if k < 4:
-            ms(A("Z", 1216 + 304 * k, 1520 + 304 * k), 0.0)
+        if k < 3:
+            ms(A("Z", 400 + 272 * k, 672 + 272 * k), 0.0)
         ts(A("raw", n, n + m), A("raw", 0, m), col("rb", k), AL.add)
 
-    send([(T.w[:, 0:G], [(cores[r], T.w[:, gcol(r, rank):gcol(r, rank) + G]) for r in twins], e_far, "ga"),
-          (T.w[:, 0:G], [(cores[sib], T.w[:, gcol(sib, rank):gcol(sib, rank) + G])], e_near, "gs")], [A("w", 0, G)], "l0")
-    landed("ga", len(e_far) * len(twins), [("w", gcol(rank, r), gcol(rank, r) + G) for r in twins])
-    landed("gs", len(e_near), [("w", gcol(rank, sib), gcol(rank, sib) + G)])
-    asel(A("If"), A("onef"), [[-1, 128]], AL.is_equal, 0, 1)
-    iota(A("nbw", V, VD), [[1, 128]], V, 0)
-    nf = len(e_all) // 4
-    send([(T.w[:, gcol(rank, r):gcol(rank, r) + G], [(cores[sib], T.w[:, gcol(sib, r):gcol(sib, r) + G])], e_all[k * nf:(k + 1) * nf], "gw")
-          for k, r in enumerate(twins)], [A("w", gcol(rank, r), gcol(rank, r) + G) for r in twins], "l1")
-    landed("gw", nf * len(twins), [("w", gcol(rank, r), gcol(rank, r) + G) for r in far if r not in twins])
+    def meanwhile():
+        asel(A("If"), A("onef"), [[-1, 128]], AL.is_equal, 0, 1)
+        iota(A("nbw", V, VD), [[1, 128]], V, 0)
+        iota(A("Z", 1216, VD), [[0, VD - 1216]], 0, 0, True)
+
+    exchange(A("w", 0, G), "w", V, G, ("ga", "gs", "gw", "l0", "l1"), meanwhile)
+    asel(A("B12"), A("onef"), [[-16, 8], [0, 16]], AL.is_equal, -12, 1)
+    asel(A("B13"), A("onef"), [[-16, 8], [0, 16]], AL.is_equal, -13, 1)
+    asel(A("BH"), A("onef"), [[-16, 8], [0, 8], [-1, 2]], AL.is_equal, -12, 1)
+    asel(A("Bu"), A("BH"), [[0, 8], [1, 2], [0, 8]], AL.is_equal, 0, 0)
+    asel(A("BH"), A("Bu"), [[0, 32], [1, 2], [0, 2]], AL.is_equal, -1, 0)
 
     def osum(k, lo, hi, step=1):
         act(A("jf", 8 * k, 8 * k + len(range(lo, hi, step))), A("OH", lo, hi, step), acc=c(k))
@@ -241,7 +262,7 @@ def rank_program(g, core, T, topo):
     act(A("pfl"), A("plcf"), scale=-1.0, bias=V - 0.5, f=AF.Sign)
     mm(A("pc", 0, 144), A("B1"), A("pfl"), True, True)
     mm(A("pd", 0, 3), A("G8", p=slice(0, 8)), A("tsf", 0, 3, p=slice(0, 8)), True, True)
-    banks = ("pS", "pE0", "pE1", "pm", "pa", "pb")
+    banks = ("pm", "pb", "pa", "pS", "pE0", "pE1")
     for r in range(16):
         mm(A(banks[r // 3], 144 * (r % 3), 144 * (r % 3) + 144), A("Sel", 128 * r, 128 * r + 128), A("plcf"), True, True)
     act(A("X"), A("Z", 0, 144))
@@ -279,91 +300,75 @@ def rank_program(g, core, T, topo):
         for k in range(2):
             ts(A("P16", 8 * k, 8 * k + 8), A("dr", 80 + 8 * k, 88 + 8 * k), s(sBa0 + k), AL.add)
 
+    def place_rows(r0, r1):
+        for r in range(r0, r1):
+            act((T.place[:, r:V:16], [("place", r, r + 1) if r < 15 else ("place", 15, V)], []),
+                A(banks[r // 3], 144 * (r % 3), 144 * (r % 3) + 144), bias=64.0)
+
+    def whole(k):
+        v = A("place", 768 * (k // 2), 768 * (k // 2) + 768)
+        act(v, v, bias=MAGIC - 64.0 if k % 2 == 0 else -MAGIC)
+
     draw_places(0)
     draw_list()
     act(A("bag", 2 * V, 4736), A("raw", V, VD))
     act(A("oneb"), A("Z", 0, 256), bias=1.0)
-    act(A("X0"), A("X"), scale=oh(0))
     act(A("I16"), A("If"), scale=1.0 / 16)
     act(A("Im"), A("If"), scale=-1.0)
     act(A("Ic"), A("If"), scale=-15.0 / 32)
     act(A("K2"), A("q", 0, 2), scale=8.0, bias=1792.0)
-    act(A("jh"), A("q", 0, 2), bias=0.5)
-    act(A("SL", 0, 512), A("Z", 0, 512))
-    for r in range(16):
-        act((T.place[:, r:V:16], [("place", r, r + 1) if r < 15 else ("place", 15, V)], []), A(banks[r // 3], 144 * (r % 3), 144 * (r % 3) + 144))
-    act(A("place", V, VD), A("seq"), bias=2.0 * V)
+    act(A("X0"), A("X"), scale=oh(0))
+    place_rows(0, 9)
 
-    def constants_a():
-        osum(cB0, 1, 16, 2)
-        osum(cA, 0, 4)
-        osum(cLo8, 0, 8)
-        osum(cH0, 2, 7, 4)
-        osum(cH1, 3, 8, 4)
-        osum(cW8, 8, 10)
-        osum(cW10, 10, 12)
-        osum(cW12, 12, 14)
-        act(c(cSg), c(cB0), scale=-2.0 * BIG, bias=BIG)
-        act(c(cCtr), c(cB0), scale=-float(V), bias=-1151.5)
-        act(c(cT), c(cA), scale=-1.0, bias=c(cLo8))
-        act(c(cT2), c(cA), bias=c(cW12))
-        act(c(cWh), c(cH0), bias=c(cH1))
-        act(c(cAU), c(cT), bias=c(cW12))
-        act(A("I1"), A("If"))
-        act(c(cBU), c(cAU), scale=-1.0, bias=c(cA))
+    osum(cB0, 1, 16, 2)
+    osum(cA, 0, 4)
+    osum(cLo8, 0, 8)
+    osum(cH0, 2, 7, 4)
+    osum(cH1, 3, 8, 4)
+    osum(cW8, 8, 10)
+    osum(cW10, 10, 12)
+    osum(cW12, 12, 14)
+    act(c(cSg), c(cB0), scale=-2.0 * BIG, bias=BIG)
+    act(c(cCtr), c(cB0), scale=-float(V), bias=-1151.5)
+    act(c(cT), c(cA), scale=-1.0, bias=c(cLo8))
+    act(c(cT2), c(cA), bias=c(cW12))
+    act(c(cWh), c(cH0), bias=c(cH1))
+    act(c(cAU), c(cT), bias=c(cW12))
+    act(A("I1"), A("If"))
+    act(c(cBU), c(cAU), scale=-1.0, bias=c(cA))
 
-    def constants_b():
-        ts(c(cWj), c(cWh), -1.0, AL.mult, c(cLo8), AL.add)
-        ts(c(cT3), c(cLo8), -1.0, AL.add)
-        tt(c(cT), c(cW8), c(cW10), AL.add)
-        ts(c(cThp), c(cSg), 2.0, AL.mult, col("ts", 0), AL.add)
-        ts(c(cK), c(cWj), BIG, AL.mult, c(cT3), AL.add)
-        ts(c(cWn), c(cWj), 0.5, AL.mult, c(cT), AL.add)
-        ts(c(cNb0), c(cB0), -1.0, AL.mult, 1.0, AL.add)
-        ts(c(cHc), c(cH1), float(V), AL.mult, c(cK), AL.add)
-        tt(c(cW810), c(cW8), c(cW10), AL.subtract)
-        ts(c(cMW10), c(cW10), -1.0, AL.mult)
-        ts(c(cBc), c(cNb0), float(V), AL.mult)
-        ms(A("BH"), 0.0)
-        ts(A("B12"), A("B1"), oh(12), AL.mult)
-        ts(A("B13"), A("B1"), oh(13), AL.mult)
-        ts(A("hm", 0, 256), A("oneb"), c(cT2), AL.mult)
-        ts(A("Dg"), A("If"), c(cSg), AL.mult)
-        ts(A("B2"), A("B1"), 2.0, AL.mult)
-        ts(A("Bm"), A("B1"), -1.0, AL.mult)
-        ts(A("B16"), A("B1"), -16.0, AL.mult)
-        ts(A("Bj"), A("B1"), c(cWn), AL.mult)
-        ts(A("Bh0"), A("B1"), c(cH0), AL.mult, 0.5, AL.mult)
-        ts(A("Xj"), A("X"), c(cWj), AL.mult)
-        ts(A("Xj4"), A("X"), c(cWj), AL.mult, -4096.0, AL.mult)
-        ts(A("Xh"), A("X"), c(cWh), AL.mult, 0.5, AL.mult)
-        ts(A("Xn"), A("X"), c(cWn), AL.mult)
-        ts(A("Xl"), A("X"), c(cW12), AL.mult, -8192.0, AL.mult)
-        for r in (2, 3, 6, 7):
-            cp((T.BH[:, r:128:16], [("BH", r, r + 1) if r < 7 else ("BH", 7, 128)], []), A("B13" if r & 1 else "B12", r, 128, 16))
+    consts = {
+        "draw": [lambda: ts(A("B2"), A("B1"), 2.0, AL.mult), lambda: ts(A("Bm"), A("B1"), -1.0, AL.mult),
+                 lambda: ts(A("B16"), A("B1"), -16.0, AL.mult), lambda: ms(A("SL", 0, 512), 0.0)],
+        "move": [lambda: ts(c(cWj), c(cWh), -1.0, AL.mult, c(cLo8), AL.add), lambda: ts(c(cT3), c(cLo8), -1.0, AL.add),
+                 lambda: ts(c(cThp), c(cSg), 2.0, AL.mult, col("ts", 0), AL.add), lambda: ts(c(cK), c(cWj), BIG, AL.mult, c(cT3), AL.add),
+                 lambda: ts(A("Dg"), A("If"), c(cSg), AL.mult)],
+        "wait": [lambda: tt(c(cT), c(cW8), c(cW10), AL.add), lambda: ts(c(cHc), c(cH1), float(V), AL.mult, c(cK), AL.add),
+                 lambda: ts(c(cNb0), c(cB0), -1.0, AL.mult, 1.0, AL.add), lambda: ts(c(cWn), c(cWj), 0.5, AL.mult, c(cT), AL.add),
+                 lambda: ts(A("hm", 0, 256), A("oneb"), c(cT2), AL.mult)],
+        "count": [lambda: ts(A("Xl"), A("X"), c(cW12), AL.mult, -8192.0, AL.mult), lambda: ts(A("Xj"), A("X"), c(cWj), AL.mult),
+                  lambda: ts(A("Xj4"), A("X"), c(cWj), AL.mult, -4096.0, AL.mult), lambda: ts(A("Bh0"), A("B1"), c(cH0), AL.mult, 0.5, AL.mult)],
+        "left": [lambda: ts(A("Bj"), A("B1"), c(cWn), AL.mult)],
+        "tail": [lambda: ts(A("Xh"), A("X"), c(cWh), AL.mult, 0.5, AL.mult), lambda: ts(A("Xn"), A("X"), c(cWn), AL.mult)],
+    }
 
-    def constants_c():
-        act(A("dB"), A("q"), bias=4736.0)
-        act(A("dB8"), A("q"), bias=4736.0 - 8192.0)
-        act(A("dP"), A("q"), bias=float(VD))
-        act(A("dP8"), A("q"), bias=VD - 8192.0)
+    def fill(k):
+        for f in consts.pop(k, []):
+            f()
 
     a = lambda k: A("a", 32 * k, 32 * k + 32)
     o = lambda k: A("o", 32 * k, 32 * k + 32)
     ww = A("w", 0, W)
-    early, later = [], []
     for t in range(2):
         pay, land = "pay%d" % t, "land%d" % t
         D = A("Uo", 0, 16)
         cp(A("Uraw", 0, 256), IND(A("bag", 0, 4736), A("P16")))
-        sel(A("pa", 0, 16), "X", "Uraw", 0, 256)
-        for f in early:
-            f()
-        cp(D, A("pa", 0, 16))
+        sel(A("pc", 0, 16), "X", "Uraw", 0, 256)
+        fill("draw")
+        cp(D, A("pc", 0, 16))
         cp(A("N16", 0, 256), IND(A("nbw"), D))
         act(A("Sp"), IND(ww, D), bias=-192.0)
-        cp(A("Nf"), A("N16", 0, 256))
-        cuts = (0, 48, 128, 192, 256)
+        cuts = (0, 72, 136, 192, 256)
 
         def sums(k):
             for i in range(16):
@@ -372,22 +377,22 @@ def rank_program(g, core, T, topo):
         def take(k, f):
             f(A("Gb", 16 * cuts[k], 16 * cuts[k + 1]), IND(ww, A("N16", cuts[k], cuts[k + 1])))
 
-        take(0, act)
+        for k in range(3):
+            take(k, act)
+        cp(A("Nf"), A("N16", 0, 256))
         cp(IND(A("Z"), D), A("oneb"))
-        cp(A("Uw", 0, 16), A("pa", 0, 16))
+        sel(A("pb", 0, 16), "X0", "Nf", 0, 256)
         scan(A("CS"), A("Z", 0, 256), 0.0, AL.max)
         for k in range(2):
-            act(A("junk", 256 * k, 256 * k + 256), A("CS"), scale=-1.0, bias=col("jh", k), f=AF.Sign, acc=col("t2", k))
-        take(1, act)
-        take(2, act)
+            ts(A("junk", 256 * k, 256 * k + 256), A("CS"), col("q", k), AL.is_le)
         for k in range(2):
-            ts(A("Dw", 8 * k, 8 * k + 8), A("Uw", 8 * k, 8 * k + 8), s(sW0 + k), AL.add)
-        sel(A("pb", 0, 16), "X0", "Nf", 0, 256)
+            scan(A("CT", 256 * k, 256 * k + 256), A("junk", 256 * k, 256 * k + 256), 0.0, AL.max)
         mm(A("pm", 0, 256), A("Im"), A("Sp"), True, False)
         mm(A("pm", 0, 256), A("Ic"), A("oneb"), False, False)
         sums(0)
-        ts(A("ix"), A("t2", 0, 2), 0.5, AL.mult, 128.0, AL.add)
-        ts(A("t2", 2, 4), A("t2", 0, 2), 0.5, AL.mult, 128.0, AL.add)
+        cnt = A("CT", 255, 512, 256)
+        cp(A("ix"), cnt)
+        ts(A("t2", 4, 6), cnt, 256.0, AL.is_ge, 4096.0, AL.mult)
         cp(A("NE"), IND(A("nbw"), A("ix")))
         ts(A("SE"), IND(ww, A("ix")), -192.0, AL.add)
         cp(A("GE"), IND(ww, A("NE")))
@@ -395,42 +400,46 @@ def rank_program(g, core, T, topo):
         mm(A("pd", 0, 32), A("Ic"), A("oneb", 0, 32), False, False)
         for i in range(16):
             mm(A("pd", 0, 32), A("I16"), A("GE", i, 512, 16), False, i == 15)
-        ts(A("t2", 4, 6), A("t2", 0, 2), 256.0, AL.is_ge, 4096.0, AL.mult)
-        cp(A("Uo", 16, 32), A("pb", 0, 16))
-        tt(A("t2", 6, 8), A("t2", 2, 4), A("t2", 4, 6), AL.add)
-        cp(A("Uw", 16, 32), A("pb", 0, 16))
+        U, U2 = A("Uo"), A("Uo", 16, 32)
+        tt(A("t2", 6, 8), cnt, A("t2", 4, 6), AL.add)
+        cp(U2, A("pb", 0, 16))
+        ts(A("Dw", 0, 8), A("pc", 0, 8), s(sW0), AL.add)
         tt(A(pay, 32, 34), A("t2", 6, 8), A("K2"), AL.min)
+        ts(A("Dw", 8, 16), A("pc", 8, 16), s(sW1), AL.add)
         ts(A("YE"), A("pd", 0, 32), 187.0, AL.max, 197.0, AL.min)
         tt(A(pay, 0, 32), A("YE"), A("SE"), AL.add)
-        slot = lambda r: T[land][:, 34 * ((r - rank) % N - 1):34 * ((r - rank) % N)]
-        send([(T[pay][:, 0:34], [(cores[r], slot(r)) for r in far], e_far, "ar%d" % t),
-              (T[pay][:, 0:34], [(cores[r], slot(r)) for r in near], e_near, "ar%d" % t)], [A(pay)], "la%d" % t)
-        landed("ar%d" % t, len(e_far) * len(far) + len(e_near) * len(near), [(land, 0, 238)])
+        exchange(A(pay, 0, 34), land, 0, 34, ["%s%d" % (k, t) for k in ("ar", "as", "aw", "la", "lb")])
         take(3, cp)
         for k in (1, 2, 3):
             sums(k)
-        U, U2 = A("Uo"), A("Uo", 16, 32)
-        cp(A("N16", 256, 512), IND(A("nbw"), U2))
         if t == 0:
-            constants_a()
+            place_rows(9, 16)
+            act(A("place", V, VD), A("seq"), bias=2.0 * V + 64.0)
+        act(A("PL64"), IND(A("place", 0, VD), U), bias=(MAGIC - 64.0) * t)
+        act(A("hm", 256, 512), IND(A("Z"), U2), scale=c(cBU), bias=c(cAU))
+        act(A("PL"), A("PL64"), bias=-MAGIC if t else -64.0)
+        cp(A("N16", 256, 512), IND(A("nbw"), U2))
+        fill("move")
         ts(A("Y"), A("pm", 0, 256), 187.0, AL.max, 197.0, AL.min)
         tt(IND(A("w", 0, W + 128), A("Dw")), A("Y"), A("Sp"), AL.add)
         if t == 1:
             dma("y", hbm(T.yx[:]), A("w", 0, V), "dyx")
-        act(A("hm", 256, 512), IND(A("Z"), U2), scale=c(cBU), bias=c(cAU))
+        act(A("Uw", 0, 16), A("pc", 0, 16))
+        act(A("Ab"), A("PL"), bias=c(cCtr), f=AF.Abs)
+        act(A("Uw", 16, 32), A("pb", 0, 16))
         act(A("SU"), IND(ww, U))
+        sel(A("pa", 0, 32), "X0", "PL", 0, 512)
         mm(A("pS"), A("I1"), A("SU"), True, True)
         for k in range(4):
             act(A("SU4", 128 * k, 128 * k + 128), A("SU", 384, 512))
-        if t == 0:
-            constants_b()
-        for f in later:
-            f()
-        act(A("PL"), IND(A("place", 0, VD), U))
-        act(A("Ab"), A("PL"), bias=c(cCtr), f=AF.Abs)
+        fill("wait")
+        if t == 1:
+            ts(A("cm"), A("Ab"), 1152.0, AL.is_lt)
         cp(A("go"), A(land))
         for d in range(N - 1):
             cp(IND(A("w", V + G * d, V + G * d + 2048), A("go", 34 * d + 32, 34 * d + 34)), A(land, 34 * d, 34 * d + 32))
+        if t == 0:
+            ts(A("cm"), A("Ab"), 1152.0, AL.is_lt)
         cp(A("Gb", 0, 16 * 160), IND(ww, A("N16", 0, 160)))
         for lo, hi in ((160, 256), (256, 384), (384, 512)):
             act(A("Gb", 16 * lo, 16 * hi), IND(ww, A("N16", lo, hi)))
@@ -466,30 +475,26 @@ def rank_program(g, core, T, topo):
             b, lo, hi = parts[k]
             act(A("junk", lo, hi), A("Lf", lo, hi), acc=s(sM0 + k))
 
-        sel(A("pa", 0, 32), "X0", "PL", 0, 512)
         for b, lo, hi in parts[:2]:
             mm(A(b, 0, hi - lo), A("B16"), A("SU", lo, hi), True, False)
         for b in dbank[:3]:
             mm(A(b), A("Im"), A("SU4"), True, False)
-        ts(A("cm"), A("Ab"), 1152.0, AL.is_lt)
-        cp(A("PLw"), A("pa", 0, 32))
+        for k in range(3):
+            masks(k)
+        ts(A("PLw"), A("pa", 0, 32), 8192.0, AL.add)
         ts(A("oldw"), A("pa", 0, 32), float(V), AL.is_ge)
         gsum(0, 160, 256)
         gsum(0, 0, 160)
-        for k in range(3):
-            masks(k)
         mm(A("pa"), A("Im"), A("SU4"), True, False)
         for i in range(16):
             vmax(0, i)
             msum(0, i)
             if i == 7:
                 gsum(1, 256, 384)
-        ts(a(7), A("oldw"), -float(V), AL.mult, 8192.0, AL.add)
         for i in range(16):
             mm(A(dbank[i // 4], 128 * (i % 4), 128 * (i % 4) + 128), A("I1"), A("Gb", 16 * 384 + i, 8192, 16), False, i % 4 == 3)
         vmax(1, 0)
         flags(0)
-        tt(A("pos8"), a(7), A("PLw"), AL.add)
         act(s(sT), s(sN1), scale=c(cH1), bias=c(cHc))
         act(s(sTop), s(sN1), bias=float(V))
         act(s(sTH), s(sN0), scale=c(cH0), bias=s(sT))
@@ -507,12 +512,23 @@ def rank_program(g, core, T, topo):
         count(2)
         flags(1)
         count(1)
+        fill("count")
+        if t == 0:
+            act(c(cW810), c(cW10), scale=-1.0, bias=c(cW8))
+            act(c(cMW10), c(cW10), scale=-1.0)
+            act(c(cBc), c(cNb0), scale=float(V))
+            act(A("dB"), A("q"), bias=4736.0 + 8192.0)
+            act(A("dB8"), A("q"), bias=4736.0 - 8192.0)
+            act(A("dP"), A("q"), bias=float(VD))
+            act(A("dP8"), A("q"), bias=VD - 8192.0)
+        else:
+            whole(0)
         for j, l in ((0, "BH"), (1, "B12"), (2, "B13")):
             b = "pc" if j == 0 else "pd"
             for i, k in enumerate((0, 2, 1)):
                 mm(col(b, j), A(l), s(sM0 + k), i == 0, i == 2)
-        m0, m1 = col("pd", 1), col("pd", 2)
         ts(A("cmp"), A("PL"), col("pc", 0), AL.add, s(sTH), AL.is_lt)
+        fill("left")
         tt(A("S", sL0, sL0 + 2), A("S", sN0, sN0 + 2), A("pd", 1, 3), AL.subtract)
         act(s(sDL), s(sL1), bias=s(sN1))
         act(s(sTL), s(sL0), scale=-1.0, bias=s(sTop))
@@ -520,61 +536,68 @@ def rank_program(g, core, T, topo):
         act(s(sD2), s(sL0), scale=-1.0, bias=s(sL1))
         act(s(sB), s(sL0), scale=c(cB0), bias=s(sB1))
         tt(IND(A("Z"), D), A("cmp", 0, 256), A("Lf", 0, 256), AL.mult)
-        ts(a(1), A("q"), m0, AL.is_ge, s(sDL), AL.mult)
-        if t == 0:
-            tt(s(sN0), s(sL0), m1, AL.add)
+        ts(a(1), A("q"), col("pd", 1), AL.is_ge, s(sDL), AL.mult)
         tt(a(2), a(1), A("q"), AL.add)
-        if t == 0:
-            tt(s(sN1), s(sL1), m0, AL.add)
         ts(a(0), a(2), s(sTL), AL.is_ge, 8192.0, AL.mult)
-        ts(a(6), A("oldw"), s(sD2), AL.mult, s(sL0), AL.add)
         tt(a(1), a(2), a(0), AL.add)
         ts(o(0), a(1), s(sL0), AL.add, 4700.0, AL.min)
+        act(s(sR1), s(sD2), bias=float(V))
         act(col("hiB", 0), s(sB))
         act(s(sU), s(sB), scale=c(cW10), bias=c(cMW10))
-        act(A("sraw"), IND(A("bag", 0, 4736), o(0)))
+        act(a(6), A("oldw"), scale=s(sR1), bias=s(sL0))
         act(s(sI), col("hiB", 0), scale=c(cW810), bias=s(sU))
         if t == 0:
+            act(s(sR0), s(sL1), scale=-1.0, bias=s(sN1))
+        act(A("sraw"), IND(A("bag", 0, 4736), o(0)))
+        if t == 0:
+            act(s(sN0), s(sR0), bias=s(sL0))
             act(A("Uraw", 256, 512), IND(A("raw"), U2))
-            constants_c()
+            act(s(sN1), s(sN0), scale=-1.0, bias=float(V))
+        else:
+            whole(1)
         sel(A("pE0", 0, 32), "Xl", "Lf", 0, 512)
         if t == 0:
             sel(A("pE1", 0, 32), "Xl", "Lf", 0, 512, True, False)
         sel(A("pa", 0, 32), "X", "sraw", 0, 512)
         tt(IND(A("Z"), U2), A("cmp", 256, 512), A("Lf", 256, 512), AL.mult)
-        tt(a(7), A("pos8"), A("pE0", 0, 32), AL.add)
+        tt(a(7), A("PLw"), A("pE0", 0, 32), AL.add)
         tt(a(3), A("Uw"), A("pE0", 0, 32), AL.add)
+        tt(a(8), a(7), a(6), AL.is_ge)
+        tt(a(0), a(3), A("dP8"), AL.min)
+        fill("tail")
         cp(o(1), A("pa", 0, 32))
         act(A("Zg"), IND(A("Z"), o(1)), scale=-1.0)
+        act(a(9), a(8), scale=8192.0)
         sel(A("pb", 0, 32), "Xj4", "Zg", 0, 512, True, False)
         scan(A("R"), A("Z"), s(sI), AL.add)
+        if t == 0:
+            iota(A("Z"), [[0, VD]], 0, 0, True)
         scan(A("CL"), A("Zg"), 0.0, AL.min)
         sel(A("pb", 0, 32), "Xj", "CL", 0, 512, False, True)
         mm(col("pc", 2), A("Bh0"), col("R", VD - 1), True, True)
         tt(A("Rg"), IND(A("R"), U), A("cm"), AL.mult)
         if t == 0:
             draw_places(1)
-        ts(a(0), A("pb", 0, 32), 512.0, AL.min)
+        else:
+            for k in range(2, 6):
+                whole(k)
+        ts(a(2), A("pb", 0, 32), 512.0, AL.min)
         ts(a(4), A("oldw"), col("pc", 2), AL.mult, -1.0, AL.add)
-        tt(a(1), a(0), A("q"), AL.add)
+        tt(a(1), a(2), A("q"), AL.add)
         sel(A("pa", 0, 32), "Xh", "Rg", 0, 512)
         if t == 0:
             sel(A("pE1", 0, 32), "Xn", "Rg", 0, 512, False, True)
         mm(A("pS"), A("Bj"), A("Rg"), True, True)
-        if t == 1:
-            act(A("J"), A("pS"))
-        tt(a(8), a(7), a(6), AL.is_ge)
+        act(A("J"), A("pS"), bias=64.0 * (1 - t))
+        ts(o(6), a(0), 8192.0, AL.add)
         cp(o(2), a(1))
         tt(a(5), a(4), A("pa", 0, 32), AL.add)
-        ts(a(9), a(8), 8192.0, AL.mult)
+        if t == 0:
+            tt(a(2), a(9), A("PLw"), AL.add)
         cp(o(3), a(5))
         cp(IND(A("SL"), o(2)), A("sraw"))
         act(A("SR"), IND(A("SL", 0, 512), o(3)))
         sel(A("pb", 0, 32), "X", "SR", 0, 512)
-
-        def place_leavers():
-            tt(a(1), a(3), A("dP8"), AL.min)
-            ts(o(6), a(1), 8192.0, AL.add)
 
         def place_stayers():
             tt(a(4), a(9), A("pb", 0, 32), AL.add)
@@ -582,20 +605,20 @@ def rank_program(g, core, T, topo):
             cp(o(7), a(5))
 
         if t == 0:
+            spread(IND(A("place"), o(6)), A("J"))
             tt(a(0), A("pE1", 0, 32), A("dB8"), AL.min)
-            tt(a(2), a(9), A("PLw"), AL.add)
-            ts(o(4), a(0), 8192.0, AL.add)
             tt(a(1), a(2), A("dB"), AL.min)
-            draw_list()
-            cp(o(5), a(1))
+            ts(o(4), a(0), 8192.0, AL.add)
+            ts(o(5), a(1), -8192.0, AL.add)
             cp(IND(A("bag"), o(4)), A("Uraw"))
-            act(A("Z"), A("R"), scale=0.0)
-            act(A("J"), A("pS"))
+            tt(a(4), a(9), A("pb", 0, 32), AL.add)
+            ts(A("P16", 0, 8), A("dr", 80, 88), s(sBa0), AL.add)
+            tt(a(5), a(4), A("dP"), AL.min)
+            ts(A("P16", 8, 16), A("dr", 88, 96), s(sBa1), AL.add)
+            cp(o(7), a(5))
+            spread(IND(A("place"), o(7)), A("PL64"))
             cp(IND(A("bag"), o(5)), A("SR"))
-            early = [place_leavers, place_stayers]
-            later = [lambda: cp(IND(A("place"), o(6)), A("J")), lambda: cp(IND(A("place"), o(7)), A("PL"))]
         else:
-            place_leavers()
             cp(IND(A("place"), o(6)), A("J"))
             place_stayers()
             cp(IND(A("place"), o(7)), A("PL"))

@@ -1,27 +1,44 @@
 from concourse.bass import DstId, RemoteDMATransfer
-from concourse.mybir import AluOpType as AL, ActivationFunctionType as AF
+from concourse.mybir import AluOpType as AL, ActivationFunctionType as AF, AxisListType as AX
 
 V, G, W = 2304, 256, 4096
 VD = V + 128
+S0 = 128
 BIG = 262144.0
+BL = 8192.0
 MAGIC = 12582912.0
-bf, f32, i32, u16 = "bfloat16", "float32", "int32", "uint16"
+OFF = 192.0
+bf, f32, i32, u16, f16 = "bfloat16", "float32", "int32", "uint16", "float16"
 _SB = {
-    bf: dict(w=5888, bag=5248, raw=VD, Z=VD, R=VD, SL=1024, Gb=8192, Mb=8192, pfl=144, seq=128, oneb=256, B1=128, B2=128, Bm=128, B16=128, Bj=128,
-             Bh0=128, I1=128, I16=128, Im=128, Ic=128, Dg=128, X=144, Xj=144, Xj4=144, Xh=144, Xn=144, Xl=144, junk=512, hiB=2, Uraw=512, Sp=256,
-             Y=256, GE=512, SE=32, YE=32, CS=256, CT=512, pay0=40, pay1=40, land0=238, land1=238, SU=512, SU4=512, cm=512, hm=512, Lf=512,
-             cmp=512, sraw=512, Zg=512, CL=512, Rg=512, SR=512),
-    f32: dict(place=VD + 512, plcf=144, tsf=4, ts=4, rb=8, onef=128, Bt=128, Bu=128, Bf=128, If=128, G8=128, Sel=2048, B12=128, B13=128, BH=128,
-              X0=144, OH=16, jf=80, C=32, q16=32, q=32, j32=8, dB=32, dB8=32, dP=32, dP8=32, K2=2, S=40, Uw=32, Nf=256, t2=8, PL=512, PL64=512,
-              Ab=512, J=512, PLw=32, oldw=32, a=320, dr=96),
-    i32: dict(nbw=VD, plci=144, tsi=4, ohi=16, ohj=16),
-    u16: dict(plc16=144, P16=16, Uo=32, Dw=16, N16=512, ix=2, NE=32, go=238, o=256),
+    bf: dict(w=6016, bag=5248, raw=VD, Z0=VD, Z1=VD, R=VD, ST0=1536, ST1=1536, Gb=8192, Mb=8192, Sel=2048, pfl=144, plh=144, pll=144, seq=128,
+             oneb=256, zer=256, B1=128, W1=64, Wh=64, Wp=64, W8=64, W4=64, KR=512, BE=128, MK=64, Bn0=128, Bn1=128, Bp1=128, B01=128, Bt0=128,
+             Bt1=128, I1=128, I16=128, Im=128, Ic=128, Ib=128, X=144, X01=144, XR=144, XT=144, XJ=144, XC=144, junk=512, PAT=256, SVD=256, SV=512,
+             MV=512, rows=256, Rg=512, Rt=512, Sp=256, Y=256, GE=512, SE=32, YE=32, CS=256, CT=512, pay0=40, pay1=40, gv=224, SU=512,
+             D01=512, FJ=1024, FU=640, JR=512, Xp=144, NF=512, CN=512, HH=1024, SR=512, cT=64, kb=4, tb=2),
+    f16: dict(Nf=256, XN=144),
+    f32: dict(place=VD + 528, TH=64, Dth=64, plcf=144, tsf=4, ts=4, onef=128, Bt=128, Bf=128, If=128, G8=128, B5=128, X0=144, OH=16, jf=256, C=128,
+              q16=32, q=32, qv=32, j32=8, dB=32, dB8=32, dP=32, dS=32, K2=2, tf=4, t2=8, PL=512, Ab=256, J=512, base=512, TSf=512, SL=8704,
+              PR=144, oldw=32, Usw=32, PLw=32, a=1280),
+    i32: dict(nbw=VD, plci=144, tsi=4, ohi=16, ohj=16, bi=4, pi=32),
+    u16: dict(plc16=144, P16=16, Uo=32, Us=32, Dw=32, Ns=512, ix=2, NE=32, go=16, o=384),
 }
-PSUM = ("pS", "pE0", "pE1", "pm", "pa", "pb", "pc", "pd")
+POOL = {}
+for _k, _n in list(_SB[bf].items()):
+    if _n in (128, 144):
+        POOL[_k] = (_SB[bf].get("pool", 0), _n)
+        _SB[bf]["pool"] = POOL[_k][0] + _SB[bf].pop(_k)
+PSUM = ("pS", "pE0", "pE1", "pK", "pa", "pb", "pc", "pd")
 SCRATCH = {k: ("sbuf", [128, n], d) for d, b in _SB.items() for k, n in b.items()}
+SCRATCH["FT"] = ("sbuf", [128, 32, 16], bf)
+SCRATCH["land0"] = SCRATCH["land1"] = ("sbuf", [128, 7, 34], bf)
 SCRATCH.update({k: ("psum", [128, 512], f32) for k in PSUM})
-SEMAPHORES = ["cv", "cs", "cp", "cg", "dx0", "dx1", "dnb", "dpl", "dth", "dsd", "dyx", "dyp", "ga", "gs", "gw", "l0", "l1",
+SEMAPHORES = ["cv", "cs", "cp", "cg", "dx0", "dx1", "dnb", "dpl", "dth", "dsd", "dyx", "dyp", "dr0", "dr1", "ga", "gs", "gw", "l0", "l1",
               "la0", "la1", "lb0", "lb1", "ar0", "ar1", "as0", "as1", "aw0", "aw1"]
+CUT = (0, 64, 128, 192, 256, 320, 384, 448, 512)
+ABS = (0, 0, 8, 8)
+ORDER = """
+0 7 9 6 10 11 8 16 35 34 18 17 32 110 46 19 23 121 158 204 139 186 33 1 117s 119s 113s 201 29s 124s 20s 112 47s 25s 21s 31 13 22 145 86 111s 2 49 115 140 62s 60s 88s 72s 171s 24s 3 52 50 4 114 147 48 12 206 53 55 137 5 54 156 56 58s 57 90s 26s 27s 126s 41 15 207s 59 208 30 42 28s 144s 64s 209 211 84 122s 203s 197s 74s 157s 210 212 142 40s 68 215 213 61 63 85 87 89 130s 148s 76s 123s 80s 172s 192s 78s 109s 118s 65 216s 70s 173s 92s 166s 160s 174s 220s 104s 38s 195s 150s 43 125s 120s 66s 105s 182s 51 82s 175s 14 79 81 67 69 71 83 196s 141s 218s 199s 116s 180s 149s 154s 134s 217 214 108 223s 178s 93s 163s 151s 73 219 221 135 152 187 225 91 75 77 131s 202s 146 95 190 128 155 193 205 133s 226 191 188 168 170 228 101s 129 183 106s 176s 143s 102s 127s 132s 98s 227s 162s 169s 153s 167s 222 232 231 107s 138s 233 234 164s 269 94s 99s 103s 44 45 229 235 270 237 230 236 238 181 165s 100s 96s 198 271 239 159s 39s 224s 161s 36s 97s 177 242 257s 189 240 37 276 241 243 184 258 185 273 279 277 280 245s 246 247 248 272 244 179 249 281 282 290 250 278 200 283 259s 261s 285s 260 289 284 287 274 296 295 297 252 251 291 263s 262 264 298 292 311 320 299 293 318 300 294 317 319 265s 266 267 253 301s 254 321s 194s 303 322 286s 136s 255 304 307s 326s 268 305 324 323 325 306 327 310 331 332 275s 330s 335s 333s 334s 308 256 371 328 368 352 338 342 341 343 312 329 339 340 345 346 347 344 348 358 356 349 355 357 369 372 353 354 359 360 350 375 351 313 361 362 363 374 337s 370 373 336s 388 385 314 364 366 367 376 377 386 365s 387 389 378 383 384 390 391 392 393 379 394 395 380 396 397 315 398 381 316 399 382s 309s 288s 400 401s 302 403 402 412 404 413 431 405 406 419 417 407 408 416 432 434 433s 450 435 420 418 414 421 446 409s 449s 422 443 451 436 444 410s 423 452 453 437 427 415 465s 455 457 439 454 462s 460s 424 459 440 438 441 425s 456s 461 463 428 442 458s 411s 426 464s 445 467 447 429 469s 468 448 470 430 472 471 474 473 475 476 510 477 479 478 480 532 511 481 512 484 482 483 499s 485 505 487s 517 497s 501s 503s 488 489 521 490 486 514 513 491 522 519 498 500 523 502 524 504 525s 492 494 493 506 527s 526s 495 496 529s 564s 538s 518 520 515 531 561 533 537 539 507 563 562 560 508 540 550 516s 569s 565 541 534 542 509 567 566 568 535 543s 528 570 554 577s 573s 578s 571 576s 581 614 611 595 536 574 545 547 575 587 584 585 586 553 582 615 612 613 616 579s 583 588 589 590 591 596 555 600 592 593 594s 598 556 599 601 617 628 597 609 602 631 610 603 604 605 580s 618 606 546 619 629 620 607 632 621 622 557s 630 634 608 635 633 626 627 636 623 466s 549 530s 637 548s 624 638 639 558 640 559 641 642 625s 572 551 643 644s 655 646 552 645 648 544s 656 678 647 649 657 679s 674 662 651 660 650 659 675 663 661 652 653 664 658 676 665 654 666 677 667 670s 668s 669 680 671 672 673 681 682
+"""
 
 
 def rank_program(g, core, T, topo):
@@ -30,12 +47,15 @@ def rank_program(g, core, T, topo):
         return
     N = len(T.cores)
     eng = {"v": g.vector, "s": g.scalar, "p": g.tensor, "g": g, "y": g.sync}
-    known = {k: {} for k in eng}
-    total = {}
-    wr, rd = {}, {}
+    ops = []
 
     def A(name, lo=0, hi=None, step=1, p=None):
+        if name in POOL:
+            at, n = POOL[name]
+            name, lo, hi = "pool", at + lo, at + (n if hi is None else hi)
         t = T[name]
+        if name.startswith("land"):
+            return (t[:, lo // 34:hi // 34, :], [(name, lo, hi)], [])
         if hi is None:
             hi = t.shape[1]
         ps = slice(None) if p is None else p
@@ -47,45 +67,7 @@ def rank_program(g, core, T, topo):
     def IND(win, off):
         return (win[0].indirect(off[0]), win[1], off[1])
 
-    def need(q, toks):
-        best = {}
-        for t in toks:
-            if t[0] not in best or best[t[0]][1] < t[1]:
-                best[t[0]] = t
-        for t in sorted(best.values(), key=lambda t: -len(t[2])):
-            if known[q].get(t[0], 0) < t[1]:
-                eng[q].wait_ge(T.sem[t[0]], t[1])
-                known[q][t[0]] = t[1]
-                for k, c in t[2].items():
-                    if known[q].get(k, 0) < c:
-                        known[q][k] = c
-
-    def deps(q, R, Wr):
-        toks = []
-        for (n, lo, hi) in R:
-            ps = n in PSUM
-            for e in wr.get(n, []):
-                if (ps or (e[0] < hi and lo < e[1])) and not (q == "p" and e[3] == "p"):
-                    toks.append(e[2])
-            if ps:
-                toks += [e[2] for e in rd.get(n, []) if e[3] != q]
-        for (n, lo, hi) in Wr:
-            ps = n in PSUM
-            for e in wr.get(n, []) + rd.get(n, []):
-                if (ps or (e[0] < hi and lo < e[1])) and not (e[3] == q and q == "p"):
-                    toks.append(e[2])
-        return toks
-
-    def note(q, tok, R, Wr):
-        for (n, lo, hi) in Wr:
-            for d in (wr, rd):
-                d[n] = [e for e in d.get(n, []) if not (lo <= e[0] and e[1] <= hi)]
-            wr[n].append((lo, hi, tok, q))
-        for (n, lo, hi) in R:
-            rd[n] = [e for e in rd.get(n, []) if not (e[3] == q and e[2][0] == tok[0] and lo <= e[0] and e[1] <= hi)]
-            rd[n].append((lo, hi, tok, q))
-
-    def run(q, fn, outs, ins, sem=None, inc=1):
+    def run(q, fn, outs, ins, sem=None, inc=1, after=(), join=False):
         R, Wr = [], []
         for o in outs:
             Wr += o[1]
@@ -93,11 +75,12 @@ def rank_program(g, core, T, topo):
         for i in ins:
             if isinstance(i, tuple):
                 R += i[1] + i[2]
-        need(q, deps(q, R, Wr))
-        sem = sem or "c" + q
-        total[sem] = total.get(sem, 0) + inc
-        fn().then_inc(T.sem[sem], inc)
-        note(q if sem == "c" + q else sem, (sem, total[sem], dict(known[q])), R, Wr)
+        if join:
+            op = ops[-1]
+            op.update(fn=op["fn"] + [fn], R=op["R"] + R, W=op["W"] + Wr)
+            return None
+        ops.append(dict(q=q, fn=[fn], R=R, W=Wr, sem=sem, inc=inc, after=after))
+        return len(ops) - 1
 
     def x(a):
         return a[0] if isinstance(a, tuple) else a
@@ -105,8 +88,8 @@ def rank_program(g, core, T, topo):
     def cp(o, i):
         run("v", lambda: g.vector.tensor_copy(o[0], i[0]), [o], [i])
 
-    def tt(o, a, b, op):
-        run("v", lambda: g.vector.tensor_tensor(o[0], a[0], b[0], op), [o], [a, b])
+    def tt(o, a, b, op, join=False):
+        run("v", lambda: g.vector.tensor_tensor(o[0], a[0], b[0], op), [o], [a, b], join=join)
 
     def ts(o, a, s1, op0, s2=None, op1=None):
         if op1 is None:
@@ -117,36 +100,46 @@ def rank_program(g, core, T, topo):
     def ms(o, c):
         run("v", lambda: g.vector.memset(o[0], c), [o], [])
 
-    def scan(o, a, init, op1):
-        run("v", lambda: g.vector.tensor_tensor_scan(o[0], a[0], a[0], x(init), AL.add, op1), [o], [a, init])
+    def scan(o, a, b, init, op0, op1):
+        run("v", lambda: g.vector.tensor_tensor_scan(o[0], a[0], b[0], x(init), op0, op1), [o], [a, b, init])
 
-    def act(o, i, scale=1.0, bias=0.0, f=AF.Identity, acc=None):
-        if acc is None:
-            run("s", lambda: g.scalar.activation(o[0], i[0], f, bias=x(bias), scale=x(scale)), [o], [i, scale, bias])
-        else:
-            run("s", lambda: g.scalar.activation(o[0], i[0], f, bias=x(bias), scale=x(scale), accum_out=acc[0]), [o, acc], [i, scale, bias])
+    def act(o, i, f, bias=0.0):
+        run("s", lambda: g.scalar.activation(o[0], i[0], f, bias=x(bias)), [o], [i, bias])
+
+    def lin(o, i, scale=1.0, bias=0.0):
+        def fn(q):
+            if q == "s":
+                return g.scalar.activation(o[0], i[0], AF.Identity, bias=x(bias), scale=x(scale))
+            if scale == 1.0 and bias == 0.0:
+                return g.vector.tensor_copy(o[0], i[0])
+            return g.vector.tensor_scalar(o[0], i[0], x(scale), x(bias), AL.mult, AL.add)
+        run("?", fn, [o], [i, scale, bias])
+
+    def total_of(o, i, junk):
+        run("?", lambda q: g.scalar.activation(junk[0], i[0], AF.Identity, accum_out=o[0]) if q == "s" else
+            g.vector.tensor_reduce(o[0], i[0], AX.X, AL.add), [o, junk], [i])
 
     def spread(o, i):
         run("s", lambda: g.scalar.activation(o[0], i[0], AF.Silu), [o], [i])
 
-    def mm(o, l, r, start, stop):
-        run("p", lambda: g.tensor.matmul(o[0], l[0], r[0], start, stop), [o], [l, r])
+    def mm(o, l, r, start, stop, join=False):
+        run("p", lambda: g.tensor.matmul(o[0], l[0], r[0], start, stop), [o], [l, r], join=join)
 
     def sel(o, xn, name, lo, hi, start=True, stop=True):
         for r in range(16):
-            mm(o, A(xn, 15 - r, 143 - r), A(name, lo + r, hi, 16), start and r == 0, stop and r == 15)
+            mm(o, A(xn, 15 - r, 143 - r), A(name, lo + r, hi, 16), start and r == 0, stop and r == 15, r > 0)
 
-    def iota(o, pat, base, cmul, small=False):
+    def iota(o, pat, base, cmul, small=False, after=()):
         if small:
-            run("g", lambda: g.iota(o[0], pat, base, cmul, allow_small_or_imprecise_dtypes=True), [o], [])
+            run("g", lambda: g.iota(o[0], pat, base, cmul, allow_small_or_imprecise_dtypes=True), [o], [], after=after)
         else:
             run("g", lambda: g.iota(o[0], pat, base, cmul), [o], [])
 
     def asel(o, i, pat, op, base, cmul):
         run("g", lambda: g.affine_select(o[0], i[0], pat, op, 0.0, base, cmul), [o], [i])
 
-    def dma(q, o, i, sem):
-        run(q, lambda: eng[q].dma_start(o[0], i[0]), [o], [i], sem, 16)
+    def dma(q, o, i, sem, after=()):
+        return run(q, lambda: eng[q].dma_start(o[0], i[0]), [o], [i], sem, 16, after)
 
     def hbm(ap):
         return (ap, [], [])
@@ -158,19 +151,13 @@ def rank_program(g, core, T, topo):
     def bits(es):
         return sum(1 << e for e in es)
 
-    def send(trs, srcs, lsem):
-        R = []
-        for s in srcs:
-            R += s[1]
-        need("g", deps("g", R, []))
-        g.remote_dma_fused([RemoteDMATransfer(dst_ids=[dst(c) for c, _a in ds], dma_engine_mask=bits(es), remote_sem=T.sem[rs],
-                                              srcs=[s], dsts=[a for _c, a in ds]) for s, ds, es, rs in trs], local_sem=T.sem[lsem])
-        total[lsem] = total.get(lsem, 0) + sum(len(t[2]) for t in trs)
-        note(lsem, (lsem, total[lsem], dict(known["g"])), R, [])
+    def send(trs, src, lsem):
+        return run("g", lambda: g.remote_dma_fused([RemoteDMATransfer(
+            dst_ids=[dst(c) for c, _a in ds], dma_engine_mask=bits(es), remote_sem=T.sem[rs], srcs=[s], dsts=[a for _c, a in ds])
+            for s, ds, es, rs in trs], local_sem=T.sem[lsem]), [], [src], lsem, -sum(len(t[2]) for t in trs))
 
-    def landed(sem, n, regions):
-        total[sem] = n
-        note(sem, (sem, n, {}), [], regions)
+    def landed(sem, n, region, at):
+        run(None, None, [(None, [region], [])], [], sem, n, [at])
 
     cores = list(T.cores)
     others = [(rank + d) % N for d in range(1, N)]
@@ -188,33 +175,43 @@ def rank_program(g, core, T, topo):
 
     takers = [r for r in far if rank in takes(r)]
     mine = takes(rank)
+    slots_first = sorted((rank - k) % N - 1 for k in mine + [sib])
+    slots_last = sorted((rank - k) % N - 1 for k in takes(sib))
 
-    def exchange(src, buf, base, n, sems, between=None):
+    def exchange(src, buf, base, n, sems):
         def span(recv, ss):
             return base + n * ((recv - ss[0]) % N - 1), base + n * ((recv - ss[-1]) % N)
         s_far, s_near, s_on, l0, l1 = sems
-        send([(src[0], [(cores[r], A(buf, *span(r, [rank]))[0]) for r in takers], e_far, s_far),
-              (src[0], [(cores[sib], A(buf, *span(sib, [rank]))[0])], e_near, s_near)], [src], l0)
-        landed(s_far, len(e_far) * len(mine), [(buf,) + span(rank, mine)])
-        landed(s_near, len(e_near), [(buf,) + span(rank, [sib])])
-        if between:
-            between()
+        at = send([(src[0], [(cores[r], A(buf, *span(r, [rank]))[0]) for r in takers], e_far, s_far),
+                   (src[0], [(cores[sib], A(buf, *span(sib, [rank]))[0])], e_near, s_near)], src, l0)
+        landed(s_far, len(e_far) * len(mine), (buf,) + span(rank, mine), at)
+        landed(s_near, len(e_near), (buf,) + span(rank, [sib]), at)
         fw = A(buf, *span(rank, mine))
-        send([(fw[0], [(cores[sib], A(buf, *span(sib, mine))[0])], e_all, s_on)], [fw], l1)
-        landed(s_on, len(e_all), [(buf,) + span(rank, takes(sib))])
+        at = send([(fw[0], [(cores[sib], A(buf, *span(sib, mine))[0])], e_all, s_on)], fw, l1)
+        landed(s_on, len(e_all), (buf,) + span(rank, takes(sib)), at)
+        return at
 
-    dma("y", A("w", 0, G), hbm(T.x[:, 0:G]), "dx0")
+    k = dma("y", A("w", S0, S0 + G), hbm(T.x[:, 0:G]), "dx0")
     dma("s", A("plci"), hbm(T.plc[:]), "dpl")
-    dma("y", A("tsi", 0, 1, p=slice(0, 8)), hbm(T.th[:]), "dth")
-    dma("y", A("tsi", 1, 3, p=slice(0, 8)), hbm(T.sd[:]), "dsd")
-    dma("y", A("nbw", 0, V), hbm(T.nb[:]), "dnb")
-    dma("y", A("w", G, V), hbm(T.x[:, G:V]), "dx1")
+    k = dma("y", A("tsi", 0, 1, p=slice(0, 8)), hbm(T.th[:]), "dth", [k])
+    k = dma("y", A("tsi", 1, 3, p=slice(0, 8)), hbm(T.sd[:]), "dsd", [k])
+    k = dma("y", A("nbw", 0, V), hbm(T.nb[:]), "dnb", [k])
+    dma("y", A("w", S0 + G, S0 + V), hbm(T.x[:, G:V]), "dx1", [k])
 
-    cR, cB0, cA, cLo8, cH0, cH1, cW8, cW10, cW12, cSg, cCtr, cAU, cBU, cWh, cWj, cHc, cWn, cThp, cNb0, cBc, cW810, cMW10, cT, cK, cT2, cT3 = range(26)
-    sN0, sN1, sL0, sL1, sT, sTH, sDL, sB1, sB, sU, sI, sE0, sE1, sV0, sV1, sBa0, sBa1, sW0, sW1, sb0, sb1, sM0, sM1, sM2, sD2, sTop, sTL, sR0, sR1, sT1 = range(30)
-    c = lambda k: col("C", k)
-    s = lambda k: col("S", k)
     oh = lambda k: col("OH", k)
+    used = {"C": 0, "a": 0, "jf": 0}
+
+    def new(name, n):
+        used[name] += n
+        return A(name, used[name] - n, used[name])
+
+    def via(f, name="C", n=1):
+        t = new(name, n)
+        f(t)
+        return t
+
+    c = lambda i, scale=1.0, bias=0.0: via(lambda t: lin(t, i, scale, bias))
+    ones = lambda lo, hi, step=1: via(lambda t: total_of(t, A("OH", lo, hi, step), new("jf", len(range(lo, hi, step)))))
     ms(A("onef"), 1.0)
     iota(A("ohi"), [[-1, 16]], 128, 1)
     iota(A("seq"), [[1, 128]], 0, 0, True)
@@ -222,405 +219,372 @@ def rank_program(g, core, T, topo):
     asel(A("Bt"), A("onef"), [[-16, 8], [0, 16]], AL.is_ge, 0, 1)
     asel(A("Bf"), A("Bt"), [[16, 8], [0, 16]], AL.is_ge, 15, -1)
     asel(A("G8"), A("onef"), [[1, 8], [0, 16]], AL.is_equal, 0, -1)
+    asel(A("If"), A("onef"), [[-1, 128]], AL.is_equal, 0, 1)
+    iota(A("nbw", V, VD), [[1, 128]], V, 0)
+    iota(A("Z0", 1216, VD), [[0, VD - 1216]], 0, 0, True)
     ts(A("ohj"), A("ohi"), 15, AL.bitwise_and)
-    ms(A("Z", 0, 400), 0.0)
     ts(A("OH"), A("ohj"), 0.0, AL.is_equal)
-    cp(c(cR), col("ohj", 0))
-    for k in range(5):
-        act(col("rb", k), oh(0), scale=128.0 * 2 ** k)
-    ts(A("raw", 0, 128), A("seq"), oh(1), AL.mult)
+    cR = via(lambda t: cp(t, col("ohj", 0)))
+    rb = c(oh(0), 128.0)
+    lin(A("raw", 0, 128), A("seq"), oh(1), c(oh(1), 64.0, rb))
     for k in range(5):
         n = 128 * 2 ** k
-        m = min(n, VD - n)
-        if k < 3:
-            ms(A("Z", 400 + 272 * k, 672 + 272 * k), 0.0)
-        ts(A("raw", n, n + m), A("raw", 0, m), col("rb", k), AL.add)
-
-    def meanwhile():
-        asel(A("If"), A("onef"), [[-1, 128]], AL.is_equal, 0, 1)
-        iota(A("nbw", V, VD), [[1, 128]], V, 0)
-        iota(A("Z", 1216, VD), [[0, VD - 1216]], 0, 0, True)
-
-    exchange(A("w", 0, G), "w", V, G, ("ga", "gs", "gw", "l0", "l1"), meanwhile)
-    asel(A("B12"), A("onef"), [[-16, 8], [0, 16]], AL.is_equal, -12, 1)
-    asel(A("B13"), A("onef"), [[-16, 8], [0, 16]], AL.is_equal, -13, 1)
-    asel(A("BH"), A("onef"), [[-16, 8], [0, 8], [-1, 2]], AL.is_equal, -12, 1)
-    asel(A("Bu"), A("BH"), [[0, 8], [1, 2], [0, 8]], AL.is_equal, 0, 0)
-    asel(A("BH"), A("Bu"), [[0, 32], [1, 2], [0, 2]], AL.is_equal, -1, 0)
-
-    def osum(k, lo, hi, step=1):
-        act(A("jf", 8 * k, 8 * k + len(range(lo, hi, step))), A("OH", lo, hi, step), acc=c(k))
-
-    act(A("q"), A("q16"), bias=c(cR))
-    act(A("B1"), A("Bf"))
-    for r in range(16):
-        act(A("Sel", 128 * r, 128 * r + 128), A("Bf"), scale=oh(r))
+        lin(A("raw", n, min(2 * n, VD)), A("raw", 0, min(n, VD - n)), 1.0, c(oh(0), float(n)) if k else rb)
+    for lo in range(0, 1216, 304):
+        ms(A("Z0", lo, lo + 304), 0.0)
+    ms(A("zer"), 0.0)
+    for lo in (0, 256):
+        lin(A("ST0", 512 + lo, 768 + lo), A("zer"))
+        lin(A("SL", lo, lo + 256), A("zer"))
+    lin(A("w", 0, S0), A("zer", 0, S0))
+    exchange(A("w", S0, S0 + G), "w", S0 + V, G, ("ga", "gs", "gw", "l0", "l1"))
+    lin(A("q"), A("q16"), 1.0, cR)
+    lin(A("B1"), A("Bf"))
     cp(A("plc16"), A("plci"))
     cp(A("plcf"), A("plci"))
     cp(A("tsf", 0, 3, p=slice(0, 8)), A("tsi", 0, 3, p=slice(0, 8)))
     cp(IND(A("bag", 0, 2 * V), A("plc16")), A("raw", 0, V))
-    act(A("pfl"), A("plcf"), scale=-1.0, bias=V - 0.5, f=AF.Sign)
+    ts(A("pfl"), A("plcf"), float(V), AL.is_lt)
     mm(A("pc", 0, 144), A("B1"), A("pfl"), True, True)
     mm(A("pd", 0, 3), A("G8", p=slice(0, 8)), A("tsf", 0, 3, p=slice(0, 8)), True, True)
-    banks = ("pm", "pb", "pa", "pS", "pE0", "pE1")
+    n2 = new("C", 2)
+    n0, n1 = A("C", used["C"] - 2, used["C"] - 1), A("C", used["C"] - 1, used["C"])
+    total_of(n0, A("pc", 0, 144), new("jf", 144))
+    lin(A("ts", 0, 3), A("pd", 0, 3))
+    n13 = c(n0, 13.0)
+    lin(A("plh"), A("plcf"))
+    tt(A("pll"), A("plcf"), A("plh"), AL.subtract)
+    banks = ("pK", "pS", "pE0", "pE1", "pb", "pa")
     for r in range(16):
-        mm(A(banks[r // 3], 144 * (r % 3), 144 * (r % 3) + 144), A("Sel", 128 * r, 128 * r + 128), A("plcf"), True, True)
-    act(A("X"), A("Z", 0, 144))
-    act(A("j32"), A("q", 0, 8), scale=32.0)
-    act(A("junk", 0, 144), A("pc", 0, 144), acc=s(sT))
-    act(A("ts", 0, 3), A("pd", 0, 3))
-    act(s(sN0), s(sT), scale=0.5, bias=0.5 * V)
-    act(s(sN1), s(sT), scale=-0.5, bias=0.5 * V)
-    act(A("X", 15, 143, 16), A("Bf", 0, 128, 16))
+        lin(A("Sel", 128 * r, 128 * r + 128), A("B1"), oh(r))
+        for k, h in enumerate(("plh", "pll")):
+            mm(A(banks[r // 3], 144 * (r % 3), 144 * (r % 3) + 144), A("Sel", 128 * r, 128 * r + 128), A(h), k == 0, k == 1, k == 1)
+    for r in range(16):
+        lin((T.place[:, r:V:16], [("place", r, r + 1) if r < 15 else ("place", 15, V)], []),
+            A(banks[r // 3], 144 * (r % 3), 144 * (r % 3) + 144), 1.0, 64.0)
+    lin(A("place", V, VD), A("seq"), 1.0, 2.0 * V + 64.0)
+    lin(A("bag", 2 * V, 4736), A("raw", V, VD))
+    lin(A("X"), A("zer", 0, 144))
+    lin(A("X", 15, 143, 16), A("Bf", 0, 128, 16))
+    lin(A("j32"), A("q", 0, 8), 32.0)
 
-    def draw_places(t):
-        n2 = A("S", sN0, sN0 + 2)
-        dr = lambda k, n=2: A("dr", 16 * k, 16 * k + n)
-        act(s(sT1), s(sN0), scale=13.0, bias=41.0 * t)
-        act(A("S", sV0, sV0 + 2), n2, scale=-1.0, bias=127.5, f=AF.Sign)
-        act(dr(0), A("ts", 1, 3), bias=s(sT1))
-        act(A("S", sR0, sR0 + 2), n2, bias=-128.0, f=AF.Relu)
-        act(dr(1), dr(0), scale=1.0 / 32, bias=-31.0 / 64)
-        act(s(sBa0), s(sV0), scale=float(V), bias=V + 0.5 * V - MAGIC)
-        act(dr(2), dr(1), bias=MAGIC)
-        act(s(sBa1), s(sV1), scale=0.5 * V, bias=1.5 * V + 0.5 * V - MAGIC)
-        act(dr(1), dr(2), scale=-32.0, bias=32.0 * MAGIC)
-        act(A("S", sE0, sE0 + 2), A("S", sR0, sR0 + 2), bias=128.0)
-        for k in range(2):
-            act(s(sb0 + k), A("dr", 16 + k, 17 + k), bias=A("dr", k, k + 1))
-        act(A("S", sW0, sW0 + 2), A("S", sV0, sV0 + 2), scale=0.5 * (W - V), bias=0.5 * (W - V))
-        for k in range(2):
-            act(A("dr", 32 + k, 33 + k), s(sb0 + k), scale=s(sE0 + k), bias=-0.5 * V * 4096)
-        for k in range(2):
-            act(A("dr", 48 + 8 * k, 56 + 8 * k), A("j32"), scale=s(sE0 + k), bias=A("dr", 32 + k, 33 + k))
-        act(dr(4, 16), dr(3, 16), scale=1.0 / 4096, bias=-0.5 + 1.0 / 8192)
-        act(dr(5, 16), dr(4, 16), bias=MAGIC)
+    c01, cT0, cT1, c8A, c45, c67, c23, cB0 = (ones(*k) for k in ((0, 2), (4, 7, 2), (5, 8, 2), (8, 12), (4, 6), (6, 8), (2, 4), (1, 16, 2)))
+    ms(A("oneb"), 1.0)
+    lin(A("X01"), A("X"), c01)
+    c0, c1 = c(cT0, 1.0, oh(10)), ones(5, 12, 2)
+    lin(A("PAT", 0, 128), A("oneb", 0, 128), c0, oh(8))
+    lin(A("PAT", 128, 256), A("oneb", 0, 128), c1, oh(8))
+    cD, cU = c(c8A, -1.0, c45), c(c8A, -1.0, c67)
+    ts(A("BE"), A("B1"), oh(8), AL.mult, -1.0, AL.mult)
+    lin(A("K2"), A("q", 0, 2), 8.0, 1792.0)
+    cS1, cS2 = c(cB0, -2.0, 1.0), c(cB0, 2.0 * V)
+    cCtr, cHalf, cSign = c(c1, -float(V), -(64.0 + 1151.5)), c(c(c0, 1.0, c1), 1152.0), c(c0, -2.0, 1.0)
+    ts(A("XN"), A("X"), oh(0), AL.mult)
+    lin(A("X0"), A("X"), oh(0))
+    lin(A("B5"), A("Bf"), oh(5))
+    lin(A("I1"), A("If"))
+    for k, f in (("I16", 1.0 / 16), ("Im", -1.0), ("Ic", -15.0 / 32), ("Ib", -BIG)):
+        lin(A(k), A("I1"), f)
+    c47, cN9 = ones(4, 8), c(oh(9), -1.0)
+    cXT, cXR = c(oh(10), -BL, c(oh(11), -BL - 256.0, c47)), c(ones(8, 11, 2), BL, c(oh(11), BL - 256.0, c47))
+    lin(A("Xp"), A("X"), ones(12, 14))
+    for k in range(4):
+        lin(A("JR", 128 * k, 128 * k + 128), A("seq"), oh(13), c(oh(12), 128.0 * k + 128.0))
+    for k, f in (("XJ", c(c45, -BL, c01)), ("XC", c(c45, 4.0, c23))):
+        lin(A(k), A("X"), f)
+    for k, f in (("Bt0", cT0), ("Bt1", cT1), ("Bp1", oh(1)), ("B01", c01)):
+        lin(A(k), A("B1"), f)
+    lin(A("Bn0"), A("Sel", 0, 128), -1.0)
+    lin(A("Bn1"), A("Sel", 128, 256), -1.0)
+    for r in range(4):
+        lin(A("W1", r, 64, 4), A("B1", 0, 128, 8), 1.0 if r in (0, 3) else -1.0)
+    for r in range(2):
+        lin(A("MK", r, 64, 2), A("Sel", 128 * (4 + r), 128 * (5 + r), 4), BIG / 2)
+    lin(A("Wh"), A("W1"), -0.5)
+    lin(A("W8"), A("W1"), -8.0)
+    lin(A("W4"), A("W1"), -4.0)
+    lin(A("Wp"), A("W1"), 0.5)
+    lin(A("Dth"), A("W1"), c(col("ts", 0), 1.0 / 32, -1.0 / 64))
+    mm(A("pS", 0, 64), A("onef"), A("Dth"), True, True)
+    lin(A("TH"), A("pS", 0, 64), 1.0, BIG / 2)
+    ms((T.FT[:], [("FT", 0, 512)], []), 0.0)
+    ms(A("cT", 0, 16), 2 * BL)
+    ms(A("cT", 16, 32), BL)
+    ms(A("cT", 32, 64), -BL)
+    for k, f in enumerate((256.0, float(V))):
+        ms(col("kb", k), f)
+    c03 = c(c01, 1.0, c23)
+    for lo in (0, 256):
+        lin(A("D01", lo, lo + 256), A("oneb"), c03)
+    lin(A("KR", 0, 128), A("seq"), c45, c(c45, 128.0, c03))
+    for n in (128, 256):
+        lin(A("KR", n, 2 * n), A("KR", 0, n), c(c45, n / 64.0 - 1.0, 1.0))
+    lin(A("FU", 0, 16), A("oneb", 0, 16), oh(2), oh(6))
+    for k, f, b in (("dS", 1.0, 513.0), ("dB", 1.0 / BL, 4736.0 / BL), ("dB8", 1.0, 4800.0 - BL), ("dP", 1.0, VD + 1 + OFF),
+                    ("qv", 1.0, -255.0 - V)):
+        lin(A(k), A("q"), f, b)
 
-    def draw_list():
-        for k in range(2):
-            ts(A("P16", 8 * k, 8 * k + 8), A("dr", 80 + 8 * k, 88 + 8 * k), s(sBa0 + k), AL.add)
-
-    def place_rows(r0, r1):
-        for r in range(r0, r1):
-            act((T.place[:, r:V:16], [("place", r, r + 1) if r < 15 else ("place", 15, V)], []),
-                A(banks[r // 3], 144 * (r % 3), 144 * (r % 3) + 144), bias=64.0)
-
-    def whole(k):
-        v = A("place", 768 * (k // 2), 768 * (k // 2) + 768)
-        act(v, v, bias=MAGIC - 64.0 if k % 2 == 0 else -MAGIC)
-
-    draw_places(0)
-    draw_list()
-    act(A("bag", 2 * V, 4736), A("raw", V, VD))
-    act(A("oneb"), A("Z", 0, 256), bias=1.0)
-    act(A("I16"), A("If"), scale=1.0 / 16)
-    act(A("Im"), A("If"), scale=-1.0)
-    act(A("Ic"), A("If"), scale=-15.0 / 32)
-    act(A("K2"), A("q", 0, 2), scale=8.0, bias=1792.0)
-    act(A("X0"), A("X"), scale=oh(0))
-    place_rows(0, 9)
-
-    osum(cB0, 1, 16, 2)
-    osum(cA, 0, 4)
-    osum(cLo8, 0, 8)
-    osum(cH0, 2, 7, 4)
-    osum(cH1, 3, 8, 4)
-    osum(cW8, 8, 10)
-    osum(cW10, 10, 12)
-    osum(cW12, 12, 14)
-    act(c(cSg), c(cB0), scale=-2.0 * BIG, bias=BIG)
-    act(c(cCtr), c(cB0), scale=-float(V), bias=-1151.5)
-    act(c(cT), c(cA), scale=-1.0, bias=c(cLo8))
-    act(c(cT2), c(cA), bias=c(cW12))
-    act(c(cWh), c(cH0), bias=c(cH1))
-    act(c(cAU), c(cT), bias=c(cW12))
-    act(A("I1"), A("If"))
-    act(c(cBU), c(cAU), scale=-1.0, bias=c(cA))
-
-    consts = {
-        "draw": [lambda: ts(A("B2"), A("B1"), 2.0, AL.mult), lambda: ts(A("Bm"), A("B1"), -1.0, AL.mult),
-                 lambda: ts(A("B16"), A("B1"), -16.0, AL.mult), lambda: ms(A("SL", 0, 512), 0.0)],
-        "move": [lambda: ts(c(cWj), c(cWh), -1.0, AL.mult, c(cLo8), AL.add), lambda: ts(c(cT3), c(cLo8), -1.0, AL.add),
-                 lambda: ts(c(cThp), c(cSg), 2.0, AL.mult, col("ts", 0), AL.add), lambda: ts(c(cK), c(cWj), BIG, AL.mult, c(cT3), AL.add),
-                 lambda: ts(A("Dg"), A("If"), c(cSg), AL.mult)],
-        "wait": [lambda: tt(c(cT), c(cW8), c(cW10), AL.add), lambda: ts(c(cHc), c(cH1), float(V), AL.mult, c(cK), AL.add),
-                 lambda: ts(c(cNb0), c(cB0), -1.0, AL.mult, 1.0, AL.add), lambda: ts(c(cWn), c(cWj), 0.5, AL.mult, c(cT), AL.add),
-                 lambda: ts(A("hm", 0, 256), A("oneb"), c(cT2), AL.mult)],
-        "count": [lambda: ts(A("Xl"), A("X"), c(cW12), AL.mult, -8192.0, AL.mult), lambda: ts(A("Xj"), A("X"), c(cWj), AL.mult),
-                  lambda: ts(A("Xj4"), A("X"), c(cWj), AL.mult, -4096.0, AL.mult), lambda: ts(A("Bh0"), A("B1"), c(cH0), AL.mult, 0.5, AL.mult)],
-        "left": [lambda: ts(A("Bj"), A("B1"), c(cWn), AL.mult)],
-        "tail": [lambda: ts(A("Xh"), A("X"), c(cWh), AL.mult, 0.5, AL.mult), lambda: ts(A("Xn"), A("X"), c(cWn), AL.mult)],
-    }
-
-    def fill(k):
-        for f in consts.pop(k, []):
-            f()
-
-    a = lambda k: A("a", 32 * k, 32 * k + 32)
     o = lambda k: A("o", 32 * k, 32 * k + 32)
-    ww = A("w", 0, W)
+    a = lambda f: via(f, "a", 32)
+    two = lambda f: (via(f, "C", 2), A("C", used["C"] - 2, used["C"] - 1), A("C", used["C"] - 1, used["C"]))
+    ww, own = A("w", S0, S0 + W), A("w", 0, S0 + V)
+    D, U, U2, Us = A("Uo", 0, 16), A("Uo"), A("Uo", 16, 32), A("Us")
+    row = A("place", 0, V, p=slice(5, 128, 16))
     for t in range(2):
-        pay, land = "pay%d" % t, "land%d" % t
-        D = A("Uo", 0, 16)
-        cp(A("Uraw", 0, 256), IND(A("bag", 0, 4736), A("P16")))
-        sel(A("pc", 0, 16), "X", "Uraw", 0, 256)
-        fill("draw")
-        cp(D, A("pc", 0, 16))
-        cp(A("N16", 0, 256), IND(A("nbw"), D))
-        act(A("Sp"), IND(ww, D), bias=-192.0)
-        cuts = (0, 72, 136, 192, 256)
-
-        def sums(k):
-            for i in range(16):
-                mm(A("pm", cuts[k], cuts[k + 1]), A("I16"), A("Gb", 16 * cuts[k] + i, 16 * cuts[k + 1], 16), False, k == 3 and i == 15)
-
-        def take(k, f):
-            f(A("Gb", 16 * cuts[k], 16 * cuts[k + 1]), IND(ww, A("N16", cuts[k], cuts[k + 1])))
-
-        for k in range(3):
-            take(k, act)
-        cp(A("Nf"), A("N16", 0, 256))
-        cp(IND(A("Z"), D), A("oneb"))
-        sel(A("pb", 0, 16), "X0", "Nf", 0, 256)
-        scan(A("CS"), A("Z", 0, 256), 0.0, AL.max)
+        pay, land, Z, ST = "pay%d" % t, "land%d" % t, "Z%d" % t, "ST%d" % t
+        lin(n1, n0, -1.0, float(V))
+        ts(A("bi", 0, 2), A("ts", 1, 3), n13, AL.add, 41.0 * t, AL.add)
+        ts(A("bi", 2, 4), A("bi", 0, 2), 31, AL.bitwise_and)
+        b2 = two(lambda k: cp(k, A("bi", 2, 4)))
+        e2 = two(lambda k: ts(k, n2, 128.0, AL.max))
+        v2 = two(lambda k: ts(k, n2, 128.0, AL.is_ge))
         for k in range(2):
-            ts(A("junk", 256 * k, 256 * k + 256), A("CS"), col("q", k), AL.is_le)
+            ts(A("pi", 8 * k, 8 * k + 8), A("j32"), b2[1 + k], AL.add, e2[1 + k], AL.mult)
+            lin(A("SVD", 128 * k, 128 * k + 128), A("PAT", 128 * k, 128 * k + 128), v2[1 + k])
+        ts(A("pi", 16, 32), A("pi", 0, 16), 12, AL.arith_shift_right)
         for k in range(2):
-            scan(A("CT", 256 * k, 256 * k + 256), A("junk", 256 * k, 256 * k + 256), 0.0, AL.max)
-        mm(A("pm", 0, 256), A("Im"), A("Sp"), True, False)
-        mm(A("pm", 0, 256), A("Ic"), A("oneb"), False, False)
-        sums(0)
+            ts(A("P16", 8 * k, 8 * k + 8), A("pi", 16 + 8 * k, 24 + 8 * k), c(v2[1 + k], (k - 2.0) * V, 2.0 * V), AL.add)
+        w2 = two(lambda k: lin(k, v2[0], float(V + S0), -V - OFF))
+        dn, top = c(n0, -2.0, float(V)), c(n0, cS1, cS2)
+        tt(A("SV", 0, 256), IND(A("bag", 0, 4736), A("P16")), A("SVD"), AL.add)
+        sel(A("pc", 0, 16), "X01", "SV", 0, 256)
+        lin(A("MV", 0, 256), A("SV", 0, 256), cD)
+        ts(D, A("pc", 0, 16), -OFF, AL.add)
+        for k in range(2):
+            ts(A("Dw", 8 * k, 8 * k + 8), A("pc", 8 * k, 8 * k + 8), w2[1 + k], AL.add)
+        cp(A("Ns", 0, 256), IND(A("nbw"), D))
+        cp(IND(A(Z), D), A("MV", 0, 256))
+        mm(A("pa", 0, 256), A("BE"), A(Z, 0, 256), True, True)
+        scan(A("CS"), A("pa", 0, 256), A("zer"), 0.0, AL.add, AL.add)
+        for k in range(2):
+            h = A("junk", 256 * k, 256 * k + 256)
+            ts(h, A("CS"), col("q", k), AL.is_le)
+            scan(A("CT", 256 * k, 256 * k + 256), h, h, 0.0, AL.add, AL.max)
         cnt = A("CT", 255, 512, 256)
         cp(A("ix"), cnt)
-        ts(A("t2", 4, 6), cnt, 256.0, AL.is_ge, 4096.0, AL.mult)
         cp(A("NE"), IND(A("nbw"), A("ix")))
-        ts(A("SE"), IND(ww, A("ix")), -192.0, AL.add)
-        cp(A("GE"), IND(ww, A("NE")))
-        mm(A("pd", 0, 32), A("Im"), A("SE"), True, False)
-        mm(A("pd", 0, 32), A("Ic"), A("oneb", 0, 32), False, False)
-        for i in range(16):
-            mm(A("pd", 0, 32), A("I16"), A("GE", i, 512, 16), False, i == 15)
-        U, U2 = A("Uo"), A("Uo", 16, 32)
+        lin(A("SE"), IND(A("w", S0, S0 + 272), A("ix")), 1.0, -192.0)
+        ts(A("t2", 4, 6), cnt, 256.0, AL.is_ge, 4096.0, AL.mult)
         tt(A("t2", 6, 8), cnt, A("t2", 4, 6), AL.add)
-        cp(U2, A("pb", 0, 16))
-        ts(A("Dw", 0, 8), A("pc", 0, 8), s(sW0), AL.add)
         tt(A(pay, 32, 34), A("t2", 6, 8), A("K2"), AL.min)
-        ts(A("Dw", 8, 16), A("pc", 8, 16), s(sW1), AL.add)
+        lin(A("GE"), IND(ww, A("NE")))
+        mm(A("pd", 0, 32), A("Im"), A("SE"), True, False)
+        mm(A("pd", 0, 32), A("Ic"), A("oneb", 0, 32), False, False, True)
+        for i in range(16):
+            mm(A("pd", 0, 32), A("I16"), A("GE", i, 512, 16), False, i == 15, i > 0)
         ts(A("YE"), A("pd", 0, 32), 187.0, AL.max, 197.0, AL.min)
         tt(A(pay, 0, 32), A("YE"), A("SE"), AL.add)
-        exchange(A(pay, 0, 34), land, 0, 34, ["%s%d" % (k, t) for k in ("ar", "as", "aw", "la", "lb")])
-        take(3, cp)
-        for k in (1, 2, 3):
-            sums(k)
+        k = exchange(A(pay, 0, 34), land, 0, 34, ["%s%d" % (k, t) for k in ("ar", "as", "aw", "la", "lb")])
         if t == 0:
-            place_rows(9, 16)
-            act(A("place", V, VD), A("seq"), bias=2.0 * V + 64.0)
-        act(A("PL64"), IND(A("place", 0, VD), U), bias=(MAGIC - 64.0) * t)
-        act(A("hm", 256, 512), IND(A("Z"), U2), scale=c(cBU), bias=c(cAU))
-        act(A("PL"), A("PL64"), bias=-MAGIC if t else -64.0)
-        cp(A("N16", 256, 512), IND(A("nbw"), U2))
-        fill("move")
-        ts(A("Y"), A("pm", 0, 256), 187.0, AL.max, 197.0, AL.min)
-        tt(IND(A("w", 0, W + 128), A("Dw")), A("Y"), A("Sp"), AL.add)
-        if t == 1:
-            dma("y", hbm(T.yx[:]), A("w", 0, V), "dyx")
-        act(A("Uw", 0, 16), A("pc", 0, 16))
-        act(A("Ab"), A("PL"), bias=c(cCtr), f=AF.Abs)
-        act(A("Uw", 16, 32), A("pb", 0, 16))
-        act(A("SU"), IND(ww, U))
-        sel(A("pa", 0, 32), "X0", "PL", 0, 512)
-        mm(A("pS"), A("I1"), A("SU"), True, True)
+            iota(A("Z1"), [[0, VD]], 0, 0, True, [k])
+            iota(A("ST1", 512, 1024), [[0, 512]], 0, 0, True, [k])
+        lin(A("Sp"), IND(own, A("Dw", 0, 16)), 1.0, -192.0)
+        mm(A("pK", 0, 256), A("Im"), A("Sp"), True, False)
+        mm(A("pK", 0, 256), A("Ic"), A("oneb"), False, False, True)
         for k in range(4):
-            act(A("SU4", 128 * k, 128 * k + 128), A("SU", 384, 512))
-        fill("wait")
-        if t == 1:
-            ts(A("cm"), A("Ab"), 1152.0, AL.is_lt)
-        cp(A("go"), A(land))
-        for d in range(N - 1):
-            cp(IND(A("w", V + G * d, V + G * d + 2048), A("go", 34 * d + 32, 34 * d + 34)), A(land, 34 * d, 34 * d + 32))
-        if t == 0:
-            ts(A("cm"), A("Ab"), 1152.0, AL.is_lt)
-        cp(A("Gb", 0, 16 * 160), IND(ww, A("N16", 0, 160)))
-        for lo, hi in ((160, 256), (256, 384), (384, 512)):
-            act(A("Gb", 16 * lo, 16 * hi), IND(ww, A("N16", lo, hi)))
-        parts = (("pE0", 0, 256), ("pE1", 256, 384), ("pm", 384, 512))
-        dbank = ("pb", "pc", "pd", "pa")
-
-        def gsum(k, lo, hi):
+            lin(A("Gb", 1024 * k, 1024 * k + 1024), IND(ww, A("Ns", 64 * k, 64 * k + 64)))
             for i in range(16):
-                mm(A(parts[k][0], lo - parts[k][1], hi - parts[k][1]), A("Bm"), A("Gb", 16 * lo + i, 16 * hi, 16), False, False)
-
-        def mo(k, i):
-            b, lo, hi = parts[k]
-            return A("Mb", 16 * lo + (hi - lo) * i, 16 * lo + (hi - lo) * (i + 1))
-
-        def vmax(k, i):
-            b, lo, hi = parts[k]
-            tt(mo(k, i), A("Gb", 16 * lo + i, 16 * hi, 16), A("pS", lo, hi), AL.max)
-
-        def msum(k, i):
-            b, lo, hi = parts[k]
-            mm(A(b, 0, hi - lo), A("B1" if k == 2 else "B2"), mo(k, i), False, i == 15)
-
-        def masks(k):
-            b, lo, hi = parts[k]
-            mm(A(b, 0, hi - lo), A("Dg"), A("hm", lo, hi), k == 2, False)
-            mm(A(b, 0, hi - lo), A("Dg"), A("cm", lo, hi), False, False)
-
-        def flags(k):
-            b, lo, hi = parts[k]
-            ts(A("Lf", lo, hi), A(b, 0, hi - lo), c(cThp), AL.is_ge, c(cB0), AL.not_equal)
-
-        def count(k):
-            b, lo, hi = parts[k]
-            act(A("junk", lo, hi), A("Lf", lo, hi), acc=s(sM0 + k))
-
-        for b, lo, hi in parts[:2]:
-            mm(A(b, 0, hi - lo), A("B16"), A("SU", lo, hi), True, False)
-        for b in dbank[:3]:
-            mm(A(b), A("Im"), A("SU4"), True, False)
-        for k in range(3):
-            masks(k)
-        ts(A("PLw"), A("pa", 0, 32), 8192.0, AL.add)
-        ts(A("oldw"), A("pa", 0, 32), float(V), AL.is_ge)
-        gsum(0, 160, 256)
-        gsum(0, 0, 160)
-        mm(A("pa"), A("Im"), A("SU4"), True, False)
-        for i in range(16):
-            vmax(0, i)
-            msum(0, i)
-            if i == 7:
-                gsum(1, 256, 384)
-        for i in range(16):
-            mm(A(dbank[i // 4], 128 * (i % 4), 128 * (i % 4) + 128), A("I1"), A("Gb", 16 * 384 + i, 8192, 16), False, i % 4 == 3)
-        vmax(1, 0)
-        flags(0)
-        act(s(sT), s(sN1), scale=c(cH1), bias=c(cHc))
-        act(s(sTop), s(sN1), bias=float(V))
-        act(s(sTH), s(sN0), scale=c(cH0), bias=s(sT))
-        for j in range(4):
-            act(A("Mb", 6144 + 512 * j, 6144 + 512 * j + 512), A(dbank[j]), f=AF.Abs)
-        count(0)
-        for i in range(1, 16):
-            vmax(1, i)
-        for j in range(4):
-            for i in range(4 * j, 4 * j + 4):
-                msum(2, i)
-            for i in range(4 * j, 4 * j + 4):
-                msum(1, i)
-        flags(2)
-        count(2)
-        flags(1)
-        count(1)
-        fill("count")
+                mm(A("pK", 64 * k, 64 * k + 64), A("I16"), A("Gb", 1024 * k + i, 1024 * k + 1024, 16), False, k == 3 and i == 15, i > 0)
+        ts(A("Y"), A("pK", 0, 256), 187.0, AL.max, 197.0, AL.min)
+        tt(IND(own, A("Dw", 0, 16)), A("Y"), A("Sp"), AL.add)
+        if t == 1:
+            dma("y", hbm(T.yx[:]), A("w", S0, S0 + V), "dyx")
+        ts(A("Nf"), A("Ns", 0, 256), -1152.0, AL.add)
+        sel(A("pb", 0, 16), "XN", "Nf", 0, 256)
+        ts(U2, A("pb", 0, 16), 1152.0, AL.add)
+        for k in range(2):
+            ts(A("Dw", 16 + 8 * k, 24 + 8 * k), A("pb", 8 * k, 8 * k + 8), w2[1 + k], AL.add, 1152.0 + OFF, AL.add)
+        cp(A("Ns", 256, 512), IND(A("nbw"), U2))
+        lin(A("SU"), IND(own, A("Dw")))
+        act(A("Ab"), IND(A("place", 0, VD), U2), AF.Abs, cCtr)
+        if t == 1:
+            spread(IND(A("place"), o(7)), A("PL"))
+        ts(A("rows"), A("Ab"), cHalf, AL.is_lt)
+        tt(A("SV", 256, 512), IND(A("raw"), U2), A("rows"), AL.add)
+        ts(A("MV", 256, 512), A("Ab"), cHalf, AL.is_lt, cU, AL.mult)
+        cp(IND(A(Z), U2), A("MV", 256, 512))
+        scan(A("R"), A(Z), A(Z), 0.0, AL.add, AL.max)
+        for k, (l, kc) in enumerate((("Bt0", 0), ("Bt1", 0), ("Bt1", 1))):
+            mm(col("pE0", k), A(l), col("R", VD - 1), True, False, k > 0)
+            mm(col("pE0", k), A("Bn0"), col("kb", kc), False, True, True)
+        for k, f in (("XR", cXR), ("XT", cXT)):
+            lin(A(k), A("X"), c(col("pE0", 0), cN9, f))
+        lin(A("tf", 1, 4), A("pE0", 0, 3))
+        lin(A("tb"), A("tf", 1, 3))
+        tt(A("Rg"), IND(A("R"), U), A("SV"), AL.mult)
+        mm(A("pa", 0, 32), A("I1"), A("cT", 0, 32), True, False)
+        sel(A("pa", 0, 32), "XR", "Rg", 0, 512, False, True)
+        ts(o(8), a(lambda k: tt(k, A("pa", 0, 32), A("dS"), AL.min)), -1.0, AL.add)
+        tt(IND(A(ST, 512, 1536), o(8)), A("SV"), A("JR"), AL.add)
+        TS, SS = A(ST, 0, 512), A(ST, 512, 1024)
+        ts(A("oldw"), A("q"), -256.0, AL.add, col("tf", 1), AL.is_ge)
+        y = a(lambda k: lin(k, A("oldw"), c(col("tf", 3), -1.0, dn), c(col("tf", 1), -1.0, n0)))
+        ts(o(0), a(lambda k: tt(k, y, A("qv"), AL.add)), n1, AL.min, V - 1.0, AL.add)
+        lin(TS, IND(A("bag", 0, 4736), o(0)))
         if t == 0:
-            act(c(cW810), c(cW10), scale=-1.0, bias=c(cW8))
-            act(c(cMW10), c(cW10), scale=-1.0)
-            act(c(cBc), c(cNb0), scale=float(V))
-            act(A("dB"), A("q"), bias=4736.0 + 8192.0)
-            act(A("dB8"), A("q"), bias=4736.0 - 8192.0)
-            act(A("dP"), A("q"), bias=float(VD))
-            act(A("dP8"), A("q"), bias=VD - 8192.0)
+            act(A("TSf"), TS, AF.Silu)
         else:
-            whole(0)
-        for j, l in ((0, "BH"), (1, "B12"), (2, "B13")):
-            b = "pc" if j == 0 else "pd"
-            for i, k in enumerate((0, 2, 1)):
-                mm(col(b, j), A(l), s(sM0 + k), i == 0, i == 2)
-        ts(A("cmp"), A("PL"), col("pc", 0), AL.add, s(sTH), AL.is_lt)
-        fill("left")
-        tt(A("S", sL0, sL0 + 2), A("S", sN0, sN0 + 2), A("pd", 1, 3), AL.subtract)
-        act(s(sDL), s(sL1), bias=s(sN1))
-        act(s(sTL), s(sL0), scale=-1.0, bias=s(sTop))
-        act(s(sB1), s(sL1), scale=c(cNb0), bias=c(cBc))
-        act(s(sD2), s(sL0), scale=-1.0, bias=s(sL1))
-        act(s(sB), s(sL0), scale=c(cB0), bias=s(sB1))
-        tt(IND(A("Z"), D), A("cmp", 0, 256), A("Lf", 0, 256), AL.mult)
-        ts(a(1), A("q"), col("pd", 1), AL.is_ge, s(sDL), AL.mult)
-        tt(a(2), a(1), A("q"), AL.add)
-        ts(a(0), a(2), s(sTL), AL.is_ge, 8192.0, AL.mult)
-        tt(a(1), a(2), a(0), AL.add)
-        ts(o(0), a(1), s(sL0), AL.add, 4700.0, AL.min)
-        act(s(sR1), s(sD2), bias=float(V))
-        act(col("hiB", 0), s(sB))
-        act(s(sU), s(sB), scale=c(cW10), bias=c(cMW10))
-        act(a(6), A("oldw"), scale=s(sR1), bias=s(sL0))
-        act(s(sI), col("hiB", 0), scale=c(cW810), bias=s(sU))
+            lin(A("TSf"), TS)
+        sel(A("pb", 0, 64), "X01", ST, 0, 1024)
+        ts(Us, A("pb", 32, 64), -OFF, AL.add, 0.0, AL.max)
+        ts(o(1), A("pb", 0, 32), -OFF, AL.add)
+        lin(A("Usw"), A("pb", 32, 64))
         if t == 0:
-            act(s(sR0), s(sL1), scale=-1.0, bias=s(sN1))
-        act(A("sraw"), IND(A("bag", 0, 4736), o(0)))
-        if t == 0:
-            act(s(sN0), s(sR0), bias=s(sL0))
-            act(A("Uraw", 256, 512), IND(A("raw"), U2))
-            act(s(sN1), s(sN0), scale=-1.0, bias=float(V))
+            lin(A("PL"), IND(A("place", 0, VD), Us))
+            sel(A("pb", 0, 32), "X0", "PL", 0, 512)
+            lin(A("PLw"), A("pb", 0, 32), 1.0 / BL, 1.0 - 64.0 / BL)
         else:
-            whole(1)
-        sel(A("pE0", 0, 32), "Xl", "Lf", 0, 512)
+            ts(A("PL"), IND(A("place", 0, VD), Us), MAGIC - 64.0, AL.add, -MAGIC, AL.add)
+            dma("y", A("PR"), row, "dr0")
+            ts(A("PR"), A("PR"), MAGIC - 64.0, AL.add, -MAGIC, AL.add)
+            dma("y", row, A("PR"), "dr1")
+        tt(A("Rt"), IND(A("R"), o(1)), SS, AL.mult)
+        mm(A("pa", 0, 32), A("I1"), A("cT", 32, 64), True, False)
+        sel(A("pa", 0, 32), "XT", "Rt", 0, 512, False, True)
+        ts(o(9), A("pa", 0, 32), 511.0, AL.add, 0.0, AL.max)
+        lin(A(ST, 1024, 1536), IND(A(ST, 0, 1024), o(9)))
+        sel(A("pa", 0, 64), "Xp", ST, 512, 1536)
+        cp(A("o", 320, 384), A("pa", 0, 64))
+        for ds in (slots_first, slots_last):
+            for d in ds:
+                ts(A("go", 2 * d, 2 * d + 2), (T[land][:, d, 32:34], [(land, 34 * d, 34 * d + 34)], []), float(G * d), AL.add)
+            gv = A("gv", 32 * ds[0], 32 * ds[-1] + 32)
+            lin(gv, (T[land][:, ds[0]:ds[-1] + 1, 0:32], [(land, 34 * ds[0], 34 * ds[-1] + 34)], []))
+            cp(IND(A("w", S0 + V), A("go", 2 * ds[0], 2 * ds[-1] + 2)), gv)
+        mm(A("pS"), A("I1"), A("SU"), True, True)
+        mm(A("pK"), A("B5"), A("PL"), True, False)
+        for lo, hi in zip(CUT, CUT[1:]):
+            lin(A("Gb", 16 * lo, 16 * hi), IND(ww, A("Ns", lo, hi)))
+        for b in range(4):
+            lo, hi, bank, at = 128 * b, 128 * b + 128, ("pE0", "pE1")[b % 2], 256 * (b // 2)
+            E = A(bank, at, at + 64)
+            nb = lambda i: A("Gb", 16 * lo + i, 16 * hi, 16)
+            m = lambda i, n=1: A("Mb", 16 * lo + 128 * i, 16 * lo + 128 * (i + n))
+            mm(E, A("SV", lo, hi), A("MK"), True, False)
+            mm(E, A("SU", lo, hi), A("W4" if ABS[b] else "W8"), False, False, True)
+            for i in range(ABS[b], 16):
+                mm(E, nb(i), A("Wh"), False, False, i % 8 > 0)
+            for j in range(0, 16, 4):
+                if j < ABS[b]:
+                    d = ("pc", "pd")[j // 4]
+                    for i in range(4):
+                        mm(A(d, 128 * i, 128 * i + 128), A("Im"), A("SU", lo, hi), i == 0, False, i > 0)
+                    for i in range(4):
+                        mm(A(d, 128 * i, 128 * i + 128), A("I1"), nb(j + i), False, i == 3, i > 0)
+                    act(m(j, 4), A(d), AF.Abs)
+                else:
+                    for i in range(j, j + 4):
+                        tt(m(i), nb(i), A("pS", lo, hi), AL.max, i > j)
+            for j in list(range(ABS[b], 16, 4)) + list(range(0, ABS[b], 4)):
+                for i in range(j, j + 4):
+                    mm(E, m(i), A("Wp" if j < ABS[b] else "W1"), False, i == (ABS[b] - 1) % 16, i > j)
+            tt((T.FT[:, 8 * b:8 * b + 8, 0:8], [("FT", lo, hi)], []), E, A("TH"), AL.is_ge)
+            mm(A(bank, at + 128, at + 256), (T.FT[:, 8 * b:8 * b + 8, :], [("FT", lo, hi)], []), A("I1"), True, True)
+            lin(A("FU", 128 + lo, 128 + hi), A(bank, at + 128, at + 256))
+        Lf, JC, CN, HC, H = A("FJ", 512, 1024), A("FJ", 0, 512), A("CN"), A("HH", 0, 512), A("HH", 512, 1024)
+        tt(A("NF"), IND(A("FU"), o(11)), A("KR"), AL.mult)
+        lin(Lf, IND(A("FU"), o(10)))
+        mm(A("pK"), A("Ib"), Lf, False, True)
+        scan(JC, A("D01"), Lf, -256.0, AL.mult, AL.add)
+        ml = col("FJ", 511)
+        for k, ls in enumerate((("Bn1",), ("Bp1", "Bn0", "Bn0"), ("Bp1", "Bn0"))[:3 - t]):
+            for j, l in enumerate(ls):
+                mm(col("pa", k), A(l), ml, j == 0, j == len(ls) - 1, j + k > 0)
+        ts(H, A("pK"), c(ml, -1.0, top), AL.subtract, 64.0 * (1 - t) - 256.0 - BIG, AL.is_lt)
+        sA = via(lambda k: ts(k, col("pa", 0), n1, AL.add, V + 255.0 + 64.0 * (1 - t), AL.add))
+        sB = via(lambda k: ts(k, col("pa", 1), dn, AL.subtract, -256.0 - V, AL.add))
+        lin(A("base"), SS, c(sB, cSign), c(sB, c0, sA))
+        scan(CN, A("D01"), A("NF"), -256.0, AL.mult, AL.add)
+        sel(A("pc", 0, 32), "XC", "CN", 0, 512)
+        ts(o(2), A("pc", 0, 32), 511.0, AL.add)
+        spread(IND(A("SL"), o(2)), A("TSf"))
+        scan(HC, A("D01"), H, -256.0, AL.mult, AL.add)
+        for b, ls in (("pE0", (("Bp1", col("tb", 0)), ("Bn0", col("CN", 511)), ("Bn0", col("HH", 511)))),
+                      ("pK", (("Bp1", col("tb", 1)), ("Bn0", col("kb", 0)), ("Bn1", col("CN", 511)), ("Bn1", col("HH", 511))))):
+            for j, (l, h) in enumerate(ls):
+                mm(col(b, 0), A(l), h, j == 0, j == len(ls) - 1, 0 < j < len(ls) - 1)
+        sel(A("pd", 0, 64), "X01", "HH", 0, 1024)
+        y = a(lambda k: ts(k, A("oldw"), col("pK", 0), AL.mult, col("pE0", 0), AL.add))
+        ts(o(3), a(lambda k: tt(k, A("pd", 0, 32), y, AL.add)), 255.0, AL.add, 0.0, AL.max)
+        lin(A("SR"), IND(A("SL", 0, 512), o(3)), c01)
+        sel(A("pS", 0, 32), "X01", "SR", 0, 512)
+        y = a(lambda k: lin(k, A("pd", 32, 64), -BL))
+        y = a(lambda k: tt(k, y, A("dP"), AL.add))
+        ts(o(7), a(lambda k: tt(k, A("pS", 0, 32), y, AL.max)), -OFF, AL.add)
+        sel(A("pb", 32 * t, 64), "XJ", "FJ", 512 * t, 1024)
         if t == 0:
-            sel(A("pE1", 0, 32), "Xl", "Lf", 0, 512, True, False)
-        sel(A("pa", 0, 32), "X", "sraw", 0, 512)
-        tt(IND(A("Z"), U2), A("cmp", 256, 512), A("Lf", 256, 512), AL.mult)
-        tt(a(7), A("PLw"), A("pE0", 0, 32), AL.add)
-        tt(a(3), A("Uw"), A("pE0", 0, 32), AL.add)
-        tt(a(8), a(7), a(6), AL.is_ge)
-        tt(a(0), a(3), A("dP8"), AL.min)
-        fill("tail")
-        cp(o(1), A("pa", 0, 32))
-        act(A("Zg"), IND(A("Z"), o(1)), scale=-1.0)
-        act(a(9), a(8), scale=8192.0)
-        sel(A("pb", 0, 32), "Xj4", "Zg", 0, 512, True, False)
-        scan(A("R"), A("Z"), s(sI), AL.add)
-        if t == 0:
-            iota(A("Z"), [[0, VD]], 0, 0, True)
-        scan(A("CL"), A("Zg"), 0.0, AL.min)
-        sel(A("pb", 0, 32), "Xj", "CL", 0, 512, False, True)
-        mm(col("pc", 2), A("Bh0"), col("R", VD - 1), True, True)
-        tt(A("Rg"), IND(A("R"), U), A("cm"), AL.mult)
-        if t == 0:
-            draw_places(1)
-        else:
-            for k in range(2, 6):
-                whole(k)
-        ts(a(2), A("pb", 0, 32), 512.0, AL.min)
-        ts(a(4), A("oldw"), col("pc", 2), AL.mult, -1.0, AL.add)
-        tt(a(1), a(2), A("q"), AL.add)
-        sel(A("pa", 0, 32), "Xh", "Rg", 0, 512)
-        if t == 0:
-            sel(A("pE1", 0, 32), "Xn", "Rg", 0, 512, False, True)
-        mm(A("pS"), A("Bj"), A("Rg"), True, True)
-        act(A("J"), A("pS"), bias=64.0 * (1 - t))
-        ts(o(6), a(0), 8192.0, AL.add)
-        cp(o(2), a(1))
-        tt(a(5), a(4), A("pa", 0, 32), AL.add)
-        if t == 0:
-            tt(a(2), a(9), A("PLw"), AL.add)
-        cp(o(3), a(5))
-        cp(IND(A("SL"), o(2)), A("sraw"))
-        act(A("SR"), IND(A("SL", 0, 512), o(3)))
-        sel(A("pb", 0, 32), "X", "SR", 0, 512)
-
-        def place_stayers():
-            tt(a(4), a(9), A("pb", 0, 32), AL.add)
-            tt(a(5), a(4), A("dP"), AL.min)
-            cp(o(7), a(5))
-
-        if t == 0:
-            spread(IND(A("place"), o(6)), A("J"))
-            tt(a(0), A("pE1", 0, 32), A("dB8"), AL.min)
-            tt(a(1), a(2), A("dB"), AL.min)
-            ts(o(4), a(0), 8192.0, AL.add)
-            ts(o(5), a(1), -8192.0, AL.add)
-            cp(IND(A("bag"), o(4)), A("Uraw"))
-            tt(a(4), a(9), A("pb", 0, 32), AL.add)
-            ts(A("P16", 0, 8), A("dr", 80, 88), s(sBa0), AL.add)
-            tt(a(5), a(4), A("dP"), AL.min)
-            ts(A("P16", 8, 16), A("dr", 88, 96), s(sBa1), AL.add)
-            cp(o(7), a(5))
-            spread(IND(A("place"), o(7)), A("PL64"))
+            was = n0
+            n2, n0, n1 = two(lambda k: None)
+            n13 = via(lambda k: ts(k, col("pa", 2), was, AL.add, 13.0, AL.mult))
+            lin(n0, col("pa", 2), 1.0, was)
+            y = a(lambda k: lin(k, A("oldw"), sB, sA))
+            y = a(lambda k: tt(k, A("pb", 0, 32), y, AL.add))
+            ts(o(4), a(lambda k: tt(k, y, A("dB8"), AL.min)), BL - 64.0, AL.add)
+            tt(IND(A("bag"), o(4)), SS, A("D01"), AL.mult)
+            y = a(lambda k: tt(k, A("PLw"), A("pd", 32, 64), AL.subtract))
+            ts(o(5), a(lambda k: tt(k, y, A("dB"), AL.min)), BL, AL.mult)
             cp(IND(A("bag"), o(5)), A("SR"))
+        y = a(lambda k: tt(k, A("pb", 32, 64), A("dP"), AL.add))
+        ts(o(6), a(lambda k: tt(k, y, A("Usw"), AL.max)), -OFF, AL.add)
+        mm(A("pE1"), A("B01"), JC, True, True)
+        if t == 0:
+            tt(A("J"), A("pE1"), A("base"), AL.add)
+            spread(IND(A("place"), o(6)), A("J"))
         else:
-            cp(IND(A("place"), o(6)), A("J"))
-            place_stayers()
+            lin(A("J"), A("pE1"))
+            tt(IND(A("place"), o(6)), A("J"), A("base"), AL.add)
             cp(IND(A("place"), o(7)), A("PL"))
-            dma("y", hbm(T.yp[:]), A("place", 0, V, p=slice(0, 128, 16)), "dyp")
+            dma("y", hbm(T.yp[:]), row, "dyp")
+
+    def meet(e, n, lo, hi):
+        return n in PSUM or (e[0] < hi and lo < e[1])
+
+    wr, rd = {}, {}
+    for i, op in enumerate(ops):
+        js = set()
+        for (n, lo, hi) in op["R"]:
+            js.update(e[2] for e in wr.get(n, []) if meet(e, n, lo, hi))
+            if n in PSUM:
+                js.update(e[2] for e in rd.get(n, []) if op["q"] == "?" or ops[e[2]]["q"] != op["q"])
+        for (n, lo, hi) in op["W"]:
+            js.update(e[2] for e in wr.get(n, []) + rd.get(n, []) if meet(e, n, lo, hi))
+        op["pre"] = js
+        for (n, lo, hi) in op["W"]:
+            for d in (wr, rd):
+                d[n] = [e for e in d.get(n, []) if not (n in PSUM or (lo <= e[0] and e[1] <= hi))]
+            wr[n].append((lo, hi, i))
+        for (n, lo, hi) in op["R"]:
+            rd.setdefault(n, []).append((lo, hi, i))
+
+    known = {k: {} for k in eng}
+    total = {}
+
+    def need(q, toks):
+        best = {}
+        for t in toks:
+            if t[0] not in best or best[t[0]][1] < t[1]:
+                best[t[0]] = t
+        for t in sorted(best.values(), key=lambda t: -len(t[2])):
+            if known[q].get(t[0], 0) < t[1]:
+                eng[q].wait_ge(T.sem[t[0]], t[1])
+                known[q][t[0]] = t[1]
+                for k, n in t[2].items():
+                    if known[q].get(k, 0) < n:
+                        known[q][k] = n
+
+    order = [(int(k.rstrip("s")), "s" if k.endswith("s") else "v") for k in ORDER.split()]
+    assert sorted(i for i, _q in order) == list(range(len(ops)))
+    for i, pick in order:
+        op = ops[i]
+        q = pick if op["q"] == "?" else op["q"]
+        assert all("tok" in ops[j] for j in list(op["pre"]) + list(op["after"]))
+        sem = op["sem"] or "c" + q
+        total[sem] = total.get(sem, 0) + abs(op["inc"]) * len(op["fn"])
+        if q is not None:
+            need(q, [ops[j]["tok"] for j in sorted(op["pre"]) if not (q == "p" and ops[j]["q"] == "p")])
+            for fn in op["fn"]:
+                call = fn(q) if op["q"] == "?" else fn()
+                if op["inc"] > 0:
+                    call.then_inc(T.sem[sem], op["inc"])
+        op["tok"] = (sem, total[sem], dict(known[q]) if q else {})
     need("g", [(k, n, {}) for k, n in total.items()])

from concourse.bass import DstId, RemoteDMATransfer
from concourse.mybir import AluOpType as AL, ActivationFunctionType as AF, AxisListType as AX

V, G, W = 2304, 256, 4096
VD = V + 128
S0 = 128
BIG = 262144.0
BL = 8192.0
MAGIC = 12582912.0
OFF = 192.0
bf, f32, i32, u16, f16 = "bfloat16", "float32", "int32", "uint16", "float16"
_SB = {
    bf: dict(w=6016, bag=5248, raw=VD, Z0=VD, Z1=VD, R=VD, ST0=1536, ST1=1536, Gb=8192, Mb=8192, Sel=2048, pfl=144, plh=144, pll=144, seq=128,
             oneb=256, zer=256, B1=128, W1=64, Wh=64, Wp=64, W8=64, W4=64, KR=512, BE=128, MK=64, Bn0=128, Bn1=128, Bp1=128, B01=128, Bt0=128,
             Bt1=128, I1=128, I16=128, Im=128, Ic=128, Ib=128, X=144, X01=144, XR=144, XT=144, XJ=144, XC=144, junk=512, PAT=256, SVD=256, SV=512,
             MV=512, rows=256, Rg=512, Rt=512, Sp=256, Y=256, GE=512, SE=32, YE=32, CS=256, CT=512, pay0=40, pay1=40, gv=224, SU=512,
             D01=512, FJ=1024, FU=640, JR=512, Xp=144, NF=512, CN=512, HH=1024, SR=512, cT=64, kb=4, tb=2),
    f16: dict(Nf=256, XN=144),
    f32: dict(place=VD + 528, TH=64, Dth=64, plcf=144, tsf=4, ts=4, onef=128, Bt=128, Bf=128, If=128, G8=128, B5=128, X0=144, OH=16, jf=256, C=128,
              q16=32, q=32, qv=32, j32=8, dB=32, dB8=32, dP=32, dS=32, K2=2, tf=4, t2=8, PL=512, Ab=256, J=512, base=512, TSf=512, SL=8704,
              PR=144, oldw=32, Usw=32, PLw=32, a=1280),
    i32: dict(nbw=VD, plci=144, tsi=4, ohi=16, ohj=16, bi=4, pi=32),
    u16: dict(plc16=144, P16=16, Uo=32, Us=32, Dw=32, Ns=512, ix=2, NE=32, go=16, o=384),
}
POOL = {}
for _k, _n in list(_SB[bf].items()):
    if _n in (128, 144):
        POOL[_k] = (_SB[bf].get("pool", 0), _n)
        _SB[bf]["pool"] = POOL[_k][0] + _SB[bf].pop(_k)
PSUM = ("pS", "pE0", "pE1", "pK", "pa", "pb", "pc", "pd")
SCRATCH = {k: ("sbuf", [128, n], d) for d, b in _SB.items() for k, n in b.items()}
SCRATCH["FT"] = ("sbuf", [128, 32, 16], bf)
SCRATCH["land0"] = SCRATCH["land1"] = ("sbuf", [128, 7, 34], bf)
SCRATCH.update({k: ("psum", [128, 512], f32) for k in PSUM})
SEMAPHORES = ["cv", "cs", "cp", "cg", "dx0", "dx1", "dnb", "dpl", "dth", "dsd", "dyx", "dyp", "dr0", "dr1", "ga", "gs", "gw", "l0", "l1",
              "la0", "la1", "lb0", "lb1", "ar0", "ar1", "as0", "as1", "aw0", "aw1"]
CUT = (0, 64, 128, 192, 256, 320, 384, 448, 512)
ABS = (0, 0, 8, 8)
ORDER = """
0 7 9 6 10 11 8 16 35 34 18 17 32 110 46 19 23 121 158 204 139 186 33 1 117s 119s 113s 201 29s 124s 20s 112 47s 25s 21s 31 13 22 145 86 111s 2 49 115 140 62s 60s 88s 72s 171s 24s 3 52 50 4 114 147 48 12 206 53 55 137 5 54 156 56 58s 57 90s 26s 27s 126s 41 15 207s 59 208 30 42 28s 144s 64s 209 211 84 122s 203s 197s 74s 157s 210 212 142 40s 68 215 213 61 63 85 87 89 130s 148s 76s 123s 80s 172s 192s 78s 109s 118s 65 216s 70s 173s 92s 166s 160s 174s 220s 104s 38s 195s 150s 43 125s 120s 66s 105s 182s 51 82s 175s 14 79 81 67 69 71 83 196s 141s 218s 199s 116s 180s 149s 154s 134s 217 214 108 223s 178s 93s 163s 151s 73 219 221 135 152 187 225 91 75 77 131s 202s 146 95 190 128 155 193 205 133s 226 191 188 168 170 228 101s 129 183 106s 176s 143s 102s 127s 132s 98s 227s 162s 169s 153s 167s 222 232 231 107s 138s 233 234 164s 269 94s 99s 103s 44 45 229 235 270 237 230 236 238 181 165s 100s 96s 198 271 239 159s 39s 224s 161s 36s 97s 177 242 257s 189 240 37 276 241 243 184 258 185 273 279 277 280 245s 246 247 248 272 244 179 249 281 282 290 250 278 200 283 259s 261s 285s 260 289 284 287 274 296 295 297 252 251 291 263s 262 264 298 292 311 320 299 293 318 300 294 317 319 265s 266 267 253 301s 254 321s 194s 303 322 286s 136s 255 304 307s 326s 268 305 324 323 325 306 327 310 331 332 275s 330s 335s 333s 334s 308 256 371 328 368 352 338 342 341 343 312 329 339 340 345 346 347 344 348 358 356 349 355 357 369 372 353 354 359 360 350 375 351 313 361 362 363 374 337s 370 373 336s 388 385 314 364 366 367 376 377 386 365s 387 389 378 383 384 390 391 392 393 379 394 395 380 396 397 315 398 381 316 399 382s 309s 288s 400 401s 302 403 402 412 404 413 431 405 406 419 417 407 408 416 432 434 433s 450 435 420 418 414 421 446 409s 449s 422 443 451 436 444 410s 423 452 453 437 427 415 465s 455 457 439 454 462s 460s 424 459 440 438 441 425s 456s 461 463 428 442 458s 411s 426 464s 445 467 447 429 469s 468 448 470 430 472 471 474 473 475 476 510 477 479 478 480 532 511 481 512 484 482 483 499s 485 505 487s 517 497s 501s 503s 488 489 521 490 486 514 513 491 522 519 498 500 523 502 524 504 525s 492 494 493 506 527s 526s 495 496 529s 564s 538s 518 520 515 531 561 533 537 539 507 563 562 560 508 540 550 516s 569s 565 541 534 542 509 567 566 568 535 543s 528 570 554 577s 573s 578s 571 576s 581 614 611 595 536 574 545 547 575 587 584 585 586 553 582 615 612 613 616 579s 583 588 589 590 591 596 555 600 592 593 594s 598 556 599 601 617 628 597 609 602 631 610 603 604 605 580s 618 606 546 619 629 620 607 632 621 622 557s 630 634 608 635 633 626 627 636 623 466s 549 530s 637 548s 624 638 639 558 640 559 641 642 625s 572 551 643 644s 655 646 552 645 648 544s 656 678 647 649 657 679s 674 662 651 660 650 659 675 663 661 652 653 664 658 676 665 654 666 677 667 670s 668s 669 680 671 672 673 681 682
"""


def rank_program(g, core, T, topo):
    rank = T.rank_of(core)
    if rank is None:
        return
    N = len(T.cores)
    eng = {"v": g.vector, "s": g.scalar, "p": g.tensor, "g": g, "y": g.sync}
    ops = []

    def A(name, lo=0, hi=None, step=1, p=None):
        if name in POOL:
            at, n = POOL[name]
            name, lo, hi = "pool", at + lo, at + (n if hi is None else hi)
        t = T[name]
        if name.startswith("land"):
            return (t[:, lo // 34:hi // 34, :], [(name, lo, hi)], [])
        if hi is None:
            hi = t.shape[1]
        ps = slice(None) if p is None else p
        return (t[ps, lo:hi:step] if step > 1 else t[ps, lo:hi], [(name, lo, hi)], [])

    def col(name, c):
        return A(name, c, c + 1)

    def IND(win, off):
        return (win[0].indirect(off[0]), win[1], off[1])

    def run(q, fn, outs, ins, sem=None, inc=1, after=(), join=False):
        R, Wr = [], []
        for o in outs:
            Wr += o[1]
            R += o[2]
        for i in ins:
            if isinstance(i, tuple):
                R += i[1] + i[2]
        if join:
            op = ops[-1]
            op.update(fn=op["fn"] + [fn], R=op["R"] + R, W=op["W"] + Wr)
            return None
        ops.append(dict(q=q, fn=[fn], R=R, W=Wr, sem=sem, inc=inc, after=after))
        return len(ops) - 1

    def x(a):
        return a[0] if isinstance(a, tuple) else a

    def cp(o, i):
        run("v", lambda: g.vector.tensor_copy(o[0], i[0]), [o], [i])

    def tt(o, a, b, op, join=False):
        run("v", lambda: g.vector.tensor_tensor(o[0], a[0], b[0], op), [o], [a, b], join=join)

    def ts(o, a, s1, op0, s2=None, op1=None):
        if op1 is None:
            run("v", lambda: g.vector.tensor_scalar(o[0], a[0], x(s1), None, op0), [o], [a, s1])
        else:
            run("v", lambda: g.vector.tensor_scalar(o[0], a[0], x(s1), x(s2), op0, op1), [o], [a, s1, s2])

    def ms(o, c):
        run("v", lambda: g.vector.memset(o[0], c), [o], [])

    def scan(o, a, b, init, op0, op1):
        run("v", lambda: g.vector.tensor_tensor_scan(o[0], a[0], b[0], x(init), op0, op1), [o], [a, b, init])

    def act(o, i, f, bias=0.0):
        run("s", lambda: g.scalar.activation(o[0], i[0], f, bias=x(bias)), [o], [i, bias])

    def lin(o, i, scale=1.0, bias=0.0):
        def fn(q):
            if q == "s":
                return g.scalar.activation(o[0], i[0], AF.Identity, bias=x(bias), scale=x(scale))
            if scale == 1.0 and bias == 0.0:
                return g.vector.tensor_copy(o[0], i[0])
            return g.vector.tensor_scalar(o[0], i[0], x(scale), x(bias), AL.mult, AL.add)
        run("?", fn, [o], [i, scale, bias])

    def total_of(o, i, junk):
        run("?", lambda q: g.scalar.activation(junk[0], i[0], AF.Identity, accum_out=o[0]) if q == "s" else
            g.vector.tensor_reduce(o[0], i[0], AX.X, AL.add), [o, junk], [i])

    def spread(o, i):
        run("s", lambda: g.scalar.activation(o[0], i[0], AF.Silu), [o], [i])

    def mm(o, l, r, start, stop, join=False):
        run("p", lambda: g.tensor.matmul(o[0], l[0], r[0], start, stop), [o], [l, r], join=join)

    def sel(o, xn, name, lo, hi, start=True, stop=True):
        for r in range(16):
            mm(o, A(xn, 15 - r, 143 - r), A(name, lo + r, hi, 16), start and r == 0, stop and r == 15, r > 0)

    def iota(o, pat, base, cmul, small=False, after=()):
        if small:
            run("g", lambda: g.iota(o[0], pat, base, cmul, allow_small_or_imprecise_dtypes=True), [o], [], after=after)
        else:
            run("g", lambda: g.iota(o[0], pat, base, cmul), [o], [])

    def asel(o, i, pat, op, base, cmul):
        run("g", lambda: g.affine_select(o[0], i[0], pat, op, 0.0, base, cmul), [o], [i])

    def dma(q, o, i, sem, after=()):
        return run(q, lambda: eng[q].dma_start(o[0], i[0]), [o], [i], sem, 16, after)

    def hbm(ap):
        return (ap, [], [])

    def dst(c):
        rid, pid, _se = topo.addr(c)
        return DstId(rid=rid, pnc=pid)

    def bits(es):
        return sum(1 << e for e in es)

    def send(trs, src, lsem):
        return run("g", lambda: g.remote_dma_fused([RemoteDMATransfer(
            dst_ids=[dst(c) for c, _a in ds], dma_engine_mask=bits(es), remote_sem=T.sem[rs], srcs=[s], dsts=[a for _c, a in ds])
            for s, ds, es, rs in trs], local_sem=T.sem[lsem]), [], [src], lsem, -sum(len(t[2]) for t in trs))

    def landed(sem, n, region, at):
        run(None, None, [(None, [region], [])], [], sem, n, [at])

    cores = list(T.cores)
    others = [(rank + d) % N for d in range(1, N)]
    near = [r for r in others if topo.chip(cores[r]) == topo.chip(core)]
    far = [r for r in others if topo.chip(cores[r]) != topo.chip(core)]
    sib = near[0]
    e_far = topo.engines(core, cores[far[0]])
    e_all = topo.engines(core, cores[sib])
    e_near = [e for e in e_all if e not in e_far]

    def takes(r):
        both = [k for k in range(N) if topo.chip(cores[k]) == topo.chip(cores[r])]
        out = sorted((k for k in range(N) if k not in both), key=lambda k: (both[0] - k) % N)
        return out[len(out) // 2:] if r == both[0] else out[:len(out) // 2]

    takers = [r for r in far if rank in takes(r)]
    mine = takes(rank)
    slots_first = sorted((rank - k) % N - 1 for k in mine + [sib])
    slots_last = sorted((rank - k) % N - 1 for k in takes(sib))

    def exchange(src, buf, base, n, sems):
        def span(recv, ss):
            return base + n * ((recv - ss[0]) % N - 1), base + n * ((recv - ss[-1]) % N)
        s_far, s_near, s_on, l0, l1 = sems
        at = send([(src[0], [(cores[r], A(buf, *span(r, [rank]))[0]) for r in takers], e_far, s_far),
                   (src[0], [(cores[sib], A(buf, *span(sib, [rank]))[0])], e_near, s_near)], src, l0)
        landed(s_far, len(e_far) * len(mine), (buf,) + span(rank, mine), at)
        landed(s_near, len(e_near), (buf,) + span(rank, [sib]), at)
        fw = A(buf, *span(rank, mine))
        at = send([(fw[0], [(cores[sib], A(buf, *span(sib, mine))[0])], e_all, s_on)], fw, l1)
        landed(s_on, len(e_all), (buf,) + span(rank, takes(sib)), at)
        return at

    k = dma("y", A("w", S0, S0 + G), hbm(T.x[:, 0:G]), "dx0")
    dma("s", A("plci"), hbm(T.plc[:]), "dpl")
    k = dma("y", A("tsi", 0, 1, p=slice(0, 8)), hbm(T.th[:]), "dth", [k])
    k = dma("y", A("tsi", 1, 3, p=slice(0, 8)), hbm(T.sd[:]), "dsd", [k])
    k = dma("y", A("nbw", 0, V), hbm(T.nb[:]), "dnb", [k])
    dma("y", A("w", S0 + G, S0 + V), hbm(T.x[:, G:V]), "dx1", [k])

    oh = lambda k: col("OH", k)
    used = {"C": 0, "a": 0, "jf": 0}

    def new(name, n):
        used[name] += n
        return A(name, used[name] - n, used[name])

    def via(f, name="C", n=1):
        t = new(name, n)
        f(t)
        return t

    c = lambda i, scale=1.0, bias=0.0: via(lambda t: lin(t, i, scale, bias))
    ones = lambda lo, hi, step=1: via(lambda t: total_of(t, A("OH", lo, hi, step), new("jf", len(range(lo, hi, step)))))
    ms(A("onef"), 1.0)
    iota(A("ohi"), [[-1, 16]], 128, 1)
    iota(A("seq"), [[1, 128]], 0, 0, True)
    iota(A("q16"), [[16, 32]], 0, 0, True)
    asel(A("Bt"), A("onef"), [[-16, 8], [0, 16]], AL.is_ge, 0, 1)
    asel(A("Bf"), A("Bt"), [[16, 8], [0, 16]], AL.is_ge, 15, -1)
    asel(A("G8"), A("onef"), [[1, 8], [0, 16]], AL.is_equal, 0, -1)
    asel(A("If"), A("onef"), [[-1, 128]], AL.is_equal, 0, 1)
    iota(A("nbw", V, VD), [[1, 128]], V, 0)
    iota(A("Z0", 1216, VD), [[0, VD - 1216]], 0, 0, True)
    ts(A("ohj"), A("ohi"), 15, AL.bitwise_and)
    ts(A("OH"), A("ohj"), 0.0, AL.is_equal)
    cR = via(lambda t: cp(t, col("ohj", 0)))
    rb = c(oh(0), 128.0)
    lin(A("raw", 0, 128), A("seq"), oh(1), c(oh(1), 64.0, rb))
    for k in range(5):
        n = 128 * 2 ** k
        lin(A("raw", n, min(2 * n, VD)), A("raw", 0, min(n, VD - n)), 1.0, c(oh(0), float(n)) if k else rb)
    for lo in range(0, 1216, 304):
        ms(A("Z0", lo, lo + 304), 0.0)
    ms(A("zer"), 0.0)
    for lo in (0, 256):
        lin(A("ST0", 512 + lo, 768 + lo), A("zer"))
        lin(A("SL", lo, lo + 256), A("zer"))
    lin(A("w", 0, S0), A("zer", 0, S0))
    exchange(A("w", S0, S0 + G), "w", S0 + V, G, ("ga", "gs", "gw", "l0", "l1"))
    lin(A("q"), A("q16"), 1.0, cR)
    lin(A("B1"), A("Bf"))
    cp(A("plc16"), A("plci"))
    cp(A("plcf"), A("plci"))
    cp(A("tsf", 0, 3, p=slice(0, 8)), A("tsi", 0, 3, p=slice(0, 8)))
    cp(IND(A("bag", 0, 2 * V), A("plc16")), A("raw", 0, V))
    ts(A("pfl"), A("plcf"), float(V), AL.is_lt)
    mm(A("pc", 0, 144), A("B1"), A("pfl"), True, True)
    mm(A("pd", 0, 3), A("G8", p=slice(0, 8)), A("tsf", 0, 3, p=slice(0, 8)), True, True)
    n2 = new("C", 2)
    n0, n1 = A("C", used["C"] - 2, used["C"] - 1), A("C", used["C"] - 1, used["C"])
    total_of(n0, A("pc", 0, 144), new("jf", 144))
    lin(A("ts", 0, 3), A("pd", 0, 3))
    n13 = c(n0, 13.0)
    lin(A("plh"), A("plcf"))
    tt(A("pll"), A("plcf"), A("plh"), AL.subtract)
    banks = ("pK", "pS", "pE0", "pE1", "pb", "pa")
    for r in range(16):
        lin(A("Sel", 128 * r, 128 * r + 128), A("B1"), oh(r))
        for k, h in enumerate(("plh", "pll")):
            mm(A(banks[r // 3], 144 * (r % 3), 144 * (r % 3) + 144), A("Sel", 128 * r, 128 * r + 128), A(h), k == 0, k == 1, k == 1)
    for r in range(16):
        lin((T.place[:, r:V:16], [("place", r, r + 1) if r < 15 else ("place", 15, V)], []),
            A(banks[r // 3], 144 * (r % 3), 144 * (r % 3) + 144), 1.0, 64.0)
    lin(A("place", V, VD), A("seq"), 1.0, 2.0 * V + 64.0)
    lin(A("bag", 2 * V, 4736), A("raw", V, VD))
    lin(A("X"), A("zer", 0, 144))
    lin(A("X", 15, 143, 16), A("Bf", 0, 128, 16))
    lin(A("j32"), A("q", 0, 8), 32.0)

    c01, cT0, cT1, c8A, c45, c67, c23, cB0 = (ones(*k) for k in ((0, 2), (4, 7, 2), (5, 8, 2), (8, 12), (4, 6), (6, 8), (2, 4), (1, 16, 2)))
    ms(A("oneb"), 1.0)
    lin(A("X01"), A("X"), c01)
    c0, c1 = c(cT0, 1.0, oh(10)), ones(5, 12, 2)
    lin(A("PAT", 0, 128), A("oneb", 0, 128), c0, oh(8))
    lin(A("PAT", 128, 256), A("oneb", 0, 128), c1, oh(8))
    cD, cU = c(c8A, -1.0, c45), c(c8A, -1.0, c67)
    ts(A("BE"), A("B1"), oh(8), AL.mult, -1.0, AL.mult)
    lin(A("K2"), A("q", 0, 2), 8.0, 1792.0)
    cS1, cS2 = c(cB0, -2.0, 1.0), c(cB0, 2.0 * V)
    cCtr, cHalf, cSign = c(c1, -float(V), -(64.0 + 1151.5)), c(c(c0, 1.0, c1), 1152.0), c(c0, -2.0, 1.0)
    ts(A("XN"), A("X"), oh(0), AL.mult)
    lin(A("X0"), A("X"), oh(0))
    lin(A("B5"), A("Bf"), oh(5))
    lin(A("I1"), A("If"))
    for k, f in (("I16", 1.0 / 16), ("Im", -1.0), ("Ic", -15.0 / 32), ("Ib", -BIG)):
        lin(A(k), A("I1"), f)
    c47, cN9 = ones(4, 8), c(oh(9), -1.0)
    cXT, cXR = c(oh(10), -BL, c(oh(11), -BL - 256.0, c47)), c(ones(8, 11, 2), BL, c(oh(11), BL - 256.0, c47))
    lin(A("Xp"), A("X"), ones(12, 14))
    for k in range(4):
        lin(A("JR", 128 * k, 128 * k + 128), A("seq"), oh(13), c(oh(12), 128.0 * k + 128.0))
    for k, f in (("XJ", c(c45, -BL, c01)), ("XC", c(c45, 4.0, c23))):
        lin(A(k), A("X"), f)
    for k, f in (("Bt0", cT0), ("Bt1", cT1), ("Bp1", oh(1)), ("B01", c01)):
        lin(A(k), A("B1"), f)
    lin(A("Bn0"), A("Sel", 0, 128), -1.0)
    lin(A("Bn1"), A("Sel", 128, 256), -1.0)
    for r in range(4):
        lin(A("W1", r, 64, 4), A("B1", 0, 128, 8), 1.0 if r in (0, 3) else -1.0)
    for r in range(2):
        lin(A("MK", r, 64, 2), A("Sel", 128 * (4 + r), 128 * (5 + r), 4), BIG / 2)
    lin(A("Wh"), A("W1"), -0.5)
    lin(A("W8"), A("W1"), -8.0)
    lin(A("W4"), A("W1"), -4.0)
    lin(A("Wp"), A("W1"), 0.5)
    lin(A("Dth"), A("W1"), c(col("ts", 0), 1.0 / 32, -1.0 / 64))
    mm(A("pS", 0, 64), A("onef"), A("Dth"), True, True)
    lin(A("TH"), A("pS", 0, 64), 1.0, BIG / 2)
    ms((T.FT[:], [("FT", 0, 512)], []), 0.0)
    ms(A("cT", 0, 16), 2 * BL)
    ms(A("cT", 16, 32), BL)
    ms(A("cT", 32, 64), -BL)
    for k, f in enumerate((256.0, float(V))):
        ms(col("kb", k), f)
    c03 = c(c01, 1.0, c23)
    for lo in (0, 256):
        lin(A("D01", lo, lo + 256), A("oneb"), c03)
    lin(A("KR", 0, 128), A("seq"), c45, c(c45, 128.0, c03))
    for n in (128, 256):
        lin(A("KR", n, 2 * n), A("KR", 0, n), c(c45, n / 64.0 - 1.0, 1.0))
    lin(A("FU", 0, 16), A("oneb", 0, 16), oh(2), oh(6))
    for k, f, b in (("dS", 1.0, 513.0), ("dB", 1.0 / BL, 4736.0 / BL), ("dB8", 1.0, 4800.0 - BL), ("dP", 1.0, VD + 1 + OFF),
                    ("qv", 1.0, -255.0 - V)):
        lin(A(k), A("q"), f, b)

    o = lambda k: A("o", 32 * k, 32 * k + 32)
    a = lambda f: via(f, "a", 32)
    two = lambda f: (via(f, "C", 2), A("C", used["C"] - 2, used["C"] - 1), A("C", used["C"] - 1, used["C"]))
    ww, own = A("w", S0, S0 + W), A("w", 0, S0 + V)
    D, U, U2, Us = A("Uo", 0, 16), A("Uo"), A("Uo", 16, 32), A("Us")
    row = A("place", 0, V, p=slice(5, 128, 16))
    for t in range(2):
        pay, land, Z, ST = "pay%d" % t, "land%d" % t, "Z%d" % t, "ST%d" % t
        lin(n1, n0, -1.0, float(V))
        ts(A("bi", 0, 2), A("ts", 1, 3), n13, AL.add, 41.0 * t, AL.add)
        ts(A("bi", 2, 4), A("bi", 0, 2), 31, AL.bitwise_and)
        b2 = two(lambda k: cp(k, A("bi", 2, 4)))
        e2 = two(lambda k: ts(k, n2, 128.0, AL.max))
        v2 = two(lambda k: ts(k, n2, 128.0, AL.is_ge))
        for k in range(2):
            ts(A("pi", 8 * k, 8 * k + 8), A("j32"), b2[1 + k], AL.add, e2[1 + k], AL.mult)
            lin(A("SVD", 128 * k, 128 * k + 128), A("PAT", 128 * k, 128 * k + 128), v2[1 + k])
        ts(A("pi", 16, 32), A("pi", 0, 16), 12, AL.arith_shift_right)
        for k in range(2):
            ts(A("P16", 8 * k, 8 * k + 8), A("pi", 16 + 8 * k, 24 + 8 * k), c(v2[1 + k], (k - 2.0) * V, 2.0 * V), AL.add)
        w2 = two(lambda k: lin(k, v2[0], float(V + S0), -V - OFF))
        dn, top = c(n0, -2.0, float(V)), c(n0, cS1, cS2)
        tt(A("SV", 0, 256), IND(A("bag", 0, 4736), A("P16")), A("SVD"), AL.add)
        sel(A("pc", 0, 16), "X01", "SV", 0, 256)
        lin(A("MV", 0, 256), A("SV", 0, 256), cD)
        ts(D, A("pc", 0, 16), -OFF, AL.add)
        for k in range(2):
            ts(A("Dw", 8 * k, 8 * k + 8), A("pc", 8 * k, 8 * k + 8), w2[1 + k], AL.add)
        cp(A("Ns", 0, 256), IND(A("nbw"), D))
        cp(IND(A(Z), D), A("MV", 0, 256))
        mm(A("pa", 0, 256), A("BE"), A(Z, 0, 256), True, True)
        scan(A("CS"), A("pa", 0, 256), A("zer"), 0.0, AL.add, AL.add)
        for k in range(2):
            h = A("junk", 256 * k, 256 * k + 256)
            ts(h, A("CS"), col("q", k), AL.is_le)
            scan(A("CT", 256 * k, 256 * k + 256), h, h, 0.0, AL.add, AL.max)
        cnt = A("CT", 255, 512, 256)
        cp(A("ix"), cnt)
        cp(A("NE"), IND(A("nbw"), A("ix")))
        lin(A("SE"), IND(A("w", S0, S0 + 272), A("ix")), 1.0, -192.0)
        ts(A("t2", 4, 6), cnt, 256.0, AL.is_ge, 4096.0, AL.mult)
        tt(A("t2", 6, 8), cnt, A("t2", 4, 6), AL.add)
        tt(A(pay, 32, 34), A("t2", 6, 8), A("K2"), AL.min)
        lin(A("GE"), IND(ww, A("NE")))
        mm(A("pd", 0, 32), A("Im"), A("SE"), True, False)
        mm(A("pd", 0, 32), A("Ic"), A("oneb", 0, 32), False, False, True)
        for i in range(16):
            mm(A("pd", 0, 32), A("I16"), A("GE", i, 512, 16), False, i == 15, i > 0)
        ts(A("YE"), A("pd", 0, 32), 187.0, AL.max, 197.0, AL.min)
        tt(A(pay, 0, 32), A("YE"), A("SE"), AL.add)
        k = exchange(A(pay, 0, 34), land, 0, 34, ["%s%d" % (k, t) for k in ("ar", "as", "aw", "la", "lb")])
        if t == 0:
            iota(A("Z1"), [[0, VD]], 0, 0, True, [k])
            iota(A("ST1", 512, 1024), [[0, 512]], 0, 0, True, [k])
        lin(A("Sp"), IND(own, A("Dw", 0, 16)), 1.0, -192.0)
        mm(A("pK", 0, 256), A("Im"), A("Sp"), True, False)
        mm(A("pK", 0, 256), A("Ic"), A("oneb"), False, False, True)
        for k in range(4):
            lin(A("Gb", 1024 * k, 1024 * k + 1024), IND(ww, A("Ns", 64 * k, 64 * k + 64)))
            for i in range(16):
                mm(A("pK", 64 * k, 64 * k + 64), A("I16"), A("Gb", 1024 * k + i, 1024 * k + 1024, 16), False, k == 3 and i == 15, i > 0)
        ts(A("Y"), A("pK", 0, 256), 187.0, AL.max, 197.0, AL.min)
        tt(IND(own, A("Dw", 0, 16)), A("Y"), A("Sp"), AL.add)
        if t == 1:
            dma("y", hbm(T.yx[:]), A("w", S0, S0 + V), "dyx")
        ts(A("Nf"), A("Ns", 0, 256), -1152.0, AL.add)
        sel(A("pb", 0, 16), "XN", "Nf", 0, 256)
        ts(U2, A("pb", 0, 16), 1152.0, AL.add)
        for k in range(2):
            ts(A("Dw", 16 + 8 * k, 24 + 8 * k), A("pb", 8 * k, 8 * k + 8), w2[1 + k], AL.add, 1152.0 + OFF, AL.add)
        cp(A("Ns", 256, 512), IND(A("nbw"), U2))
        lin(A("SU"), IND(own, A("Dw")))
        act(A("Ab"), IND(A("place", 0, VD), U2), AF.Abs, cCtr)
        if t == 1:
            spread(IND(A("place"), o(7)), A("PL"))
        ts(A("rows"), A("Ab"), cHalf, AL.is_lt)
        tt(A("SV", 256, 512), IND(A("raw"), U2), A("rows"), AL.add)
        ts(A("MV", 256, 512), A("Ab"), cHalf, AL.is_lt, cU, AL.mult)
        cp(IND(A(Z), U2), A("MV", 256, 512))
        scan(A("R"), A(Z), A(Z), 0.0, AL.add, AL.max)
        for k, (l, kc) in enumerate((("Bt0", 0), ("Bt1", 0), ("Bt1", 1))):
            mm(col("pE0", k), A(l), col("R", VD - 1), True, False, k > 0)
            mm(col("pE0", k), A("Bn0"), col("kb", kc), False, True, True)
        for k, f in (("XR", cXR), ("XT", cXT)):
            lin(A(k), A("X"), c(col("pE0", 0), cN9, f))
        lin(A("tf", 1, 4), A("pE0", 0, 3))
        lin(A("tb"), A("tf", 1, 3))
        tt(A("Rg"), IND(A("R"), U), A("SV"), AL.mult)
        mm(A("pa", 0, 32), A("I1"), A("cT", 0, 32), True, False)
        sel(A("pa", 0, 32), "XR", "Rg", 0, 512, False, True)
        ts(o(8), a(lambda k: tt(k, A("pa", 0, 32), A("dS"), AL.min)), -1.0, AL.add)
        tt(IND(A(ST, 512, 1536), o(8)), A("SV"), A("JR"), AL.add)
        TS, SS = A(ST, 0, 512), A(ST, 512, 1024)
        ts(A("oldw"), A("q"), -256.0, AL.add, col("tf", 1), AL.is_ge)
        y = a(lambda k: lin(k, A("oldw"), c(col("tf", 3), -1.0, dn), c(col("tf", 1), -1.0, n0)))
        ts(o(0), a(lambda k: tt(k, y, A("qv"), AL.add)), n1, AL.min, V - 1.0, AL.add)
        lin(TS, IND(A("bag", 0, 4736), o(0)))
        if t == 0:
            act(A("TSf"), TS, AF.Silu)
        else:
            lin(A("TSf"), TS)
        sel(A("pb", 0, 64), "X01", ST, 0, 1024)
        ts(Us, A("pb", 32, 64), -OFF, AL.add, 0.0, AL.max)
        ts(o(1), A("pb", 0, 32), -OFF, AL.add)
        lin(A("Usw"), A("pb", 32, 64))
        if t == 0:
            lin(A("PL"), IND(A("place", 0, VD), Us))
            sel(A("pb", 0, 32), "X0", "PL", 0, 512)
            lin(A("PLw"), A("pb", 0, 32), 1.0 / BL, 1.0 - 64.0 / BL)
        else:
            ts(A("PL"), IND(A("place", 0, VD), Us), MAGIC - 64.0, AL.add, -MAGIC, AL.add)
            dma("y", A("PR"), row, "dr0")
            ts(A("PR"), A("PR"), MAGIC - 64.0, AL.add, -MAGIC, AL.add)
            dma("y", row, A("PR"), "dr1")
        tt(A("Rt"), IND(A("R"), o(1)), SS, AL.mult)
        mm(A("pa", 0, 32), A("I1"), A("cT", 32, 64), True, False)
        sel(A("pa", 0, 32), "XT", "Rt", 0, 512, False, True)
        ts(o(9), A("pa", 0, 32), 511.0, AL.add, 0.0, AL.max)
        lin(A(ST, 1024, 1536), IND(A(ST, 0, 1024), o(9)))
        sel(A("pa", 0, 64), "Xp", ST, 512, 1536)
        cp(A("o", 320, 384), A("pa", 0, 64))
        for ds in (slots_first, slots_last):
            for d in ds:
                ts(A("go", 2 * d, 2 * d + 2), (T[land][:, d, 32:34], [(land, 34 * d, 34 * d + 34)], []), float(G * d), AL.add)
            gv = A("gv", 32 * ds[0], 32 * ds[-1] + 32)
            lin(gv, (T[land][:, ds[0]:ds[-1] + 1, 0:32], [(land, 34 * ds[0], 34 * ds[-1] + 34)], []))
            cp(IND(A("w", S0 + V), A("go", 2 * ds[0], 2 * ds[-1] + 2)), gv)
        mm(A("pS"), A("I1"), A("SU"), True, True)
        mm(A("pK"), A("B5"), A("PL"), True, False)
        for lo, hi in zip(CUT, CUT[1:]):
            lin(A("Gb", 16 * lo, 16 * hi), IND(ww, A("Ns", lo, hi)))
        for b in range(4):
            lo, hi, bank, at = 128 * b, 128 * b + 128, ("pE0", "pE1")[b % 2], 256 * (b // 2)
            E = A(bank, at, at + 64)
            nb = lambda i: A("Gb", 16 * lo + i, 16 * hi, 16)
            m = lambda i, n=1: A("Mb", 16 * lo + 128 * i, 16 * lo + 128 * (i + n))
            mm(E, A("SV", lo, hi), A("MK"), True, False)
            mm(E, A("SU", lo, hi), A("W4" if ABS[b] else "W8"), False, False, True)
            for i in range(ABS[b], 16):
                mm(E, nb(i), A("Wh"), False, False, i % 8 > 0)
            for j in range(0, 16, 4):
                if j < ABS[b]:
                    d = ("pc", "pd")[j // 4]
                    for i in range(4):
                        mm(A(d, 128 * i, 128 * i + 128), A("Im"), A("SU", lo, hi), i == 0, False, i > 0)
                    for i in range(4):
                        mm(A(d, 128 * i, 128 * i + 128), A("I1"), nb(j + i), False, i == 3, i > 0)
                    act(m(j, 4), A(d), AF.Abs)
                else:
                    for i in range(j, j + 4):
                        tt(m(i), nb(i), A("pS", lo, hi), AL.max, i > j)
            for j in list(range(ABS[b], 16, 4)) + list(range(0, ABS[b], 4)):
                for i in range(j, j + 4):
                    mm(E, m(i), A("Wp" if j < ABS[b] else "W1"), False, i == (ABS[b] - 1) % 16, i > j)
            tt((T.FT[:, 8 * b:8 * b + 8, 0:8], [("FT", lo, hi)], []), E, A("TH"), AL.is_ge)
            mm(A(bank, at + 128, at + 256), (T.FT[:, 8 * b:8 * b + 8, :], [("FT", lo, hi)], []), A("I1"), True, True)
            lin(A("FU", 128 + lo, 128 + hi), A(bank, at + 128, at + 256))
        Lf, JC, CN, HC, H = A("FJ", 512, 1024), A("FJ", 0, 512), A("CN"), A("HH", 0, 512), A("HH", 512, 1024)
        tt(A("NF"), IND(A("FU"), o(11)), A("KR"), AL.mult)
        lin(Lf, IND(A("FU"), o(10)))
        mm(A("pK"), A("Ib"), Lf, False, True)
        scan(JC, A("D01"), Lf, -256.0, AL.mult, AL.add)
        ml = col("FJ", 511)
        for k, ls in enumerate((("Bn1",), ("Bp1", "Bn0", "Bn0"), ("Bp1", "Bn0"))[:3 - t]):
            for j, l in enumerate(ls):
                mm(col("pa", k), A(l), ml, j == 0, j == len(ls) - 1, j + k > 0)
        ts(H, A("pK"), c(ml, -1.0, top), AL.subtract, 64.0 * (1 - t) - 256.0 - BIG, AL.is_lt)
        sA = via(lambda k: ts(k, col("pa", 0), n1, AL.add, V + 255.0 + 64.0 * (1 - t), AL.add))
        sB = via(lambda k: ts(k, col("pa", 1), dn, AL.subtract, -256.0 - V, AL.add))
        lin(A("base"), SS, c(sB, cSign), c(sB, c0, sA))
        scan(CN, A("D01"), A("NF"), -256.0, AL.mult, AL.add)
        sel(A("pc", 0, 32), "XC", "CN", 0, 512)
        ts(o(2), A("pc", 0, 32), 511.0, AL.add)
        spread(IND(A("SL"), o(2)), A("TSf"))
        scan(HC, A("D01"), H, -256.0, AL.mult, AL.add)
        for b, ls in (("pE0", (("Bp1", col("tb", 0)), ("Bn0", col("CN", 511)), ("Bn0", col("HH", 511)))),
                      ("pK", (("Bp1", col("tb", 1)), ("Bn0", col("kb", 0)), ("Bn1", col("CN", 511)), ("Bn1", col("HH", 511))))):
            for j, (l, h) in enumerate(ls):
                mm(col(b, 0), A(l), h, j == 0, j == len(ls) - 1, 0 < j < len(ls) - 1)
        sel(A("pd", 0, 64), "X01", "HH", 0, 1024)
        y = a(lambda k: ts(k, A("oldw"), col("pK", 0), AL.mult, col("pE0", 0), AL.add))
        ts(o(3), a(lambda k: tt(k, A("pd", 0, 32), y, AL.add)), 255.0, AL.add, 0.0, AL.max)
        lin(A("SR"), IND(A("SL", 0, 512), o(3)), c01)
        sel(A("pS", 0, 32), "X01", "SR", 0, 512)
        y = a(lambda k: lin(k, A("pd", 32, 64), -BL))
        y = a(lambda k: tt(k, y, A("dP"), AL.add))
        ts(o(7), a(lambda k: tt(k, A("pS", 0, 32), y, AL.max)), -OFF, AL.add)
        sel(A("pb", 32 * t, 64), "XJ", "FJ", 512 * t, 1024)
        if t == 0:
            was = n0
            n2, n0, n1 = two(lambda k: None)
            n13 = via(lambda k: ts(k, col("pa", 2), was, AL.add, 13.0, AL.mult))
            lin(n0, col("pa", 2), 1.0, was)
            y = a(lambda k: lin(k, A("oldw"), sB, sA))
            y = a(lambda k: tt(k, A("pb", 0, 32), y, AL.add))
            ts(o(4), a(lambda k: tt(k, y, A("dB8"), AL.min)), BL - 64.0, AL.add)
            tt(IND(A("bag"), o(4)), SS, A("D01"), AL.mult)
            y = a(lambda k: tt(k, A("PLw"), A("pd", 32, 64), AL.subtract))
            ts(o(5), a(lambda k: tt(k, y, A("dB"), AL.min)), BL, AL.mult)
            cp(IND(A("bag"), o(5)), A("SR"))
        y = a(lambda k: tt(k, A("pb", 32, 64), A("dP"), AL.add))
        ts(o(6), a(lambda k: tt(k, y, A("Usw"), AL.max)), -OFF, AL.add)
        mm(A("pE1"), A("B01"), JC, True, True)
        if t == 0:
            tt(A("J"), A("pE1"), A("base"), AL.add)
            spread(IND(A("place"), o(6)), A("J"))
        else:
            lin(A("J"), A("pE1"))
            tt(IND(A("place"), o(6)), A("J"), A("base"), AL.add)
            cp(IND(A("place"), o(7)), A("PL"))
            dma("y", hbm(T.yp[:]), row, "dyp")

    def meet(e, n, lo, hi):
        return n in PSUM or (e[0] < hi and lo < e[1])

    wr, rd = {}, {}
    for i, op in enumerate(ops):
        js = set()
        for (n, lo, hi) in op["R"]:
            js.update(e[2] for e in wr.get(n, []) if meet(e, n, lo, hi))
            if n in PSUM:
                js.update(e[2] for e in rd.get(n, []) if op["q"] == "?" or ops[e[2]]["q"] != op["q"])
        for (n, lo, hi) in op["W"]:
            js.update(e[2] for e in wr.get(n, []) + rd.get(n, []) if meet(e, n, lo, hi))
        op["pre"] = js
        for (n, lo, hi) in op["W"]:
            for d in (wr, rd):
                d[n] = [e for e in d.get(n, []) if not (n in PSUM or (lo <= e[0] and e[1] <= hi))]
            wr[n].append((lo, hi, i))
        for (n, lo, hi) in op["R"]:
            rd.setdefault(n, []).append((lo, hi, i))

    known = {k: {} for k in eng}
    total = {}

    def need(q, toks):
        best = {}
        for t in toks:
            if t[0] not in best or best[t[0]][1] < t[1]:
                best[t[0]] = t
        for t in sorted(best.values(), key=lambda t: -len(t[2])):
            if known[q].get(t[0], 0) < t[1]:
                eng[q].wait_ge(T.sem[t[0]], t[1])
                known[q][t[0]] = t[1]
                for k, n in t[2].items():
                    if known[q].get(k, 0) < n:
                        known[q][k] = n

    order = [(int(k.rstrip("s")), "s" if k.endswith("s") else "v") for k in ORDER.split()]
    assert sorted(i for i, _q in order) == list(range(len(ops)))
    for i, pick in order:
        op = ops[i]
        q = pick if op["q"] == "?" else op["q"]
        assert all("tok" in ops[j] for j in list(op["pre"]) + list(op["after"]))
        sem = op["sem"] or "c" + q
        total[sem] = total.get(sem, 0) + abs(op["inc"]) * len(op["fn"])
        if q is not None:
            need(q, [ops[j]["tok"] for j in sorted(op["pre"]) if not (q == "p" and ops[j]["q"] == "p")])
            for fn in op["fn"]:
                call = fn(q) if op["q"] == "?" else fn()
                if op["inc"] > 0:
                    call.then_inc(T.sem[sem], op["inc"])
        op["tok"] = (sem, total[sem], dict(known[q]) if q else {})
    need("g", [(k, n, {}) for k, n in total.items()])
